import numpy as np, ml_dtypes
CORES = [9,25,41,57]
N = 4
import mx_ref
BF = ml_dtypes.bfloat16
def pick(q, e):
    c = np.concatenate([q[0].reshape(128, -1, 4), np.zeros((128, 1, 4), np.uint8)], axis=1); s = np.concatenate([q[1], np.ones((16, 1), np.uint8)], axis=1)
    return (np.ascontiguousarray(c[:, e].reshape(128, -1)), np.ascontiguousarray(s[:, e]))
def join(*qs):
    return (np.concatenate([q[0] for q in qs], axis=1), np.concatenate([q[1] for q in qs], axis=1))
def put(q, e, v):
    c, s = q[0].reshape(128, -1, 4).copy(), q[1].copy(); c[:, e] = v[0].reshape(128, -1, 4); s[:, e] = v[1]
    return (c.reshape(128, -1), s)
def pk(c, s):
    return (np.ascontiguousarray(c), mx_ref.live(s))
def emit(q):
    return q[0], q[1]
def packed(v, rng):
    q = [mx_ref.quantize(np.ascontiguousarray(v[r])) for r in range(N)]
    return np.stack([a for a, b in q]), np.stack([mx_ref.plane(b, rng) for a, b in q])
def values_of_codes():
    e, c = np.zeros((128, 128, 4), np.float32), np.zeros((128, 2, 4), np.uint8)
    e[np.arange(128), np.arange(128), 0] = 1
    c[:127, :, 0] = np.arange(256).reshape(2, 128).T[:127]
    return mx_ref.matmul(mx_ref.quantize(e.reshape(128, 512).astype(BF)), (c.reshape(128, 8), np.full((16, 2), 127, np.uint8))).T.reshape(-1).astype(np.float64)
CODE_VALUE, SCALE_VALUE = values_of_codes(), 2.0 ** (np.arange(256) - 127.0)
def decode(q):
    return (CODE_VALUE[q[0]].reshape(16, 8, -1, 4) * SCALE_VALUE[q[1]][:, None, :, None] + 0.0).reshape(128, -1).astype(np.float32)
def f(rng, *shape):
    return mx_ref.flush((rng.standard_normal(shape, dtype=np.float32) * np.exp2(rng.integers(-2, 3, shape[:-1] + (1,)))).astype(BF))
def wide(rng, *shape, cols=0):
    v = rng.standard_normal(shape, dtype=np.float32) * np.exp2(rng.integers(-12, 13, shape)).astype(np.float32)
    if cols: v *= np.repeat(np.exp2(rng.integers(-cols, cols + 1, shape[:-2] + (1, shape[-1] // 4))) * (rng.random(shape[:-2] + (1, shape[-1] // 4)) > 0.0625), 4, axis=-1).astype(np.float32)
    return mx_ref.flush(v.astype(BF))
C, L, R = 384, 96, 3
def match(p):
    s = np.array(p.reshape(8, 16, C)[:, :8].transpose(2, 0, 1) + np.float32(0.0), order="C")
    j = np.arange(C)
    g = np.zeros((8, C), np.int64)
    for k in range(8):
        e = np.argmax(s.reshape(C, 64), axis=1)
        g[e % 8, j] = e // 8
        s[j, e // 8] = -np.inf
        s[j, :, e % 8] = -np.inf
    return g
def order(p, g):
    m = p[16 * g + np.arange(8)[:, None], np.arange(C)]
    return np.argsort(-(m + np.float32(0.0)), axis=1, kind="stable")
def sung(t, g, o):
    b = t.reshape(8, 16, C, 4)[np.take_along_axis(g, o, axis=1), :, o]
    return np.ascontiguousarray(b.transpose(0, 2, 1, 3)).reshape(128, -1)
def numbers_of(rng):
    return {"x": np.array(f(rng, N, 128, 4 * C)), "u": np.array(f(rng, N, 128, 512)), "v": np.array(f(rng, N, 128, 512))}
def weights(rng, w):
    c, p = packed(w, rng)
    return {"wc": c, "ws": p}
def still(rng):
    return weights(rng, np.zeros((N, 128, 2048), BF))
def setup_inputs(rng):
    return {**numbers_of(rng), **weights(rng, f(rng, N, 128, 2048))}
def setup_inputs_ties(rng):
    d = numbers_of(rng)
    e = rng.permutation(N)
    x = d["x"].reshape(N, 8, 16, C, 4)
    u = d["u"].reshape(N, 8, 16, 128, 4)
    for r in range(N):
        k = np.zeros(C, int) if r == e[2] else rng.permutation(C) % 3
        a = x[r][:, :8, :3].copy()
        a[:, :, 2] = 0
        x[r][:, :8] = a[:, :, k]
        i = np.ones((8, 16), int)
        i[np.arange(8), rng.permutation(8)] = 0
        if r == e[0]: i[:] = 0
        a = u[r][:, :8, :2].copy()
        u[r][:, :8] = a[:, :, i.reshape(-1)]
    x[e[1]] = 0
    u[:, :, 8:] = 0
    w = np.array(f(rng, N, 128, 2048)).reshape(N, 8, 16, 4, 8, 16, 4)
    w[:, :, 8:, :, :, :8] = 0
    return {"x": x.reshape(N, 128, 4 * C), "u": u.reshape(N, 128, 512), "v": d["v"], **weights(rng, w.reshape(N, 128, 2048))}
def setup_inputs_near(rng):
    d = numbers_of(rng)
    turned = np.argsort(rng.random((N, 8)), axis=1) + 8 * rng.integers(0, 32, (N, 8))
    s = (np.arange(C) // 2) ^ turned[:, :, None]
    a = np.stack([rng.permutation([1.0, 1.0, 1.0, -1.0, -1.0, -1.0, 0.0, 0.0]) for r in range(N)])
    x = (rng.integers(4, 8, (N, 8, 16, C, 4)) * rng.choice([-1.0, 1.0], (N, 8, 16, C, 4))).astype(np.float32)
    x[:, :, :8] *= np.float32(2.0 ** -9)
    x[:, :, 8:] *= np.float32(2.0 ** -27)
    x[:, :, 0] = 0
    x[:, :, 0, :, 0] = a[:, :, None] * 2.0 ** -7
    b = ((s[..., None] >> np.arange(8)) & 1) * np.exp2(np.arange(8) - 30.0)
    x[:, :, 8] = b[..., :4]
    x[:, :, 9] = b[..., 4:]
    c = 4 + np.repeat(rng.integers(0, 2, (N, 8, C // 2, 4)), 2, axis=2) + (np.arange(C) % 2)[:, None]
    x[:, :, 11] = (a == 0)[:, :, None, None] * c * 2.0 ** -32
    for r in range(N):
        x[r, rng.permutation(8)[:4], 0, int(rng.integers(C)), 0] = np.array([1.0, 1.0, -1.0, -1.0]) * 2.0 ** 30
    u = d["u"].reshape(N, 128, 128, 4)
    k = np.where(rng.permutation(N) < N // 2, 2.0 ** -30, 1.0).astype(np.float32).astype(BF)
    for g in range(8):
        for h in range(8):
            u[:, :, 16 * g + h] = 0
            u[:, 16 * g, 16 * g + h, 0] = k
            u[:, 16 * g + 8:16 * g + 10, 16 * g + h] = k[:, None, None]
            u[:, 16 * g + 8 + h // 4, 16 * g + h, h % 4] = 0
            u[:, 16 * g + 11, 16 * g + h, h % 4] = k
    return {"x": x.reshape(N, 128, 4 * C).astype(BF), "u": u.reshape(N, 128, 512), "v": d["v"], **still(rng)}
def setup_inputs_huge(rng):
    d = numbers_of(rng)
    o = rng.permutation(N) % 4
    c, a = np.ones((N, C)), np.ones((N, 128))
    for r in range(N):
        if o[r] == 0: a[r] = -1
        if o[r] == 2: c[r] = rng.permutation(C) % 2 * 2.0 - 1.0
        if o[r] == 3: a[r] = rng.permutation(128) % 2 * 2.0 - 1.0
    x = 2.0 ** 30 * (0.6 + 0.4 * rng.random((N, 128, C, 4))) * c[:, None, :, None]
    u = 2.0 ** 30 * (1 - 0.25 * rng.random((N, 128, 128, 4))) * a[:, None, :, None]
    return {"x": x.astype(np.float32).reshape(N, 128, 4 * C).astype(BF), "u": u.astype(np.float32).reshape(N, 128, 512).astype(BF), "v": d["v"], **still(rng)}
def setup_inputs_spread(rng):
    d = setup_inputs(rng)
    d["x"] = wide(rng, N, 128, 4 * C, cols=6)
    return d
def check_inputs(d):
    b = []
    for k in ("x", "u", "v"):
        a = np.abs(d[k].astype(np.float32))
        if not (np.isfinite(a).all() and ((a == 0) | (a >= 2.0 ** -30) & (a <= 2.0 ** 30)).all()): b.append("a value of " + k)
    if np.isin(d["wc"], (127, 255)).any(): b.append("a code of wc")
    none, low, high = [int(mx_ref.quantize(np.full((128, 16), k, np.float32).astype(BF))[1].max()) for k in (0.0, 2.0 ** -30, 2.0 ** 30)]
    s = np.stack([mx_ref.live(p) for p in d["ws"]])
    if not ((s == none) | (s >= low) & (s <= high)).all(): b.append("a scale of ws")
    return b
def reference(x, u, v, wc, ws):
    qu = [mx_ref.quantize(u[r]) for r in range(N)]
    lay = [pk(wc[r], ws[r]) for r in range(N)]
    now = [mx_ref.quantize(x[r]) for r in range(N)]
    for t in range(R):
        g, o, sent = [], [], []
        for r in range(N):
            p = mx_ref.matmul(qu[r], now[r])
            g.append(match(p))
            o.append(order(p, g[r]))
            sent.append(mx_ref.quantize(sung(decode(now[r]).astype(BF), g[r], o[r])))
        for r in range(N):
            m = join(*[pick(sent[s], np.arange(L * r, L * r + L)) for s in range(N)])
            z = np.stack([np.maximum(mx_ref.matmul(pick(lay[r], np.arange(128 * b, 128 * b + 128)), m), np.float32(0.0)) * np.float32(0.03125) for b in range(4)], axis=2)
            now[r] = mx_ref.quantize((decode(m) + z.reshape(128, -1)).astype(BF))
    y, ol = np.zeros((N, 128, C), np.float32), np.zeros((N, 8, 2 * C), np.float32)
    oc, osc = np.zeros((N, 128, 4 * C), np.uint8), np.zeros((N, 16, C), np.uint8)
    for r in range(N):
        y[r] = mx_ref.matmul(mx_ref.quantize(v[r]), now[r])
        ol[r] = np.concatenate([o[r], g[r]], axis=1)
        oc[r], osc[r] = emit(now[r])
    return {"y": y, "ol": ol, "oc": oc, "osc": osc}

@@ -1,0 +1,511 @@
+from concourse.bass import DstId, RemoteDMATransfer
+from concourse.mybir import dt, AluOpType, ActivationFunctionType
+
+ALU = AluOpType
+ACT = ActivationFunctionType
+C, L, R = 384, 96, 3
+PAD = 128 - L
+BIG = float(2 ** 80)
+FREE = float(2 ** 96)
+LIFT = float(2 ** 22)
+MAGIC = float(3 * 2 ** 22)
+F32, BF, I32, U16, X4, U8 = "float32", "bfloat16", "int32", "uint16", "float8_e4m3fn_x4", "uint8"
+
+TILES = [[21, 22, 23, "E"], [17, 18, 19, 20], [13, 14, 15, 16], [9, 10, 11, 12], [5, 6, 7, 8], [1, 2, 3, 4], [0]]
+ON_SCALAR = [23, 22, 21]
+TN = [max(128, 16 * (max(m for m in t if m != "E") + 1)) for t in TILES]
+TB = [sum(TN[:k]) for k in range(len(TN))]
+CW = sum(TN)
+O_U, O_HS, O_ROW, O_XS, O_XV, O_OWN, O_OX, O_I = 0, 8, 10, 34, 58, 82, 84, 108
+
+SCRATCH = {"ps": ("psum", [128, 4096], F32)}
+for _d, _l in (
+    (BF, dict(xin=4 * C, uin=512, vin=512, xs=4 * C, en=516, ep=516, wall=512, q128=128, g512=512, t128=256, htab=64,
+              wh=216, keep8=C, h16=48, horn=C, stp=8 * 216, hs=224, oh=8 * 64, low=64, penh=7 * 192, ct=4 * CW, sg=4 * C,
+              sj=8 * 24 * 23, dp=4 * C, win=32 * C, bt=4 * C)),
+    (F32, dict(z=4 * C, pf=24, tq1=8, tab16=24, jb=4, lik=192, lik2=192, capg=192, run=8 * 192, vc=24, junk=192, sk=C, sks=C,
+               yy=96, zz=64, own=32, xe=C, xv=C, srow=C, vrow=C, rs=24, rs2=24, rs3=24, rk=24, m1=C, m2=C, orow=C, olb=2 * C,
+               ot=2 * C, yo=C, hs7=216)),
+    (X4, dict(uq=128, upq=128, vq=128, wq=512, enq=512, epq=512, waq=256, cq=CW)),
+    (U8, dict(us=128, ups=128, vs=128, wsc=512, ens=512, eps=512, was=256, cs=CW)),
+    (I32, dict(pi=8, it=128)),
+    (U16, dict(off=132, rku=24, pick=48)),
+):
+    for _n, _w in _l.items():
+        SCRATCH[_n] = ("sbuf", [128, _w], _d)
+for _t in range(R + 1):
+    for _n, _w in (("t", C), ("b", C - L), ("m", C + PAD))[:1 if _t == R else 3]:
+        SCRATCH["%sq_%d" % (_n, _t)] = ("sbuf", [128, _w], X4)
+        SCRATCH["%ss_%d" % (_n, _t)] = ("sbuf", [128, _w], U8)
+
+SEMAPHORES = ["ev", "es", "et", "eg", "lx", "lu", "lv", "lw", "so", "sy", "sl"]
+for _t in range(R):
+    SEMAPHORES += ["rep%d" % _t, "arr%d" % _t, "out%d" % _t]
+
+
+def rank_program(g, core, T, topo):
+    rank = T.rank_of(core)
+    if rank is None:
+        return
+    n_ranks = len(T.cores)
+    ops = []
+
+    def op(eng, fn, r=(), w=(), x=(), sem=None, inc=16):
+        ops.append({"e": eng, "fn": fn, "r": list(r), "w": list(w), "x": list(x), "sem": sem, "inc": inc})
+
+    def emit():
+        queue = {"v": g.vector, "s": g.scalar, "t": g.tensor, "g": g, "y": g.sync}
+        wrote, read, held = {}, {}, {}
+        for k, o in enumerate(ops):
+            d = set()
+            for a in o["r"]:
+                d.update(wrote.get(a, []))
+            for a in o["w"]:
+                d.update(read.get(a, []))
+                d.update(q for q in wrote.get(a, []) if not (o["sem"] and ops[q]["sem"] == o["sem"]))
+            for a in o["x"]:
+                d.update(q for q in held.get(a, []) if ops[q]["e"] != o["e"])
+            for a in o["r"]:
+                read.setdefault(a, []).append(k)
+            for a in o["w"]:
+                same = [q for q in wrote.get(a, []) if o["sem"] and ops[q]["sem"] == o["sem"]]
+                wrote[a], read[a] = same + [k], []
+            for a in o["x"]:
+                held[a] = [k]
+            d.discard(k)
+            o["d"] = d
+        known = {e: {} for e in queue}
+        for k, o in enumerate(ops):
+            o["key"] = o["sem"] or o["e"]
+            o["waits"] = []
+            if o["fn"] is None:
+                o["knew"] = {}
+                continue
+            kn = known[o["e"]]
+            for q in sorted(o["d"], reverse=True):
+                p = ops[q]
+                pos = len(ops) if p["sem"] else q
+                if kn.get(p["key"], -1) >= pos:
+                    continue
+                o["waits"].append(q)
+                p["sig"] = True
+                kn[p["key"]] = pos
+                group = [z for z in ops[:k] if z["sem"] == p["sem"]] if p["sem"] else [p]
+                for z in group:
+                    for a, b in z["knew"].items():
+                        if kn.get(a, -1) < b:
+                            kn[a] = b
+            o["knew"] = dict(kn)
+        total, waited = {}, {}
+        for o in ops:
+            if o["sem"]:
+                total[o["sem"]] = total.get(o["sem"], 0) + o["inc"]
+        for o in ops:
+            if not o["sem"] and o.get("sig"):
+                name = "e" + o["e"]
+                total[name] = total.get(name, 0) + 1
+                o["val"] = total[name]
+        for o in ops:
+            if o["fn"] is None:
+                continue
+            for q in o["waits"]:
+                p = ops[q]
+                name, val = (p["sem"], total[p["sem"]]) if p["sem"] else ("e" + p["e"], p["val"])
+                queue[o["e"]].wait_ge(T.sem[name], val)
+                waited[name] = max(waited.get(name, 0), val)
+            ins = o["fn"]()
+            if o["sem"] and not o["sem"].startswith("out"):
+                ins.then_inc(T.sem[o["sem"]], 16)
+            elif o.get("sig") and not o["sem"]:
+                ins.then_inc(T.sem["e" + o["e"]], 1)
+        for name, val in total.items():
+            if waited.get(name, 0) < val:
+                g.wait_ge(T.sem[name], val)
+
+    V, S = g.vector, g.scalar
+
+    def ts(out, in0, s1, s2, o0, o1, r, w, x=()):
+        if o1 is None:
+            op("v", lambda: V.tensor_scalar(out, in0, s1, None, o0), r, w, x)
+        else:
+            op("v", lambda: V.tensor_scalar(out, in0, s1, s2, o0, o1), r, w, x)
+
+    def tt(out, a, b, o, r, w, x=()):
+        op("v", lambda: V.tensor_tensor(out, a, b, o), r, w, x)
+
+    def cp(out, a, r, w, x=()):
+        op("v", lambda: V.tensor_copy(out, a), r, w, x)
+
+    def ms(ap, c, w):
+        op("v", lambda: V.memset(ap, c), (), w)
+
+    def scan(out, d0, d1, init, o0, o1, r, w, x=()):
+        op("v", lambda: V.tensor_tensor_scan(out, d0, d1, init, o0, o1), r, w, x)
+
+    def tr(out, a, r, w):
+        op("v", lambda: V.transpose(out, a), r, w)
+
+    def quant(q, s, a, r, w):
+        op("v", lambda: V.quantize_mx(q, s, a), r, w)
+
+    def act(out, a, f, r, w, x=(), **kw):
+        op("s", lambda: S.activation(out, a, f, **kw), r, w, x)
+
+    def mm(bank, n, lq, ls, rq, rs_, r, start=True, stop=True):
+        op("t", lambda: g.tensor.matmul_mx(T.ps[:, 512 * bank:512 * bank + n], lq, ls, rq, rs_, start, stop), r, (), ["b%d" % bank])
+
+    def iota(out, pat, base, ch, w, small=False):
+        if small:
+            op("g", lambda: g.iota(out, pat, base, ch, allow_small_or_imprecise_dtypes=True), (), w)
+        else:
+            op("g", lambda: g.iota(out, pat, base, ch), (), w)
+
+    def dma(eng, out, a, r, w, sem):
+        q = {"y": g.sync, "s": g.scalar, "g": g}[eng]
+        op(eng, lambda: q.dma_start(out, a), r, w, sem=sem)
+
+    def offs(a, k):
+        return T.off[:, a:a + k]
+
+    def bank(b, n, a=0):
+        return T.ps[:, 512 * b + a:512 * b + n]
+
+    def piece(buf, c, w=128):
+        return buf[:, w * c:w * c + w]
+
+    def quant_state(t, tile, r):
+        for c in range(3):
+            quant(piece(T["tq_%d" % t], c), piece(T["ts_%d" % t], c), piece(tile, c, 512), r, ["t%d_%d" % (t, c)])
+
+    dma("s", T.uin[:], T.u[:], (), ["uin"], "lu")
+    dma("y", T.xin[:], T.x[:], (), ["xin"], "lx")
+    dma("y", T.wq[:].bitcast(dt.uint8), T.wc[:], (), ["w"], "lw")
+    dma("y", T.wsc[:], T.ws[:], (), ["w"], "lw")
+    dma("y", T.vin[:], T.v[:], (), ["vin"], "lv")
+
+    iota(T.pi[:, 0:1], [[0, 1]], 0, 1, ["p"])
+    iota(T.q128[:], [[1, 128]], 0, 0, ["q128"], True)
+    iota(T.it[:, 0:8], [[0, 2], [32, 4]], 0, 0, ["it0"])
+    iota(T.it[:, 10:22], [[9, 3], [2, 4]], 0, 0, ["it2"])
+    iota(T.it[:, 8:10], [[128, 2]], 0, 0, ["it1"])
+    iota(T.htab[:], [[0, 8], [-1, 8]], 8, 0, ["htab"], True)
+    iota(T.it[:, 84:108], [[1, 24]], 0, 0, ["it7"])
+    iota(T.it[:, 34:82], [[1, 2], [2, 3], [6, 8]], 0, 0, ["it4"])
+    iota(T.it[:, 82:84], [[2, 2]], 0, 0, ["it6"])
+    iota(T.jb[:, 0:3], [[128, 3]], 8 * 4 * C, 1, ["jb"], True)
+    iota(T.g512[:], [[1, 8], [0, 64]], 0, 0, ["g512"], True)
+    iota(T.tab16[:], [[16, 24]], 0, 0, ["tab16"], True)
+
+    ms(T.en[:], 0.0, ["en"])
+    ms(T.ep[:], 0.0, ["ep"])
+    ms(T.wh[:], 1.0, ["wh"])
+    ms(T.keep8[:], 1.0, ["keep8"])
+    ms(T.low[:], -BIG, ["low"])
+    ms(T.yy[:, 48:64], 0.0, ["ypad"])
+    ms(T.rs[:, 0:1], 0.0, ["rs0"])
+    ms(T.wh[:, 0:216:8], -7.0, ["wh"])
+    ms(T.keep8[:, 0:C:8], 0.0, ["keep8"])
+    for k in range(4):
+        act(T.stp[:, 432 * k:432 * k + 432], T.en[:, 0:432], ACT.Copy, ["en"], ["stp%d_%d" % (2 * k + q, c) for q in range(2) for c in range(3)])
+    act(T.oh[:], T.en[:, 0:512], ACT.Copy, ["en"], ["ohg%d" % k for k in range(8)] + ["ohh%d" % k for k in range(8)])
+    P_I, P_I8, P_I7, P_A, P_F, P_E, P_G = range(1, 8)
+    for col, sh, mask in ((P_I, 0, 15), (P_I8, 3, 1), (P_I7, 0, 7), (P_A, 1, 3), (P_F, 0, 1), (P_E, 4, 1), (P_G, 4, 7)):
+        ts(T.pi[:, col:col + 1], T.pi[:, 0:1], sh, mask, ALU.logical_shift_right, ALU.bitwise_and, ["p"], ["pi%d" % col])
+    cp(T.pf[:, 0:8], T.pi[:], ["p"] + ["pi%d" % c for c in range(1, 8)], ["pf"])
+
+    def pc(k):
+        return T.pf[:, k:k + 1]
+
+    ts(pc(10), pc(P_I), 8.0, pc(P_G), ALU.mult, ALU.add, ["pf"], ["pf10"])
+    ts(pc(8), pc(P_I8), 8.0, pc(P_I), ALU.mult, ALU.add, ["pf"], ["pf8"])
+    ts(pc(9), pc(P_I8), 64.0, pc(P_I7), ALU.mult, ALU.add, ["pf"], ["pf9"])
+    ts(T.ep[:, 3:515:4], T.q128[:], pc(10), None, ALU.is_equal, None, ["pf10", "q128", "ep"], ["ep"])
+    ts(offs(O_U, 8), T.it[:, 0:8], pc(8), None, ALU.add, None, ["pf8", "it0"], ["o_u"])
+    act(pc(11), pc(P_A), ACT.Identity, ["pf"], ["pf11"], scale=6.0, bias=pc(P_I8))
+    act(pc(14), pc(P_G), ACT.Identity, ["pf"], ["pf14"], scale=16.0, bias=15.0)
+    act(pc(17), pc(P_I), ACT.Identity, ["pf"], ["pf17"], bias=1.0)
+    act(pc(12), pc(P_E), ACT.Identity, ["pf", "pf11"], ["pf12"], scale=3.0, bias=pc(11))
+    for b in range(4):
+        quant(piece(T.epq, b), piece(T.eps, b), T.ep[:, 3 - b:515 - b], ["ep"], ["epq%d" % b])
+    quant(T.uq[:], T.us[:], T.uin[:], ["uin"], ["uq"])
+    ts(offs(O_ROW, 12), T.it[:, 10:22], pc(P_I8), None, ALU.add, None, ["pf", "it2"], ["o_row"])
+    op("v", lambda: V.tensor_copy(T.upq[:].bitcast(dt.uint32), T.uq[:].bitcast(dt.uint32).indirect(offs(O_U, 8))), ["uq", "o_u"], ["upq"])
+    op("s", lambda: S.activation(T.ups[:], T.us[:].indirect(offs(O_U, 8)), ACT.Copy), ["uq", "o_u"], ["ups"])
+    act(T.jb[:, 0:3], T.jb[:, 0:3], ACT.Copy, ["jb"], ["jb"], scale=0.125)
+    ts(T.h16[:, 0:16], T.q128[:, 0:16], pc(P_I), None, ALU.not_equal, None, ["pf", "q128"], ["h16a"])
+    ts(T.h16[:, 16:32], T.q128[:, 0:16], pc(17), LIFT, ALU.is_equal, ALU.mult, ["pf17", "q128"], ["h16b"])
+    ts(offs(O_I, 24), T.it[:, 84:108], 0.0, pc(P_I), ALU.mult, ALU.add, ["it7", "pf"], ["o_i"])
+    tt(T.h16[:, 32:48], T.h16[:, 0:16], T.h16[:, 16:32], ALU.max, ["h16a", "h16b"], ["h16c"])
+    for k, t in enumerate(TILES):
+        lo = 0 if len(t) < 4 else 16 * (min(m for m in t if m != "E") + 1)
+        act(T.ct[:, 4 * (TB[k] + lo):4 * (TB[k] + TN[k])], T.en[:, 0:4 * (TN[k] - lo)], ACT.Copy, ["en"], ["ct%d_%d" % (k, s) for s in range(4)])
+    act(T.horn[:], T.h16[:, 32:48].indirect(offs(O_I, 24)), ACT.Copy, ["h16c", "o_i"], ["horn"])
+    ts(offs(O_HS, 2), T.it[:, 8:10], pc(9), 191.0, ALU.add, ALU.min, ["pf9", "it1"], ["o_hs"])
+    ms(T.htab[:, 0:64:8], 0.0, ["htab"])
+    ts(pc(13), pc(P_F), pc(P_E), None, ALU.is_equal, None, ["pf"], ["pf13"])
+    ts(pc(15), pc(P_I), 15.0, LIFT, ALU.not_equal, ALU.mult, ["pf"], ["pf15"])
+    ts(pc(16), pc(P_I), 15.0, 1.0 / LIFT, ALU.is_equal, ALU.max, ["pf"], ["pf16"])
+    ts(T.t128[:, 0:128], T.q128[:], pc(0), None, ALU.is_gt, None, ["pf", "q128"], ["t128a"])
+    ts(T.t128[:, 128:256], T.q128[:], pc(14), None, ALU.is_le, None, ["pf14", "q128"], ["t128b"])
+    ts(pc(18), pc(15), 1.0, None, ALU.max, None, ["pf15"], ["pf18"])
+    quant_state(0, T.xin, ["xin"])
+
+    def later_constants():
+        ts(T.tq1[:, 0:2], T.it[:, 82:84], pc(12), None, ALU.add, None, ["pf12", "it6"], ["tq1a"])
+        cp(offs(O_XS, 48), T.it[:, 34:82], ["it4"], ["o_x"])
+        ts(T.tq1[:, 2:4], T.tq1[:, 0:2], 64.0, pc(13), ALU.subtract, ALU.mult, ["tq1a", "pf13"], ["tq1b"])
+        cp(offs(O_OX, 24), T.it[:, 84:108], ["it7"], ["o_ox"])
+        tt(T.tq1[:, 4:6], T.tq1[:, 0:2], T.tq1[:, 2:4], ALU.add, ["tq1a", "tq1b"], ["tq1c"])
+        ts(offs(O_OWN, 2), T.tq1[:, 4:6], 64.0, None, ALU.add, None, ["tq1c"], ["o_own"])
+
+    def last_constants():
+        ts(T.en[:, 3:515:4], T.q128[:], pc(0), None, ALU.is_equal, None, ["pf", "q128", "en"], ["en"])
+        for b in range(4):
+            quant(piece(T.enq, b), piece(T.ens, b), T.en[:, 3 - b:515 - b], ["en"], ["enq%d" % b])
+        quant(T.vq[:], T.vs[:], T.vin[:], ["vin"], ["vq"])
+
+    def one_round(t):
+        tq, tsc, tn = T["tq_%d" % t], T["ts_%d" % t], ["t%d_%d" % (t, c) for c in range(3)]
+        for c in range(3):
+            mm(c, 128, piece(tq, c), piece(tsc, c), T.upq[:], T.ups[:], [tn[c], "upq", "ups"])
+        for b in range(4):
+            mm(4 + b, C, piece(T.epq, b), piece(T.eps, b), tq[:], tsc[:], tn + ["epq%d" % b])
+        if t == 0:
+            later_constants()
+
+        def unpack(b):
+            act(piece(T.dp, b, C), bank(4 + b, C), ACT.Copy, (), ["dp%d" % b], ["b%d" % (4 + b)])
+
+        def record(k, c, what):
+            src, top = T.oh[:, 64 * k + 32 + 8 * c:64 * k + 40 + 8 * c], T.run[:, 192 * k + 64 * c + 63:192 * k + 64 * c + 64]
+            code = T.vc[:, 3 * k + c:3 * k + c + 1]
+            if what == 0:
+                act(T.junk[:, 24 * k + 8 * c:24 * k + 8 * c + 8], T.stp[:, 216 * k + 72 * c + 15:216 * k + 72 * c + 72:8], ACT.Identity,
+                    ["stp%d_%d" % (k, c), "jb"], ["vc%d_%d" % (k, c)], bias=T.jb[:, c:c + 1], scale=float(-4 * C), accum_out=code)
+            elif what == 1:
+                act(T.oh[:, 64 * k + 32:64 * k + 64], piece(T.penh, k, 192).indirect(offs(O_HS, 2)), ACT.Copy,
+                    ["penh%d_%d" % (k, q) for q in range(3)] + ["o_hs"], ["ohh%d" % k], scale=-1.0 / BIG)
+            elif what == 2:
+                act(T.sk[:, 16 * c + 8 + k:C:48], src, ACT.Copy, ["ohh%d" % k, "vc%d_%d" % (k, c)], ["sv%d_%d" % (k, c)], scale=code)
+            else:
+                act(T.sk[:, 16 * c + k:C:48], src, ACT.Copy, ["ohh%d" % k, "run%d_%d" % (k, c)], ["sk%d_%d" % (k, c)], scale=top)
+
+        unpack(0)
+        lik, fre, todo = ["lik0", "lik1", "lik2"], ["fre0", "fre1", "fre2"], []
+        for k in range(8):
+            run, stp, oh = 192 * k, 216 * k, 64 * k
+            rn = ["run%d_%d" % (k, c) for c in range(3)]
+            sn = ["stp%d_%d" % (k, c) for c in range(3)]
+            top = [T.run[:, run + 64 * c + 63:run + 64 * c + 64] for c in range(3)]
+            for c in range(3):
+                if k:
+                    scan(T.run[:, run + 64 * c:run + 64 * c + 64], piece(T.lik2, c, 64), piece(T.lik2, c, 64), -BIG, ALU.max, ALU.max, [fre[c]], [rn[c]])
+                else:
+                    scan(piece(T.run, c, 64), T.low[:], bank(c, 64), -BIG, ALU.max, ALU.max, ["low"], [rn[c]], ["b%d" % c])
+            for c in range(3):
+                ts(T.stp[:, stp + 72 * c + 8:stp + 72 * c + 72], T.run[:, run + 64 * c:run + 64 * c + 64], top[c], None, ALU.is_ge, None,
+                   [rn[c]], [sn[c]])
+            if t == 0 and k == 0:
+                ts(T.wall[:], T.g512[:], pc(P_G), None, ALU.is_equal, None, ["pf", "g512"], ["wall"])
+            if t == 0 and k == 1:
+                quant(T.waq[:, 0:128], T.was[:, 0:128], T.wall[:], ["wall"], ["waq0"])
+            if t == 0 and k == 2:
+                tt(T.wall[:, 3:512:4], T.t128[:, 0:128], T.t128[:, 128:256], ALU.mult, ["t128a", "t128b"], ["wall"])
+            if t == 0 and k == 3:
+                quant(T.waq[:, 128:256], T.was[:, 128:256], T.wall[:], ["wall"], ["waq1"])
+            if k == 7:
+                todo = [(k, c, 0) for c in range(3)] + todo
+                while todo:
+                    record(*todo.pop(0))
+            hs = T.hs if k < 7 else T.hs7
+            scan(hs[:, 0:216], T.wh[:], T.stp[:, stp:stp + 216], 0.0, ALU.add, ALU.mult, sn + ["wh"], ["hs"])
+            voice = [hs[:, 72 * c + 71:72 * c + 72] for c in range(3)]
+            if k < 7:
+                tt(T.oh[:, oh:oh + 26], T.stp[:, stp + 15:stp + 216:8], T.stp[:, stp + 7:stp + 208:8], ALU.subtract, sn, ["ohg%d" % k])
+                act(T.capg[:], T.oh[:, oh:oh + 32].indirect(offs(O_ROW, 12)), ACT.Identity, ["ohg%d" % k, "o_row"], ["capg"],
+                    scale=-(FREE + BIG), bias=FREE)
+                pen = [T.penh[:, run + 64 * c:run + 64 * c + 64] for c in range(3)]
+                for c in range(3):
+                    ts(pen[c], T.htab[:], voice[c], -BIG, ALU.is_equal, ALU.mult, ["hs", "htab"], ["penh%d_%d" % (k, c)])
+                for c in range(3):
+                    if k:
+                        tt(piece(T.lik, c, 64), pen[c], piece(T.lik2, c, 64), ALU.add, [fre[c], "penh%d_%d" % (k, c)], [lik[c]])
+                    else:
+                        tt(piece(T.lik, c, 64), bank(c, 64), pen[c], ALU.add, ["penh%d_%d" % (k, c)], [lik[c]], ["b%d" % c])
+                for c in range(3):
+                    scan(piece(T.lik2, c, 64), piece(T.capg, c, 64), piece(T.lik, c, 64), 0.0, ALU.add, ALU.min, [lik[c], "capg"], [fre[c]])
+                todo += [(k, c, 0) for c in range(3)] + [(k, 0, 1)] + [(k, c, w) for w in (2, 3) for c in range(3)]
+            else:
+                for c in range(3):
+                    ts(T.sk[:, 16 * c + k:C:48], T.htab[:, 0:8], voice[c], top[c], ALU.is_equal, ALU.mult,
+                       ["hs", "htab", rn[c]], ["sk%d_%d" % (k, c)])
+                for c in range(3):
+                    ts(T.sk[:, 16 * c + 8 + k:C:48], T.htab[:, 0:8], voice[c], T.vc[:, 3 * k + c:3 * k + c + 1], ALU.is_equal, ALU.mult,
+                       ["hs", "htab", "vc%d_%d" % (k, c)], ["sv%d_%d" % (k, c)])
+            if k == 0:
+                unpack(1)
+                unpack(2)
+            if k == 1:
+                unpack(3)
+                for h in range(8):
+                    dma("y", T.win[16 * h:16 * h + 16, :], T.dp[:], ["dp%d" % b for b in range(4)], ["win"], "rep%d" % t)
+            for _ in range(min(len(todo), (0, 8, 12, 12, 12, 12, 12, 0)[k])):
+                record(*todo.pop(0))
+        done = ["keep8"] + ["%s%d_%d" % (a, k, c) for a in ("sk", "sv") for k in range(8) for c in range(3)]
+        for q in range(2):
+            scan(piece(T.sks, q, 192), piece(T.keep8, q, 192), piece(T.sk, q, 192), 0.0, ALU.mult, ALU.add, done, ["sks%d" % q])
+
+        yy = []
+        for b in range(4):
+            for a in range(4):
+                src, dst = T.sks[32 * a:32 * a + 32, 96 * b + 7:96 * b + 96:8], T.yy[32 * b:32 * b + 32, 12 * a:12 * a + 12]
+                yy.append("yy%d_%d" % (a, b))
+                if b < 2 or (b == 2 and a == 0):
+                    act(dst, src, ACT.Copy, ["sks%d" % (b // 2)], [yy[-1]])
+                else:
+                    cp(dst, src, ["sks%d" % (b // 2)], [yy[-1]])
+        tr(T.zz[:, 0:32], T.yy[:, 0:64:2], yy + ["ypad"], ["zz0"])
+        tr(T.zz[:, 32:64], T.yy[:, 0:64:2], yy + ["ypad"], ["zz1"])
+        for q in range(2):
+            act(piece(T.xe, q, 192), T.yy[:, 0:64].indirect(offs(O_XS + 12 * q, 12)), ACT.Copy, yy + ["ypad", "o_x"], ["xe%d" % q])
+        tr(T.yy[:, 64:96], T.zz[:, 16:48], ["zz0", "zz1"], ["ysw"])
+        cp(T.own[:], T.yy[:].indirect(offs(O_OWN, 2)), yy + ["ypad", "ysw", "o_own"], ["own"])
+        for q in range(2):
+            tr(piece(T.srow, q, 192), piece(T.xe, q, 192), ["xe%d" % q], ["srow%d" % q])
+        act(T.xv[:], T.yy[:, 0:64].indirect(offs(O_XV, 24)), ACT.Copy, yy + ["ypad", "o_x"], ["xv"])
+        srow = ["srow0", "srow1", "own"]
+
+        def slot(k, s, a, b):
+            return T.ct[:, 4 * (TB[k] + a) + s:4 * (TB[k] + b):4]
+
+        def squeeze(k):
+            quant(T.cq[:, TB[k]:TB[k] + TN[k]], T.cs[:, TB[k]:TB[k] + TN[k]], T.ct[:, 4 * TB[k]:4 * (TB[k] + TN[k])],
+                  ["ct%d_%d" % (k, s) for s in range(4)] + ["cd%d" % m for m in TILES[k] if m in ON_SCALAR], ["cq%d" % k])
+
+        def count(k):
+            w = 128 if "E" in TILES[k] else 0
+            mm(3, TN[k], T.waq[:, w:w + 128], T.was[:, w:w + 128], T.cq[:, TB[k]:TB[k] + TN[k]], T.cs[:, TB[k]:TB[k] + TN[k]],
+               ["cq%d" % k, "waq%d" % (w // 128)], k == 0, k == len(TILES) - 1)
+
+        def compare(m):
+            k, s = where[m]
+            ts(slot(k, s, 0, 16 * m + 16), T.srow[:, 0:16 * m + 16], T.own[:, m:m + 1], None, ALU.is_lt, None, srow, ["ct%d_%d" % (k, s)])
+            if m:
+                act(T.sj[:, 8 * m * (m - 1):8 * m * (m + 1)], slot(k, s, 0, 16 * m), ACT.Copy, ["ct%d_%d" % (k, s)], ["rs%d" % m],
+                    accum_out=T.rs[:, m:m + 1])
+
+        where = {m: (k, s) for k, tl in enumerate(TILES) for s, m in enumerate(tl)}
+        for n, m in enumerate(ON_SCALAR):
+            act(T.sg[:, C * n:C * n + 16 * m + 16], T.srow[:, 0:16 * m + 16], ACT.Sign, srow, ["sg%d" % n], bias=T.own[:, m:m + 1], scale=-1.0)
+        for n, m in enumerate(ON_SCALAR):
+            k, s = where[m]
+            act(slot(k, s, 0, 16 * m), T.sg[:, C * n:C * n + 16 * m], ACT.Relu, ["sg%d" % n], ["ct%d_%d" % (k, s), "rs%d" % m],
+                accum_out=T.rs[:, m:m + 1])
+            act(slot(k, s, 16 * m, 16 * m + 16), T.sg[:, C * n + 16 * m:C * n + 16 * m + 16], ACT.Relu, ["sg%d" % n], ["cd%d" % m])
+        ke, se = where["E"]
+        for m in reversed(TILES[1]):
+            compare(m)
+        tt(slot(ke, se, 0, C), T.own[:].indirect(offs(O_OX, 24)), T.srow[:], ALU.is_equal, srow + ["o_ox"], ["ct%d_%d" % (ke, se)])
+        squeeze(1)
+        for k in range(2, len(TILES)):
+            for n, m in enumerate(reversed(TILES[k])):
+                compare(m)
+                if n == 0 and k > 2:
+                    squeeze(k - 1)
+                    if k == 3:
+                        squeeze(0)
+                        count(0)
+                        count(1)
+                    count(k - 1)
+        squeeze(len(TILES) - 1)
+        count(len(TILES) - 1)
+        tr(T.vrow[:], T.xv[:], ["xv"], ["vrow"])
+        tt(T.rs2[:], T.tab16[:], T.rs[:], ALU.subtract, ["tab16"] + ["rs%d" % m for m in range(24)], ["rs2"])
+        scan(T.m1[:], T.horn[:], bank(3, C), 0.0, ALU.mult, ALU.add, ["horn"], ["m1"], ["b3"])
+        ts(T.rs3[:], T.rs2[:], pc(18), None, ALU.mult, None, ["rs2", "pf18"], ["rs3"])
+        tt(T.rk[:], T.m1[:, 15:C:16], T.rs3[:], ALU.add, ["m1", "rs3"], ["rk"])
+        ts(T.rku[:], T.rk[:], pc(16), None, ALU.mult, None, ["rk", "pf16"], ["rku"])
+        cp(T.orow[:].indirect(T.rku[:]), T.vrow[:], ["rku", "vrow"], ["orow"])
+        scan(T.m2[:], T.horn[:], T.orow[:], 0.0, ALU.mult, ALU.add, ["horn", "orow"], ["m2"])
+        per = L // 16
+        ts(T.pick[:, 0:24], T.m2[:, 15:C:16], pc(16), None, ALU.mult, None, ["m2", "pf16"], ["pick0"])
+        if rank:
+            ts(T.pick[:, 24:24 + per * rank], T.m2[:, 15:L * rank:16], pc(16), None, ALU.mult, None, ["m2", "pf16"], ["pick1"])
+
+        def gather(first, n, at, name):
+            for b in range(4):
+                src = T.win[:, C * b:32 * C].indirect(T.pick[:, first:first + n // 16])
+                dst = T.bt[:, 4 * at + b:4 * (at + n):4]
+                if b % 2:
+                    act(dst, src, ACT.Copy, ["win", "pick0", "pick1"], ["%s%d" % (name, b)])
+                else:
+                    cp(dst, src, ["win", "pick0", "pick1"], ["%s%d" % (name, b)])
+
+        bq, bs, mq, msc = [T["%s_%d" % (a, t)] for a in ("bq", "bs", "mq", "ms")]
+        away = ["bt%d" % b for b in range(4)]
+        gather(per * (rank + 1), C - L, 0, "bt")
+        quant(bq[:], bs[:], T.bt[:, 0:4 * (C - L)], away, ["b%d_" % t])
+
+        codes, planes, sent = [], [], 0
+        for d in range(1, n_ranks):
+            peer = (rank + d) % n_ranks
+            rid, pid = topo.addr(T.cores[peer])[:2]
+            eng = topo.engines(core, T.cores[peer])
+            half, quarter = len(eng) // 2, len(eng) // 4
+            first = eng[:half] if d == 1 else eng[half + (d - 2) * quarter:half + (d - 1) * quarter]
+            second = eng[half:] if d == 1 else eng[(d - 2) * quarter:(d - 1) * quarter]
+            there, land = slice(L * (d - 1), L * d), slice(PAD + L * (n_ranks - d), PAD + L * (n_ranks - d + 1))
+            sent += len(first) + len(second)
+            codes.append(RemoteDMATransfer(dst_ids=[DstId(rid=rid, pnc=pid)], dma_engine_mask=sum(1 << e for e in first),
+                                           remote_sem=T.sem["arr%d" % t], src=bq[:, there].bitcast(dt.uint8), dst=mq[:, land].bitcast(dt.uint8)))
+            planes.append(RemoteDMATransfer(dst_ids=[DstId(rid=rid, pnc=pid)], dma_engine_mask=sum(1 << e for e in second),
+                                            remote_sem=T.sem["arr%d" % t], src=bs[:, there], dst=msc[:, land]))
+        op("g", lambda: g.remote_dma_fused(codes, local_sem=T.sem["out%d" % t]), ["b%d_" % t], (), sem="out%d" % t, inc=sent // 2)
+        op("g", lambda: g.remote_dma_fused(planes, local_sem=T.sem["out%d" % t]), ["b%d_" % t], (), sem="out%d" % t, inc=sent // 2)
+        op("g", None, (), ["ma%d" % t], sem="arr%d" % t, inc=sent)
+        gather(per * rank, L, C - L, "bk")
+        quant(mq[:, 0:128], msc[:, 0:128], T.bt[:, 4 * (C - 128):4 * C], away + ["bk%d" % b for b in range(4)], ["mo%d" % t])
+        if t == 0:
+            last_constants()
+
+        xs = []
+
+        def new_state(first, n, skip, name):
+            for b in range(4):
+                mm(b, n, piece(T.wq, b), piece(T.wsc, b), mq[:, first:first + n], msc[:, first:first + n], [name, "w"])
+                mm(4 + b, n, piece(T.enq, b), piece(T.ens, b), mq[:, first:first + n], msc[:, first:first + n], [name, "enq%d" % b])
+            at = (L * rank + first + skip - PAD) % C
+            cut = min(n, skip + C - at)
+            for b in range(4):
+                act(T.z[:, C * b + skip:C * b + n], bank(b, n, skip), ACT.Relu, (), ["z%d" % b], ["b%d" % b], scale=0.03125)
+                for lo, hi, to in ((skip, cut, at), (cut, n, 0)):
+                    if hi > lo:
+                        xs.append("xs%d_%d" % (b, to))
+                        tt(T.xs[:, 4 * to + b:4 * (to + hi - lo):4], bank(4 + b, hi, lo), T.z[:, C * b + lo:C * b + hi], ALU.add,
+                           ["z%d" % b], [xs[-1]], ["b%d" % (4 + b)])
+
+        new_state(0, 128, PAD, "mo%d" % t)
+        if t == R - 1:
+            ts(T.ot[:, 0:C], T.orow[:], 1.0 / (4 * C), MAGIC, ALU.mult, ALU.add, ["orow"], ["ot0"])
+            ts(T.ot[:, C:2 * C], T.vrow[:], 1.0 / (4 * C), MAGIC, ALU.mult, ALU.add, ["vrow"], ["ot1"])
+            ts(T.ot[:, 0:C], T.ot[:, 0:C], MAGIC, float(4 * C), ALU.subtract, ALU.mult, ["ot0"], ["ot0"])
+            ts(T.olb[:, C:2 * C], T.ot[:, C:2 * C], MAGIC, None, ALU.subtract, None, ["ot1"], ["ol1"])
+            tt(T.olb[:, 0:C], T.orow[:], T.ot[:, 0:C], ALU.subtract, ["orow", "ot0"], ["ol0"])
+            dma("y", T.ol[:], T.olb[0:128:16, :], ["ol0", "ol1"], (), "sl")
+        new_state(128, C - L, 0, "ma%d" % t)
+        quant_state(t + 1, T.xs, xs)
+
+    for t in range(R):
+        one_round(t)
+
+    tq, tsc, tn = T["tq_%d" % R], T["ts_%d" % R], ["t%d_%d" % (R, c) for c in range(3)]
+    for c in range(3):
+        mm(c, 128, T.vq[:], T.vs[:], piece(tq, c), piece(tsc, c), [tn[c], "vq"])
+    for c in range(2):
+        act(piece(T.yo, c), bank(c, 128), ACT.Copy, (), ["yo%d" % c], ["b%d" % c])
+    cp(piece(T.yo, 2), bank(2, 128), (), ["yo2"], ["b2"])
+    dma("y", T.oc[:], tq[:].bitcast(dt.uint8), tn, (), "so")
+    dma("s", T.y[:], T.yo[:], ["yo0", "yo1", "yo2"], (), "sy")
+    for k in range(4):
+        dma("y", T.osc[4 * k:4 * k + 4, :], tsc[32 * k:32 * k + 4, :], tn, (), "so")
+    emit()

@@ -13,6 +13,7 @@ F32, BF, I32, U16, X4, U8 = "float32", "bfloat16", "int32", "uint16", "float8_e4
 
 TILES = [[21, 22, 23, "E"], [17, 18, 19, 20], [13, 14, 15, 16], [9, 10, 11, 12], [5, 6, 7, 8], [1, 2, 3, 4], [0]]
 ON_SCALAR = [23, 22, 21]
+FIRST = 7
 TN = [max(128, 16 * (max(m for m in t if m != "E") + 1)) for t in TILES]
 TB = [sum(TN[:k]) for k in range(len(TN))]
 CW = sum(TN)
@@ -20,11 +21,11 @@ O_U, O_HS, O_ROW, O_XS, O_XV, O_OWN, O_OX, O_I = 0, 8, 10, 34, 58, 82, 84, 108
 
 SCRATCH = {"ps": ("psum", [128, 4096], F32)}
 for _d, _l in (
-    (BF, dict(xin=4 * C, uin=512, vin=512, xs=4 * C, en=516, ep=516, wall=512, q128=128, g512=512, t128=256, htab=64,
-              wh=216, keep8=C, h16=48, horn=C, stp=8 * 216, hs=224, oh=8 * 64, low=64, penh=7 * 192, ct=4 * CW, sg=4 * C,
-              sj=8 * 24 * 23, dp=4 * C, win=32 * C, bt=4 * C)),
-    (F32, dict(z=4 * C, pf=24, tq1=8, tab16=24, jb=4, lik=192, lik2=192, capg=192, run=8 * 192, vc=24, junk=192, sk=C, sks=C,
-               yy=96, zz=64, own=32, xe=C, xv=C, srow=C, vrow=C, rs=24, rs2=24, rs3=24, rk=24, m1=C, m2=C, orow=C, olb=2 * C,
+    (BF, dict(xin=4 * C, uin=512, vin=512, xs=4 * C, en=516, ep=516, wall=512, q128=128, g512=512,
+              t128=256, htab=64, wh=216, keep8=C, h16=48, horn=C, stp=8 * 216, hs=224, oh=8 * 64, low=64, penh=7 * 192,
+              ct=4 * CW, sg=4 * C, sj=8 * 24 * 23, dp=4 * C, win=32 * C, bt=4 * C)),
+    (F32, dict(z=4 * C, pf=24, tq1=8, jb=4, lik=192, lik2=192, capg=192, run=8 * 192, vc=24, junk=192, sk=C, sks=C,
+               yy=96, zz=64, own=32, xe=C, xv=C, srow=C, vrow=C, rs=24, rs2=4, rk=24, m1=C, m2=C, orow=C, olb=2 * C,
                ot=2 * C, yo=C, hs7=216)),
     (X4, dict(uq=128, upq=128, vq=128, wq=512, enq=512, epq=512, waq=256, cq=CW)),
     (U8, dict(us=128, ups=128, vs=128, wsc=512, ens=512, eps=512, was=256, cs=CW)),
@@ -173,6 +174,9 @@ def rank_program(g, core, T, topo):
     def piece(buf, c, w=128):
         return buf[:, w * c:w * c + w]
 
+    def pc(k):
+        return T.pf[:, k:k + 1]
+
     def quant_state(t, tile, r):
         for c in range(3):
             quant(piece(T["tq_%d" % t], c), piece(T["ts_%d" % t], c), piece(tile, c, 512), r, ["t%d_%d" % (t, c)])
@@ -184,79 +188,85 @@ def rank_program(g, core, T, topo):
     dma("y", T.vin[:], T.v[:], (), ["vin"], "lv")
 
     iota(T.pi[:, 0:1], [[0, 1]], 0, 1, ["p"])
-    iota(T.q128[:], [[1, 128]], 0, 0, ["q128"], True)
     iota(T.it[:, 0:8], [[0, 2], [32, 4]], 0, 0, ["it0"])
+    iota(T.q128[:], [[1, 128]], 0, 0, ["q128"], True)
     iota(T.it[:, 10:22], [[9, 3], [2, 4]], 0, 0, ["it2"])
-    iota(T.it[:, 8:10], [[128, 2]], 0, 0, ["it1"])
     iota(T.htab[:], [[0, 8], [-1, 8]], 8, 0, ["htab"], True)
+    iota(T.it[:, 8:10], [[128, 2]], 0, 0, ["it1"])
+    iota(T.jb[:, 0:3], [[128, 3]], 8 * 4 * C, 1, ["jb"], True)
     iota(T.it[:, 84:108], [[1, 24]], 0, 0, ["it7"])
     iota(T.it[:, 34:82], [[1, 2], [2, 3], [6, 8]], 0, 0, ["it4"])
     iota(T.it[:, 82:84], [[2, 2]], 0, 0, ["it6"])
-    iota(T.jb[:, 0:3], [[128, 3]], 8 * 4 * C, 1, ["jb"], True)
     iota(T.g512[:], [[1, 8], [0, 64]], 0, 0, ["g512"], True)
-    iota(T.tab16[:], [[16, 24]], 0, 0, ["tab16"], True)
+    iota(T.keep8[:], [[0, C]], 1, 0, ["keep8"], True)
+    for k, t in enumerate(TILES):
+        lo = 0 if len(t) < 4 else 16 * (min(m for m in t if m != "E") + 1)
+        iota(T.ct[:, 4 * (TB[k] + lo):4 * (TB[k] + TN[k])], [[0, 4 * (TN[k] - lo)]], 0, 0, ["ct%d_%d" % (k, s) for s in range(4)], True)
 
     ms(T.en[:], 0.0, ["en"])
-    ms(T.ep[:], 0.0, ["ep"])
     ms(T.wh[:], 1.0, ["wh"])
-    ms(T.keep8[:], 1.0, ["keep8"])
     ms(T.low[:], -BIG, ["low"])
-    ms(T.yy[:, 48:64], 0.0, ["ypad"])
-    ms(T.rs[:, 0:1], 0.0, ["rs0"])
-    ms(T.wh[:, 0:216:8], -7.0, ["wh"])
-    ms(T.keep8[:, 0:C:8], 0.0, ["keep8"])
+    act(T.ep[:], T.en[:], ACT.Copy, ["en"], ["ep"])
     for k in range(4):
         act(T.stp[:, 432 * k:432 * k + 432], T.en[:, 0:432], ACT.Copy, ["en"], ["stp%d_%d" % (2 * k + q, c) for q in range(2) for c in range(3)])
-    act(T.oh[:], T.en[:, 0:512], ACT.Copy, ["en"], ["ohg%d" % k for k in range(8)] + ["ohh%d" % k for k in range(8)])
     P_I, P_I8, P_I7, P_A, P_F, P_E, P_G = range(1, 8)
     for col, sh, mask in ((P_I, 0, 15), (P_I8, 3, 1), (P_I7, 0, 7), (P_A, 1, 3), (P_F, 0, 1), (P_E, 4, 1), (P_G, 4, 7)):
         ts(T.pi[:, col:col + 1], T.pi[:, 0:1], sh, mask, ALU.logical_shift_right, ALU.bitwise_and, ["p"], ["pi%d" % col])
+    ms(T.wh[:, 0:216:8], -7.0, ["wh"])
     cp(T.pf[:, 0:8], T.pi[:], ["p"] + ["pi%d" % c for c in range(1, 8)], ["pf"])
-
-    def pc(k):
-        return T.pf[:, k:k + 1]
-
+    ms(T.rs[:, 0:1], 0.0, ["rs0"])
     ts(pc(10), pc(P_I), 8.0, pc(P_G), ALU.mult, ALU.add, ["pf"], ["pf10"])
     ts(pc(8), pc(P_I8), 8.0, pc(P_I), ALU.mult, ALU.add, ["pf"], ["pf8"])
-    ts(pc(9), pc(P_I8), 64.0, pc(P_I7), ALU.mult, ALU.add, ["pf"], ["pf9"])
+    ts(pc(15), pc(P_I), 15.0, LIFT, ALU.not_equal, ALU.mult, ["pf"], ["pf15"])
     ts(T.ep[:, 3:515:4], T.q128[:], pc(10), None, ALU.is_equal, None, ["pf10", "q128", "ep"], ["ep"])
     ts(offs(O_U, 8), T.it[:, 0:8], pc(8), None, ALU.add, None, ["pf8", "it0"], ["o_u"])
-    act(pc(11), pc(P_A), ACT.Identity, ["pf"], ["pf11"], scale=6.0, bias=pc(P_I8))
-    act(pc(14), pc(P_G), ACT.Identity, ["pf"], ["pf14"], scale=16.0, bias=15.0)
-    act(pc(17), pc(P_I), ACT.Identity, ["pf"], ["pf17"], bias=1.0)
-    act(pc(12), pc(P_E), ACT.Identity, ["pf", "pf11"], ["pf12"], scale=3.0, bias=pc(11))
+    ts(pc(18), pc(15), 1.0, None, ALU.max, None, ["pf15"], ["pf18"])
     for b in range(4):
         quant(piece(T.epq, b), piece(T.eps, b), T.ep[:, 3 - b:515 - b], ["ep"], ["epq%d" % b])
     quant(T.uq[:], T.us[:], T.uin[:], ["uin"], ["uq"])
     ts(offs(O_ROW, 12), T.it[:, 10:22], pc(P_I8), None, ALU.add, None, ["pf", "it2"], ["o_row"])
     op("v", lambda: V.tensor_copy(T.upq[:].bitcast(dt.uint32), T.uq[:].bitcast(dt.uint32).indirect(offs(O_U, 8))), ["uq", "o_u"], ["upq"])
     op("s", lambda: S.activation(T.ups[:], T.us[:].indirect(offs(O_U, 8)), ACT.Copy), ["uq", "o_u"], ["ups"])
+    act(T.oh[:], T.en[:, 0:512], ACT.Copy, ["en"], ["ohg%d" % k for k in range(8)] + ["ohh%d" % k for k in range(8)])
+    act(pc(9), pc(P_I8), ACT.Identity, ["pf"], ["pf9"], scale=64.0, bias=pc(P_I7))
+    act(pc(11), pc(P_A), ACT.Identity, ["pf"], ["pf11"], scale=6.0, bias=pc(P_I8))
+    act(pc(14), pc(P_G), ACT.Identity, ["pf"], ["pf14"], scale=16.0, bias=15.0)
+    act(pc(17), pc(P_I), ACT.Identity, ["pf"], ["pf17"], bias=1.0)
+    act(pc(12), pc(P_E), ACT.Identity, ["pf", "pf11"], ["pf12"], scale=3.0, bias=pc(11))
     act(T.jb[:, 0:3], T.jb[:, 0:3], ACT.Copy, ["jb"], ["jb"], scale=0.125)
-    ts(T.h16[:, 0:16], T.q128[:, 0:16], pc(P_I), None, ALU.not_equal, None, ["pf", "q128"], ["h16a"])
-    ts(T.h16[:, 16:32], T.q128[:, 0:16], pc(17), LIFT, ALU.is_equal, ALU.mult, ["pf17", "q128"], ["h16b"])
-    ts(offs(O_I, 24), T.it[:, 84:108], 0.0, pc(P_I), ALU.mult, ALU.add, ["it7", "pf"], ["o_i"])
-    tt(T.h16[:, 32:48], T.h16[:, 0:16], T.h16[:, 16:32], ALU.max, ["h16a", "h16b"], ["h16c"])
-    for k, t in enumerate(TILES):
-        lo = 0 if len(t) < 4 else 16 * (min(m for m in t if m != "E") + 1)
-        act(T.ct[:, 4 * (TB[k] + lo):4 * (TB[k] + TN[k])], T.en[:, 0:4 * (TN[k] - lo)], ACT.Copy, ["en"], ["ct%d_%d" % (k, s) for s in range(4)])
-    act(T.horn[:], T.h16[:, 32:48].indirect(offs(O_I, 24)), ACT.Copy, ["h16c", "o_i"], ["horn"])
-    ts(offs(O_HS, 2), T.it[:, 8:10], pc(9), 191.0, ALU.add, ALU.min, ["pf9", "it1"], ["o_hs"])
+    act(pc(19), pc(18), ACT.Copy, ["pf18"], ["pf19"], scale=-1.0)
+    for n, m in enumerate(ON_SCALAR):
+        act(pc(20 + n), pc(18), ACT.Copy, ["pf18"], ["pf%d" % (20 + n)], scale=16.0 * m)
     ms(T.htab[:, 0:64:8], 0.0, ["htab"])
-    ts(pc(13), pc(P_F), pc(P_E), None, ALU.is_equal, None, ["pf"], ["pf13"])
-    ts(pc(15), pc(P_I), 15.0, LIFT, ALU.not_equal, ALU.mult, ["pf"], ["pf15"])
-    ts(pc(16), pc(P_I), 15.0, 1.0 / LIFT, ALU.is_equal, ALU.max, ["pf"], ["pf16"])
-    ts(T.t128[:, 0:128], T.q128[:], pc(0), None, ALU.is_gt, None, ["pf", "q128"], ["t128a"])
-    ts(T.t128[:, 128:256], T.q128[:], pc(14), None, ALU.is_le, None, ["pf14", "q128"], ["t128b"])
-    ts(pc(18), pc(15), 1.0, None, ALU.max, None, ["pf15"], ["pf18"])
     quant_state(0, T.xin, ["xin"])
 
-    def later_constants():
-        ts(T.tq1[:, 0:2], T.it[:, 82:84], pc(12), None, ALU.add, None, ["pf12", "it6"], ["tq1a"])
-        cp(offs(O_XS, 48), T.it[:, 34:82], ["it4"], ["o_x"])
-        ts(T.tq1[:, 2:4], T.tq1[:, 0:2], 64.0, pc(13), ALU.subtract, ALU.mult, ["tq1a", "pf13"], ["tq1b"])
-        cp(offs(O_OX, 24), T.it[:, 84:108], ["it7"], ["o_ox"])
-        tt(T.tq1[:, 4:6], T.tq1[:, 0:2], T.tq1[:, 2:4], ALU.add, ["tq1a", "tq1b"], ["tq1c"])
-        ts(offs(O_OWN, 2), T.tq1[:, 4:6], 64.0, None, ALU.add, None, ["tq1c"], ["o_own"])
+    later = [
+        lambda: ts(offs(O_HS, 2), T.it[:, 8:10], pc(9), 191.0, ALU.add, ALU.min, ["pf9", "it1"], ["o_hs"]),
+        lambda: ts(T.h16[:, 0:16], T.q128[:, 0:16], pc(P_I), None, ALU.not_equal, None, ["pf", "q128"], ["h16a"]),
+        lambda: ts(T.h16[:, 16:32], T.q128[:, 0:16], pc(17), LIFT, ALU.is_equal, ALU.mult, ["pf17", "q128"], ["h16b"]),
+        lambda: ts(pc(13), pc(P_F), pc(P_E), None, ALU.is_equal, None, ["pf"], ["pf13"]),
+        lambda: tt(T.h16[:, 32:48], T.h16[:, 0:16], T.h16[:, 16:32], ALU.max, ["h16a", "h16b"], ["h16c"]),
+        lambda: ts(offs(O_I, 24), T.it[:, 84:108], 0.0, pc(P_I), ALU.mult, ALU.add, ["it7", "pf"], ["o_i"]),
+        lambda: ts(pc(16), pc(P_I), 15.0, 1.0 / LIFT, ALU.is_equal, ALU.max, ["pf"], ["pf16"]),
+        lambda: ts(T.t128[:, 0:128], T.q128[:], pc(0), None, ALU.is_gt, None, ["pf", "q128"], ["t128a"]),
+        lambda: ts(T.t128[:, 128:256], T.q128[:], pc(14), None, ALU.is_le, None, ["pf14", "q128"], ["t128b"]),
+        lambda: ts(T.tq1[:, 0:2], T.it[:, 82:84], pc(12), None, ALU.add, None, ["pf12", "it6"], ["tq1a"]),
+        lambda: cp(offs(O_XS, 48), T.it[:, 34:82], ["it4"], ["o_x"]),
+        lambda: ts(T.wall[:], T.g512[:], pc(P_G), None, ALU.is_equal, None, ["pf", "g512"], ["wall"]),
+        lambda: ts(T.tq1[:, 2:4], T.tq1[:, 0:2], 64.0, pc(13), ALU.subtract, ALU.mult, ["tq1a", "pf13"], ["tq1b"]),
+        lambda: quant(T.waq[:, 0:128], T.was[:, 0:128], T.wall[:], ["wall"], ["waq0"]),
+        lambda: tt(T.tq1[:, 4:6], T.tq1[:, 0:2], T.tq1[:, 2:4], ALU.add, ["tq1a", "tq1b"], ["tq1c"]),
+        lambda: tt(T.wall[:, 3:512:4], T.t128[:, 0:128], T.t128[:, 128:256], ALU.mult, ["t128a", "t128b"], ["wall"]),
+        lambda: ts(offs(O_OWN, 2), T.tq1[:, 4:6], 64.0, None, ALU.add, None, ["tq1c"], ["o_own"]),
+        lambda: quant(T.waq[:, 128:256], T.was[:, 128:256], T.wall[:], ["wall"], ["waq1"]),
+        lambda: cp(offs(O_OX, 24), T.it[:, 84:108], ["it7"], ["o_ox"]),
+        lambda: ms(T.keep8[:, 0:C:8], 0.0, ["keep8"]),
+        lambda: ms(T.yy[:, 48:64], 0.0, ["ypad"]),
+    ]
+
+    def make_later(n):
+        for _ in range(min(n, len(later))):
+            later.pop(0)()
 
     def last_constants():
         ts(T.en[:, 3:515:4], T.q128[:], pc(0), None, ALU.is_equal, None, ["pf", "q128", "en"], ["en"])
@@ -270,8 +280,7 @@ def rank_program(g, core, T, topo):
             mm(c, 128, piece(tq, c), piece(tsc, c), T.upq[:], T.ups[:], [tn[c], "upq", "ups"])
         for b in range(4):
             mm(4 + b, C, piece(T.epq, b), piece(T.eps, b), tq[:], tsc[:], tn + ["epq%d" % b])
-        if t == 0:
-            later_constants()
+        make_later(5)
 
         def unpack(b):
             act(piece(T.dp, b, C), bank(4 + b, C), ACT.Copy, (), ["dp%d" % b], ["b%d" % (4 + b)])
@@ -305,28 +314,23 @@ def rank_program(g, core, T, topo):
             for c in range(3):
                 ts(T.stp[:, stp + 72 * c + 8:stp + 72 * c + 72], T.run[:, run + 64 * c:run + 64 * c + 64], top[c], None, ALU.is_ge, None,
                    [rn[c]], [sn[c]])
-            if t == 0 and k == 0:
-                ts(T.wall[:], T.g512[:], pc(P_G), None, ALU.is_equal, None, ["pf", "g512"], ["wall"])
-            if t == 0 and k == 1:
-                quant(T.waq[:, 0:128], T.was[:, 0:128], T.wall[:], ["wall"], ["waq0"])
-            if t == 0 and k == 2:
-                tt(T.wall[:, 3:512:4], T.t128[:, 0:128], T.t128[:, 128:256], ALU.mult, ["t128a", "t128b"], ["wall"])
-            if t == 0 and k == 3:
-                quant(T.waq[:, 128:256], T.was[:, 128:256], T.wall[:], ["wall"], ["waq1"])
+            make_later(2)
             if k == 7:
                 todo = [(k, c, 0) for c in range(3)] + todo
                 while todo:
                     record(*todo.pop(0))
-            hs = T.hs if k < 7 else T.hs7
-            scan(hs[:, 0:216], T.wh[:], T.stp[:, stp:stp + 216], 0.0, ALU.add, ALU.mult, sn + ["wh"], ["hs"])
-            voice = [hs[:, 72 * c + 71:72 * c + 72] for c in range(3)]
+            hs, hn = T.hs if k < 7 else T.hs7, ["hsa", "hsa", "hsb"]
+            scan(hs[:, 0:144], T.wh[:, 0:144], T.stp[:, stp:stp + 144], 0.0, ALU.add, ALU.mult, sn[:2] + ["wh"], ["hsa"])
             if k < 7:
                 tt(T.oh[:, oh:oh + 26], T.stp[:, stp + 15:stp + 216:8], T.stp[:, stp + 7:stp + 208:8], ALU.subtract, sn, ["ohg%d" % k])
                 act(T.capg[:], T.oh[:, oh:oh + 32].indirect(offs(O_ROW, 12)), ACT.Identity, ["ohg%d" % k, "o_row"], ["capg"],
                     scale=-(FREE + BIG), bias=FREE)
+            scan(hs[:, 144:216], T.wh[:, 144:216], T.stp[:, stp + 144:stp + 216], 0.0, ALU.add, ALU.mult, sn[2:] + ["wh"], ["hsb"])
+            voice = [hs[:, 72 * c + 71:72 * c + 72] for c in range(3)]
+            if k < 7:
                 pen = [T.penh[:, run + 64 * c:run + 64 * c + 64] for c in range(3)]
                 for c in range(3):
-                    ts(pen[c], T.htab[:], voice[c], -BIG, ALU.is_equal, ALU.mult, ["hs", "htab"], ["penh%d_%d" % (k, c)])
+                    ts(pen[c], T.htab[:], voice[c], -BIG, ALU.is_equal, ALU.mult, [hn[c], "htab"], ["penh%d_%d" % (k, c)])
                 for c in range(3):
                     if k:
                         tt(piece(T.lik, c, 64), pen[c], piece(T.lik2, c, 64), ALU.add, [fre[c], "penh%d_%d" % (k, c)], [lik[c]])
@@ -338,10 +342,10 @@ def rank_program(g, core, T, topo):
             else:
                 for c in range(3):
                     ts(T.sk[:, 16 * c + k:C:48], T.htab[:, 0:8], voice[c], top[c], ALU.is_equal, ALU.mult,
-                       ["hs", "htab", rn[c]], ["sk%d_%d" % (k, c)])
+                       [hn[c], "htab", rn[c]], ["sk%d_%d" % (k, c)])
                 for c in range(3):
                     ts(T.sk[:, 16 * c + 8 + k:C:48], T.htab[:, 0:8], voice[c], T.vc[:, 3 * k + c:3 * k + c + 1], ALU.is_equal, ALU.mult,
-                       ["hs", "htab", "vc%d_%d" % (k, c)], ["sv%d_%d" % (k, c)])
+                       [hn[c], "htab", "vc%d_%d" % (k, c)], ["sv%d_%d" % (k, c)])
             if k == 0:
                 unpack(1)
                 unpack(2)
@@ -351,29 +355,31 @@ def rank_program(g, core, T, topo):
                     dma("y", T.win[16 * h:16 * h + 16, :], T.dp[:], ["dp%d" % b for b in range(4)], ["win"], "rep%d" % t)
             for _ in range(min(len(todo), (0, 8, 12, 12, 12, 12, 12, 0)[k])):
                 record(*todo.pop(0))
+            if t == 0 and k in (4, 5):
+                act(piece(T.horn, k - 4, 192), T.h16[:, 32:48].indirect(offs(O_I, 12)), ACT.Copy, ["h16c", "o_i"], ["horn%d" % (k - 4)])
         done = ["keep8"] + ["%s%d_%d" % (a, k, c) for a in ("sk", "sv") for k in range(8) for c in range(3)]
         for q in range(2):
             scan(piece(T.sks, q, 192), piece(T.keep8, q, 192), piece(T.sk, q, 192), 0.0, ALU.mult, ALU.add, done, ["sks%d" % q])
 
         yy = []
-        for b in range(4):
+        for b in (0, 1, 2, 3):
             for a in range(4):
                 src, dst = T.sks[32 * a:32 * a + 32, 96 * b + 7:96 * b + 96:8], T.yy[32 * b:32 * b + 32, 12 * a:12 * a + 12]
                 yy.append("yy%d_%d" % (a, b))
-                if b < 2 or (b == 2 and a == 0):
-                    act(dst, src, ACT.Copy, ["sks%d" % (b // 2)], [yy[-1]])
-                else:
+                if (b, a) == (1, 0) or (b >= 2 and (b, a) != (3, 3)):
                     cp(dst, src, ["sks%d" % (b // 2)], [yy[-1]])
+                else:
+                    act(dst, src, ACT.Copy, ["sks%d" % (b // 2)], [yy[-1]])
         tr(T.zz[:, 0:32], T.yy[:, 0:64:2], yy + ["ypad"], ["zz0"])
         tr(T.zz[:, 32:64], T.yy[:, 0:64:2], yy + ["ypad"], ["zz1"])
-        for q in range(2):
-            act(piece(T.xe, q, 192), T.yy[:, 0:64].indirect(offs(O_XS + 12 * q, 12)), ACT.Copy, yy + ["ypad", "o_x"], ["xe%d" % q])
+        act(T.xe[:, 128:C], T.yy[:, 0:64].indirect(offs(O_XS + 8, 16)), ACT.Copy, yy + ["ypad", "o_x"], ["xe1"])
+        cp(T.xe[:, 0:128], T.yy[:, 0:64].indirect(offs(O_XS, 8)), yy + ["ypad", "o_x"], ["xe0"])
         tr(T.yy[:, 64:96], T.zz[:, 16:48], ["zz0", "zz1"], ["ysw"])
+        tr(T.srow[:, 0:128], T.xe[:, 0:128], ["xe0"], ["srow0"])
         cp(T.own[:], T.yy[:].indirect(offs(O_OWN, 2)), yy + ["ypad", "ysw", "o_own"], ["own"])
-        for q in range(2):
-            tr(piece(T.srow, q, 192), piece(T.xe, q, 192), ["xe%d" % q], ["srow%d" % q])
+        tr(T.srow[:, 128:C], T.xe[:, 128:C], ["xe1"], ["srow1"])
         act(T.xv[:], T.yy[:, 0:64].indirect(offs(O_XV, 24)), ACT.Copy, yy + ["ypad", "o_x"], ["xv"])
-        srow = ["srow0", "srow1", "own"]
+        srow = ["srow0", "own", "srow1"]
 
         def slot(k, s, a, b):
             return T.ct[:, 4 * (TB[k] + a) + s:4 * (TB[k] + b):4]
@@ -389,27 +395,39 @@ def rank_program(g, core, T, topo):
 
         def compare(m):
             k, s = where[m]
-            ts(slot(k, s, 0, 16 * m + 16), T.srow[:, 0:16 * m + 16], T.own[:, m:m + 1], None, ALU.is_lt, None, srow, ["ct%d_%d" % (k, s)])
+            ts(slot(k, s, 0, 16 * m + 16), T.srow[:, 0:16 * m + 16], T.own[:, m:m + 1], None, ALU.is_lt, None,
+               srow[:2 if m <= FIRST else 3], ["ct%d_%d" % (k, s)])
+
+        def unbeaten(m):
+            k, s = where[m]
             if m:
-                act(T.sj[:, 8 * m * (m - 1):8 * m * (m + 1)], slot(k, s, 0, 16 * m), ACT.Copy, ["ct%d_%d" % (k, s)], ["rs%d" % m],
-                    accum_out=T.rs[:, m:m + 1])
+                act(T.sj[:, 8 * m * (m - 1):8 * m * (m + 1)], slot(k, s, 0, 16 * m), ACT.Identity, ["ct%d_%d" % (k, s), "pf18", "pf19"],
+                    ["rs%d" % m], scale=pc(19), bias=pc(18), accum_out=T.rs[:, m:m + 1])
 
         where = {m: (k, s) for k, tl in enumerate(TILES) for s, m in enumerate(tl)}
+        compare(FIRST)
         for n, m in enumerate(ON_SCALAR):
             act(T.sg[:, C * n:C * n + 16 * m + 16], T.srow[:, 0:16 * m + 16], ACT.Sign, srow, ["sg%d" % n], bias=T.own[:, m:m + 1], scale=-1.0)
         for n, m in enumerate(ON_SCALAR):
             k, s = where[m]
-            act(slot(k, s, 0, 16 * m), T.sg[:, C * n:C * n + 16 * m], ACT.Relu, ["sg%d" % n], ["ct%d_%d" % (k, s), "rs%d" % m],
-                accum_out=T.rs[:, m:m + 1])
+            act(slot(k, s, 0, 16 * m), T.sg[:, C * n:C * n + 16 * m], ACT.Relu, ["sg%d" % n], ["ct%d_%d" % (k, s), "won%d" % n],
+                accum_out=T.rs2[:, n:n + 1])
             act(slot(k, s, 16 * m, 16 * m + 16), T.sg[:, C * n + 16 * m:C * n + 16 * m + 16], ACT.Relu, ["sg%d" % n], ["cd%d" % m])
+        unbeaten(FIRST)
+        for n, m in enumerate(ON_SCALAR):
+            act(T.rs[:, m:m + 1], T.rs2[:, n:n + 1], ACT.Identity, ["won%d" % n, "pf19", "pf%d" % (20 + n)], ["rs%d" % m],
+                scale=pc(19), bias=pc(20 + n))
         ke, se = where["E"]
         for m in reversed(TILES[1]):
             compare(m)
+            unbeaten(m)
         tt(slot(ke, se, 0, C), T.own[:].indirect(offs(O_OX, 24)), T.srow[:], ALU.is_equal, srow + ["o_ox"], ["ct%d_%d" % (ke, se)])
         squeeze(1)
-        for k in range(2, len(TILES)):
-            for n, m in enumerate(reversed(TILES[k])):
+        last = len(TILES) - 1
+        for k in range(2, last + 1):
+            for n, m in enumerate(m for m in reversed(TILES[k]) if m != FIRST):
                 compare(m)
+                unbeaten(m)
                 if n == 0 and k > 2:
                     squeeze(k - 1)
                     if k == 3:
@@ -417,20 +435,20 @@ def rank_program(g, core, T, topo):
                         count(0)
                         count(1)
                     count(k - 1)
-        squeeze(len(TILES) - 1)
-        count(len(TILES) - 1)
+        squeeze(last)
+        count(last)
         tr(T.vrow[:], T.xv[:], ["xv"], ["vrow"])
-        tt(T.rs2[:], T.tab16[:], T.rs[:], ALU.subtract, ["tab16"] + ["rs%d" % m for m in range(24)], ["rs2"])
-        scan(T.m1[:], T.horn[:], bank(3, C), 0.0, ALU.mult, ALU.add, ["horn"], ["m1"], ["b3"])
-        ts(T.rs3[:], T.rs2[:], pc(18), None, ALU.mult, None, ["rs2", "pf18"], ["rs3"])
-        tt(T.rk[:], T.m1[:, 15:C:16], T.rs3[:], ALU.add, ["m1", "rs3"], ["rk"])
+        scan(T.m1[:], T.horn[:], bank(3, C), 0.0, ALU.mult, ALU.add, ["horn0", "horn1"], ["m1"], ["b3"])
+        tt(T.rk[:], T.m1[:, 15:C:16], T.rs[:], ALU.add, ["m1"] + ["rs%d" % m for m in range(24)], ["rk"])
         ts(T.rku[:], T.rk[:], pc(16), None, ALU.mult, None, ["rk", "pf16"], ["rku"])
         cp(T.orow[:].indirect(T.rku[:]), T.vrow[:], ["rku", "vrow"], ["orow"])
-        scan(T.m2[:], T.horn[:], T.orow[:], 0.0, ALU.mult, ALU.add, ["horn", "orow"], ["m2"])
         per = L // 16
-        ts(T.pick[:, 0:24], T.m2[:, 15:C:16], pc(16), None, ALU.mult, None, ["m2", "pf16"], ["pick0"])
+        for q in range(2):
+            scan(piece(T.m2, q, 192), piece(T.horn, q, 192), piece(T.orow, q, 192), 0.0, ALU.mult, ALU.add, ["horn%d" % q, "orow"], ["m2%d" % q])
         if rank:
-            ts(T.pick[:, 24:24 + per * rank], T.m2[:, 15:L * rank:16], pc(16), None, ALU.mult, None, ["m2", "pf16"], ["pick1"])
+            ts(T.pick[:, 24:24 + per * rank], T.m2[:, 15:L * rank:16], pc(16), None, ALU.mult, None,
+               ["m20", "pf16"] + (["m21"] if L * rank > 192 else []), ["pick1"])
+        ts(T.pick[:, 0:24], T.m2[:, 15:C:16], pc(16), None, ALU.mult, None, ["m20", "m21", "pf16"], ["pick0"])
 
         def gather(first, n, at, name):
             for b in range(4):
@@ -473,11 +491,14 @@ def rank_program(g, core, T, topo):
         def new_state(first, n, skip, name):
             for b in range(4):
                 mm(b, n, piece(T.wq, b), piece(T.wsc, b), mq[:, first:first + n], msc[:, first:first + n], [name, "w"])
+            for b in range(4):
                 mm(4 + b, n, piece(T.enq, b), piece(T.ens, b), mq[:, first:first + n], msc[:, first:first + n], [name, "enq%d" % b])
             at = (L * rank + first + skip - PAD) % C
             cut = min(n, skip + C - at)
-            for b in range(4):
+            ts(T.z[:, skip:n], bank(0, n, skip), 0.0, 0.03125, ALU.max, ALU.mult, (), ["z0"], ["b0"])
+            for b in range(1, 4):
                 act(T.z[:, C * b + skip:C * b + n], bank(b, n, skip), ACT.Relu, (), ["z%d" % b], ["b%d" % b], scale=0.03125)
+            for b in range(4):
                 for lo, hi, to in ((skip, cut, at), (cut, n, 0)):
                     if hi > lo:
                         xs.append("xs%d_%d" % (b, to))
@@ -507,5 +528,5 @@ def rank_program(g, core, T, topo):
     dma("y", T.oc[:], tq[:].bitcast(dt.uint8), tn, (), "so")
     dma("s", T.y[:], T.yo[:], ["yo0", "yo1", "yo2"], (), "sy")
     for k in range(4):
-        dma("y", T.osc[4 * k:4 * k + 4, :], tsc[32 * k:32 * k + 4, :], tn, (), "so")
+        dma("y" if k < 3 else "s", T.osc[4 * k:4 * k + 4, :], tsc[32 * k:32 * k + 4, :], tn, (), "so")
     emit()

@@ -1,15 +1,23 @@
 from concourse.bass import DstId, RemoteDMATransfer
-from concourse.mybir import dt, AluOpType, ActivationFunctionType
+from concourse.mybir import dt, AluOpType, AxisListType, ActivationFunctionType
 
 ALU = AluOpType
 ACT = ActivationFunctionType
 C, L, R = 384, 96, 3
-PAD = 128 - L
-BIG = float(2 ** 80)
-FREE = float(2 ** 96)
+E = 72
+BIG = float(2 ** 73)
+FREE = float(2 ** 78)
+SINK = 32.0
+RISE = 2048.0
 LIFT = float(2 ** 22)
 MAGIC = float(3 * 2 ** 22)
 F32, BF, I32, U16, X4, U8 = "float32", "bfloat16", "int32", "uint16", "float8_e4m3fn_x4", "uint8"
+GROUPS = ((0, 1), (2,))
+ALL = (0, 1, 2)
+STEP_ORDER = [("count", (0,)), ("count", (1,)), ("part", ALL), ("count", (2,)), ("hit", (0,)), ("pad", ALL), ("hit", (1,)), ("hit", (2,)),
+              ("cap", (0,)), ("cap", (1,)), ("cap", (2,))]
+PRODUCTS = [(1, 0), (1, 1), (0, 0), (1, 2), (0, 1), (1, 3), (0, 2), (0, 3)]
+MOVES_ON_SCALAR = 7
 
 TILES = [[21, 22, 23, "E"], [17, 18, 19, 20], [13, 14, 15, 16], [9, 10, 11, 12], [5, 6, 7, 8], [1, 2, 3, 4], [0]]
 ON_SCALAR = [23, 22, 21]
@@ -17,31 +25,31 @@ FIRST = 7
 TN = [max(128, 16 * (max(m for m in t if m != "E") + 1)) for t in TILES]
 TB = [sum(TN[:k]) for k in range(len(TN))]
 CW = sum(TN)
-O_U, O_HS, O_ROW, O_XS, O_XV, O_OWN, O_OX, O_I = 0, 8, 10, 34, 58, 82, 84, 108
+O_U, O_XS, O_XV, O_OWN, O_OX, O_I = 0, 8, 32, 56, 58, 82
 
-SCRATCH = {"ps": ("psum", [128, 4096], F32)}
+SCRATCH = {"ps": ("psum", [128, 4096], F32), "pen": ("sbuf", [128, 192, 9], BF)}
 for _d, _l in (
     (BF, dict(xin=4 * C, uin=512, vin=512, xs=4 * C, en=516, ep=516, wall=512, q128=128, g512=512,
-              t128=256, htab=64, wh=216, keep8=C, h16=48, horn=C, stp=8 * 216, hs=224, oh=8 * 64, low=64, penh=7 * 192,
-              ct=4 * CW, sg=4 * C, sj=8 * 24 * 23, dp=4 * C, win=32 * C, bt=4 * C)),
-    (F32, dict(z=4 * C, pf=24, tq1=8, jb=4, lik=192, lik2=192, capg=192, run=8 * 192, vc=24, junk=192, sk=C, sks=C,
+              t128=256, wh=3 * E, keep=108, h16=48, horn=C, stp=21 * E, hs=24 * E, ohg=7 * 24, low=E,
+              cap=21 * E, ct=4 * CW, sg=4 * C, sj=8 * 24 * 23, dp=4 * C, win=32 * C, bt=4 * C)),
+    (F32, dict(z=4 * C, pf=24, tq1=48, htab=64, lik=6 * E, run=24 * E, sk=6 * E, sks=6 * E, junk=24, v7=4,
                yy=96, zz=64, own=32, xe=C, xv=C, srow=C, vrow=C, rs=24, rs2=4, rk=24, m1=C, m2=C, orow=C, olb=2 * C,
-               ot=2 * C, yo=C, hs7=216)),
+               ot=3 * C, yo=C)),
     (X4, dict(uq=128, upq=128, vq=128, wq=512, enq=512, epq=512, waq=256, cq=CW)),
     (U8, dict(us=128, ups=128, vs=128, wsc=512, ens=512, eps=512, was=256, cs=CW)),
     (I32, dict(pi=8, it=128)),
-    (U16, dict(off=132, rku=24, pick=48)),
+    (U16, dict(off=108, rku=24, pick=24)),
 ):
     for _n, _w in _l.items():
         SCRATCH[_n] = ("sbuf", [128, _w], _d)
 for _t in range(R + 1):
-    for _n, _w in (("t", C), ("b", C - L), ("m", C + PAD))[:1 if _t == R else 3]:
+    for _n, _w in (("t", C), ("b", 2 * L), ("m", C + L))[:1 if _t == R else 3]:
         SCRATCH["%sq_%d" % (_n, _t)] = ("sbuf", [128, _w], X4)
         SCRATCH["%ss_%d" % (_n, _t)] = ("sbuf", [128, _w], U8)
 
-SEMAPHORES = ["ev", "es", "et", "eg", "lx", "lu", "lv", "lw", "so", "sy", "sl"]
+SEMAPHORES = ["ev", "es", "et", "eg", "lx0", "lx1", "lu", "lv", "lw", "so", "sy", "sl"]
 for _t in range(R):
-    SEMAPHORES += ["rep%d" % _t, "arr%d" % _t, "out%d" % _t]
+    SEMAPHORES += ["rep%d" % _t, "arr0_%d" % _t, "arr1_%d" % _t, "out%d" % _t]
 
 
 def rank_program(g, core, T, topo):
@@ -49,6 +57,7 @@ def rank_program(g, core, T, topo):
     if rank is None:
         return
     n_ranks = len(T.cores)
+    turn = L * rank
     ops = []
 
     def op(eng, fn, r=(), w=(), x=(), sem=None, inc=16):
@@ -177,209 +186,266 @@ def rank_program(g, core, T, topo):
     def pc(k):
         return T.pf[:, k:k + 1]
 
-    def quant_state(t, tile, r):
-        for c in range(3):
-            quant(piece(T["tq_%d" % t], c), piece(T["ts_%d" % t], c), piece(tile, c, 512), r, ["t%d_%d" % (t, c)])
+    def tq1(k):
+        return T.tq1[:, 8 * k:8 * k + 8]
+
+    def runs(first, n):
+        first %= C
+        cut = min(n, C - first)
+        return [(0, first, cut)] + ([(cut, 0, n - cut)] if cut < n else [])
+
+    def weave(main, fill):
+        for f in main:
+            if f is None:
+                if fill:
+                    fill.pop(0)()
+            else:
+                f()
 
     dma("s", T.uin[:], T.u[:], (), ["uin"], "lu")
-    dma("y", T.xin[:], T.x[:], (), ["xin"], "lx")
+    for n, grp in enumerate(GROUPS):
+        for at, col, k in runs(turn + 128 * grp[0], 128 * len(grp)):
+            at += 128 * grp[0]
+            dma("y", T.xin[:, 4 * at:4 * (at + k)], T.x[:, 4 * col:4 * (col + k)], (), ["xin%d" % n], "lx%d" % n)
     dma("y", T.wq[:].bitcast(dt.uint8), T.wc[:], (), ["w"], "lw")
     dma("y", T.wsc[:], T.ws[:], (), ["w"], "lw")
     dma("y", T.vin[:], T.v[:], (), ["vin"], "lv")
 
     iota(T.pi[:, 0:1], [[0, 1]], 0, 1, ["p"])
-    iota(T.it[:, 0:8], [[0, 2], [32, 4]], 0, 0, ["it0"])
+    iota(T.it[:, 0:8], [[16, 8]], -5, 0, ["it0"])
     iota(T.q128[:], [[1, 128]], 0, 0, ["q128"], True)
-    iota(T.it[:, 10:22], [[9, 3], [2, 4]], 0, 0, ["it2"])
-    iota(T.htab[:], [[0, 8], [-1, 8]], 8, 0, ["htab"], True)
-    iota(T.it[:, 8:10], [[128, 2]], 0, 0, ["it1"])
-    iota(T.jb[:, 0:3], [[128, 3]], 8 * 4 * C, 1, ["jb"], True)
-    iota(T.it[:, 84:108], [[1, 24]], 0, 0, ["it7"])
-    iota(T.it[:, 34:82], [[1, 2], [2, 3], [6, 8]], 0, 0, ["it4"])
-    iota(T.it[:, 82:84], [[2, 2]], 0, 0, ["it6"])
+    iota(T.htab[:], [[0, 8], [-1, 8]], int(MAGIC) - 8, 0, ["htab"], True)
+    iota(T.sk[:, 17:6 * E:18], [[64 * C, 8], [128, 3]], 4 * C * 7 - 64 * C * 8, 1, ["skj"], True)
+    iota(T.it[:, 8:56], [[0, 2], [1, 24]], 0, 0, ["it7"])
+    for q in range(2):
+        iota(T.it[:, 56 + 24 * q:80 + 24 * q], [[2, 3], [12, 4], [6, 2]], 0, 0, ["it4%d" % q])
+    iota(T.it[:, 104:106], [[2, 2]], 0, 0, ["it6"])
     iota(T.g512[:], [[1, 8], [0, 64]], 0, 0, ["g512"], True)
-    iota(T.keep8[:], [[0, C]], 1, 0, ["keep8"], True)
     for k, t in enumerate(TILES):
         lo = 0 if len(t) < 4 else 16 * (min(m for m in t if m != "E") + 1)
         iota(T.ct[:, 4 * (TB[k] + lo):4 * (TB[k] + TN[k])], [[0, 4 * (TN[k] - lo)]], 0, 0, ["ct%d_%d" % (k, s) for s in range(4)], True)
 
-    ms(T.en[:], 0.0, ["en"])
-    ms(T.wh[:], 1.0, ["wh"])
-    ms(T.low[:], -BIG, ["low"])
-    act(T.ep[:], T.en[:], ACT.Copy, ["en"], ["ep"])
-    for k in range(4):
-        act(T.stp[:, 432 * k:432 * k + 432], T.en[:, 0:432], ACT.Copy, ["en"], ["stp%d_%d" % (2 * k + q, c) for q in range(2) for c in range(3)])
-    P_I, P_I8, P_I7, P_A, P_F, P_E, P_G = range(1, 8)
-    for col, sh, mask in ((P_I, 0, 15), (P_I8, 3, 1), (P_I7, 0, 7), (P_A, 1, 3), (P_F, 0, 1), (P_E, 4, 1), (P_G, 4, 7)):
+    ms(T.ep[:], 0.0, ["ep"])
+    P_I, P_G, P_I8, P_A, P_F, P_E = range(1, 7)
+
+    def digit(col, sh, mask):
         ts(T.pi[:, col:col + 1], T.pi[:, 0:1], sh, mask, ALU.logical_shift_right, ALU.bitwise_and, ["p"], ["pi%d" % col])
-    ms(T.wh[:, 0:216:8], -7.0, ["wh"])
-    cp(T.pf[:, 0:8], T.pi[:], ["p"] + ["pi%d" % c for c in range(1, 8)], ["pf"])
-    ms(T.rs[:, 0:1], 0.0, ["rs0"])
-    ts(pc(10), pc(P_I), 8.0, pc(P_G), ALU.mult, ALU.add, ["pf"], ["pf10"])
-    ts(pc(8), pc(P_I8), 8.0, pc(P_I), ALU.mult, ALU.add, ["pf"], ["pf8"])
-    ts(pc(15), pc(P_I), 15.0, LIFT, ALU.not_equal, ALU.mult, ["pf"], ["pf15"])
-    ts(T.ep[:, 3:515:4], T.q128[:], pc(10), None, ALU.is_equal, None, ["pf10", "q128", "ep"], ["ep"])
-    ts(offs(O_U, 8), T.it[:, 0:8], pc(8), None, ALU.add, None, ["pf8", "it0"], ["o_u"])
-    ts(pc(18), pc(15), 1.0, None, ALU.max, None, ["pf15"], ["pf18"])
-    for b in range(4):
+
+    def unpacker(b):
         quant(piece(T.epq, b), piece(T.eps, b), T.ep[:, 3 - b:515 - b], ["ep"], ["epq%d" % b])
+
+    for col, sh, mask in ((P_I, 0, 15), (P_G, 4, 7), (P_I8, 3, 1), (P_A, 1, 3)):
+        digit(col, sh, mask)
+    cp(T.pf[:, 0:3], T.pi[:, 0:3], ["p", "pi1", "pi2"], ["pf0"])
+    digit(P_F, 0, 1)
+    digit(P_E, 4, 1)
+    ts(tq1(1), T.it[:, 0:8], pc(P_I), 1.0 / 9, ALU.add, ALU.mult, ["pf0", "it0"], ["ub"])
+    ts(pc(10), pc(P_I), 8.0, pc(P_G), ALU.mult, ALU.add, ["pf0"], ["pf10"])
+    ts(tq1(0), T.it[:, 0:8], pc(P_I), 4.0, ALU.add, ALU.add, ["pf0", "it0"], ["ua"])
+    ts(tq1(2), tq1(1), MAGIC, MAGIC, ALU.add, ALU.subtract, ["ub"], ["uc"])
+    ts(T.ep[:, 3:515:4], T.q128[:], pc(10), None, ALU.is_equal, None, ["pf10", "q128", "ep"], ["ep"])
+    ms(T.wh[:], 1.0, ["wh"])
+    ts(tq1(3), tq1(2), 9.0, 7.0, ALU.mult, ALU.add, ["uc"], ["ud"])
+    ts(tq1(4), tq1(2), 7.0, None, ALU.mult, None, ["uc"], ["ue"])
+    ms(T.low[:], -BIG, ["low"])
+    tt(tq1(3), tq1(3), tq1(0), ALU.min, ["ud", "ua"], ["ud"])
+    unpacker(0)
+    tt(tq1(4), tq1(4), tq1(3), ALU.add, ["ud", "ue"], ["ue"])
+    unpacker(1)
+    ts(offs(O_U, 8), tq1(4), 127.0, 0.0, ALU.min, ALU.max, ["ue"], ["o_u"])
+    cp(T.pf[:, 3:7], T.pi[:, 3:7], ["pf0"] + ["pi%d" % c for c in range(3, 7)], ["pf"])
+    ms(T.wh[:, 0:3 * E:9], -8.0625, ["wh"])
+    ms(T.stp[:, 0:21 * E:E], 0.0, ["stp%d_%d" % (k, c) for k in range(7) for c in range(3)])
+    unpacker(2)
+    ms(T.wh[:, E - 1:3 * E:E], -15.0, ["wh"])
     quant(T.uq[:], T.us[:], T.uin[:], ["uin"], ["uq"])
-    ts(offs(O_ROW, 12), T.it[:, 10:22], pc(P_I8), None, ALU.add, None, ["pf", "it2"], ["o_row"])
+    unpacker(3)
     op("v", lambda: V.tensor_copy(T.upq[:].bitcast(dt.uint32), T.uq[:].bitcast(dt.uint32).indirect(offs(O_U, 8))), ["uq", "o_u"], ["upq"])
     op("s", lambda: S.activation(T.ups[:], T.us[:].indirect(offs(O_U, 8)), ACT.Copy), ["uq", "o_u"], ["ups"])
-    act(T.oh[:], T.en[:, 0:512], ACT.Copy, ["en"], ["ohg%d" % k for k in range(8)] + ["ohh%d" % k for k in range(8)])
-    act(pc(9), pc(P_I8), ACT.Identity, ["pf"], ["pf9"], scale=64.0, bias=pc(P_I7))
-    act(pc(11), pc(P_A), ACT.Identity, ["pf"], ["pf11"], scale=6.0, bias=pc(P_I8))
-    act(pc(14), pc(P_G), ACT.Identity, ["pf"], ["pf14"], scale=16.0, bias=15.0)
-    act(pc(17), pc(P_I), ACT.Identity, ["pf"], ["pf17"], bias=1.0)
-    act(pc(12), pc(P_E), ACT.Identity, ["pf", "pf11"], ["pf12"], scale=3.0, bias=pc(11))
-    act(T.jb[:, 0:3], T.jb[:, 0:3], ACT.Copy, ["jb"], ["jb"], scale=0.125)
-    act(pc(19), pc(18), ACT.Copy, ["pf18"], ["pf19"], scale=-1.0)
-    for n, m in enumerate(ON_SCALAR):
-        act(pc(20 + n), pc(18), ACT.Copy, ["pf18"], ["pf%d" % (20 + n)], scale=16.0 * m)
-    ms(T.htab[:, 0:64:8], 0.0, ["htab"])
-    quant_state(0, T.xin, ["xin"])
 
+    back = (24 - turn // 16) % 24
     later = [
-        lambda: ts(offs(O_HS, 2), T.it[:, 8:10], pc(9), 191.0, ALU.add, ALU.min, ["pf9", "it1"], ["o_hs"]),
+        lambda: ts(pc(15), pc(P_I), 15.0, LIFT, ALU.not_equal, ALU.mult, ["pf"], ["pf15"]),
+        lambda: act(pc(11), pc(P_A), ACT.Identity, ["pf"], ["pf11"], scale=6.0, bias=pc(P_I8)),
+        lambda: act(pc(14), pc(P_G), ACT.Identity, ["pf"], ["pf14"], scale=16.0, bias=15.0),
+        lambda: act(pc(17), pc(P_I), ACT.Identity, ["pf"], ["pf17"], bias=1.0),
+        lambda: act(pc(12), pc(P_E), ACT.Identity, ["pf", "pf11"], ["pf12"], scale=3.0, bias=pc(11)),
+        lambda: ts(pc(18), pc(15), 1.0, None, ALU.max, None, ["pf15"], ["pf18"]),
         lambda: ts(T.h16[:, 0:16], T.q128[:, 0:16], pc(P_I), None, ALU.not_equal, None, ["pf", "q128"], ["h16a"]),
         lambda: ts(T.h16[:, 16:32], T.q128[:, 0:16], pc(17), LIFT, ALU.is_equal, ALU.mult, ["pf17", "q128"], ["h16b"]),
         lambda: ts(pc(13), pc(P_F), pc(P_E), None, ALU.is_equal, None, ["pf"], ["pf13"]),
         lambda: tt(T.h16[:, 32:48], T.h16[:, 0:16], T.h16[:, 16:32], ALU.max, ["h16a", "h16b"], ["h16c"]),
-        lambda: ts(offs(O_I, 24), T.it[:, 84:108], 0.0, pc(P_I), ALU.mult, ALU.add, ["it7", "pf"], ["o_i"]),
+        lambda: ts(offs(O_I, 24), T.it[:, 8:32], 0.0, pc(P_I), ALU.mult, ALU.add, ["it7", "pf"], ["o_i"]),
         lambda: ts(pc(16), pc(P_I), 15.0, 1.0 / LIFT, ALU.is_equal, ALU.max, ["pf"], ["pf16"]),
         lambda: ts(T.t128[:, 0:128], T.q128[:], pc(0), None, ALU.is_gt, None, ["pf", "q128"], ["t128a"]),
         lambda: ts(T.t128[:, 128:256], T.q128[:], pc(14), None, ALU.is_le, None, ["pf14", "q128"], ["t128b"]),
-        lambda: ts(T.tq1[:, 0:2], T.it[:, 82:84], pc(12), None, ALU.add, None, ["pf12", "it6"], ["tq1a"]),
-        lambda: cp(offs(O_XS, 48), T.it[:, 34:82], ["it4"], ["o_x"]),
+        lambda: ts(T.tq1[:, 40:42], T.it[:, 104:106], pc(12), None, ALU.add, None, ["pf12", "it6"], ["tq1a"]),
+        lambda: cp(offs(O_XS, 24), T.it[:, 56 + back:80 + back], ["it40", "it41"], ["o_xs"]),
         lambda: ts(T.wall[:], T.g512[:], pc(P_G), None, ALU.is_equal, None, ["pf", "g512"], ["wall"]),
-        lambda: ts(T.tq1[:, 2:4], T.tq1[:, 0:2], 64.0, pc(13), ALU.subtract, ALU.mult, ["tq1a", "pf13"], ["tq1b"]),
+        lambda: ts(T.tq1[:, 42:44], T.tq1[:, 40:42], 64.0, pc(13), ALU.subtract, ALU.mult, ["tq1a", "pf13"], ["tq1b"]),
         lambda: quant(T.waq[:, 0:128], T.was[:, 0:128], T.wall[:], ["wall"], ["waq0"]),
-        lambda: tt(T.tq1[:, 4:6], T.tq1[:, 0:2], T.tq1[:, 2:4], ALU.add, ["tq1a", "tq1b"], ["tq1c"]),
+        lambda: tt(T.tq1[:, 44:46], T.tq1[:, 40:42], T.tq1[:, 42:44], ALU.add, ["tq1a", "tq1b"], ["tq1c"]),
         lambda: tt(T.wall[:, 3:512:4], T.t128[:, 0:128], T.t128[:, 128:256], ALU.mult, ["t128a", "t128b"], ["wall"]),
-        lambda: ts(offs(O_OWN, 2), T.tq1[:, 4:6], 64.0, None, ALU.add, None, ["tq1c"], ["o_own"]),
+        lambda: ts(offs(O_OWN, 2), T.tq1[:, 44:46], 64.0, None, ALU.add, None, ["tq1c"], ["o_own"]),
         lambda: quant(T.waq[:, 128:256], T.was[:, 128:256], T.wall[:], ["wall"], ["waq1"]),
-        lambda: cp(offs(O_OX, 24), T.it[:, 84:108], ["it7"], ["o_ox"]),
-        lambda: ms(T.keep8[:, 0:C:8], 0.0, ["keep8"]),
+        lambda: cp(offs(O_OX, 24), T.it[:, 8 + back:32 + back], ["it7"], ["o_ox"]),
+        lambda: ts(offs(O_XV, 24), T.it[:, 56 + back:80 + back], 1.0, None, ALU.add, None, ["it40", "it41"], ["o_xv"]),
+        lambda: ms(T.keep[:], 1.0, ["keep"]),
         lambda: ms(T.yy[:, 48:64], 0.0, ["ypad"]),
-    ]
+        lambda: ms(T.keep[:, 0:108:9], 0.0, ["keep"]),
+        lambda: ms(T.sk[:, 8:6 * E:18], 0.0, ["skj"]),
+        lambda: ms(T.hs[:, 21 * E:24 * E], 0.0, ["hs_last"]),
+        lambda: ms(T.keep[:, 17:108:18], 64.0 * C, ["keep"]),
+        lambda: ms(T.rs[:, 0:1], 0.0, ["rs0"]),
+        lambda: act(pc(19), pc(18), ACT.Copy, ["pf18"], ["pf19"], scale=-1.0),
+    ] + [lambda n=n, m=m: act(pc(20 + n), pc(18), ACT.Copy, ["pf18"], ["pf%d" % (20 + n)], scale=16.0 * m) for n, m in enumerate(ON_SCALAR)]
+    spare = [lambda: ms(T.en[:], 0.0, ["en"]),
+             lambda: ts(T.en[:, 3:515:4], T.q128[:], pc(0), None, ALU.is_equal, None, ["pf", "q128", "en"], ["en"])]
+    spare += [lambda b=b: quant(piece(T.enq, b), piece(T.ens, b), T.en[:, 3 - b:515 - b], ["en"], ["enq%d" % b]) for b in range(4)]
+    spare += [lambda: quant(T.vq[:], T.vs[:], T.vin[:], ["vin"], ["vq"])]
 
-    def make_later(n):
-        for _ in range(min(n, len(later))):
-            later.pop(0)()
+    def gap():
+        weave([None], spare)
 
-    def last_constants():
-        ts(T.en[:, 3:515:4], T.q128[:], pc(0), None, ALU.is_equal, None, ["pf", "q128", "en"], ["en"])
-        for b in range(4):
-            quant(piece(T.enq, b), piece(T.ens, b), T.en[:, 3 - b:515 - b], ["en"], ["enq%d" % b])
-        quant(T.vq[:], T.vs[:], T.vin[:], ["vin"], ["vq"])
+    def quant_piece(t, c, tile, r):
+        quant(piece(T["tq_%d" % t], c), piece(T["ts_%d" % t], c), piece(tile, c, 512), r, ["t%d_%d" % (t, c)])
+
+    def at(buf, k, c, n=1):
+        return buf[:, 3 * E * k + E * c:3 * E * k + E * (c + n)]
+
+    def names(a, k, cs):
+        return ["%s%d_%d" % (a, k, c) for c in cs]
+
+    def top(k, c):
+        return T.run[:, 3 * E * k + E * c + E - 1:3 * E * k + E * c + E]
+
+    def voice(k, c):
+        return T.hs[:, 3 * E * k + E * c + E - 1:3 * E * k + E * c + E] if k < 7 else T.v7[:, c:c + 1]
+
+    def most(k, c):
+        if k:
+            scan(at(T.run, k, c), T.low[:], at(T.lik, k % 2, c), -BIG, ALU.max, ALU.max, ["low", "lik%d_%d" % (k % 2, c)], ["run%d_%d" % (k, c)])
+        else:
+            scan(T.run[:, E * c + 1:E * c + E], T.low[:, 1:E], bank(2 * c, E, 1), -BIG, ALU.max, ALU.max, ["low"], ["run0_%d" % c], ["b%d" % (2 * c)])
+
+    def keep_likings():
+        for c in range(3):
+            act(at(T.lik, 0, c), bank(2 * c, E), ACT.Copy, (), ["lik0_%d" % c], ["b%d" % (2 * c)])
+        act(T.lik[:, 0:3 * E:9], T.low[:, 0:24], ACT.Copy, ["low"], names("lik", 0, range(3)))
+
+    def step(k, c):
+        a = 3 * E * k + E * c
+        ts(T.stp[:, a + 1:a + E], T.run[:, a + 1:a + E], top(k, c), None, ALU.is_ge, None, ["run%d_%d" % (k, c)], ["stp%d_%d" % (k, c)])
+
+    def ones(k, cs):
+        scan(at(T.hs, k, cs[0], len(cs)), T.wh[:, 0:len(cs) * E], at(T.stp, k, cs[0], len(cs)), 0.0, ALU.add, ALU.mult,
+             names("stp", k, cs) + ["wh"], names("hs", k, cs))
+
+    def part(k, cs):
+        a = 3 * E * k
+        tt(piece(T.ohg, k, 24), T.stp[:, a + 8:a + 3 * E:9], T.stp[:, a:a + 3 * E:9], ALU.subtract, names("stp", k, cs), ["ohg%d" % k])
+
+    def pad(k, cs):
+        ts(T.pen[:, 24 * k:24 * k + 24, 0], piece(T.ohg, k, 24), RISE + SINK, RISE, ALU.mult, ALU.subtract, ["ohg%d" % k], ["pad%d" % k])
+
+    def hit(k, cs):
+        c = cs[0]
+        row, rows = 24 * k + 8 * c, 8 if k < 7 else 1
+        ts(T.pen[:, row:row + rows, 1:9], T.htab[:, 0:8 * rows], voice(k, c), MAGIC, ALU.subtract, ALU.is_equal,
+           ["hs%d_%d" % (k, c), "htab"], ["pen%d_%d" % (k, c)])
+
+    def cap(k, cs):
+        row = 24 * k + 8 * cs[0]
+        ts(at(T.cap, k, cs[0], len(cs)), T.pen[:, row:row + 8 * len(cs), :], -(FREE + BIG), FREE, ALU.mult, ALU.add,
+           names("pen", k, cs) + ["pad%d" % k], names("cap", k, cs))
+
+    def sink(k, c):
+        scan(at(T.lik, (k + 1) % 2, c), at(T.cap, k, c), at(T.lik, k % 2, c), 0.0, ALU.add, ALU.min,
+             ["cap%d_%d" % (k, c), "lik%d_%d" % (k % 2, c)], ["lik%d_%d" % ((k + 1) % 2, c)])
+
+    def record(k, c):
+        one, r, a = T.pen[:, 24 * k + 8 * c, 1:9], ["pen%d_%d" % (k, c)], 18 * c + k
+        act(T.sk[:, a + 9:6 * E:54], one, ACT.Relu, r + ["hs%d_%d" % (k, c)], ["sk1_%d_%d" % (k, c)], scale=16.0, bias=voice(k, c))
+        if k < 7:
+            act(T.sk[:, a:6 * E:54], one, ACT.Copy, r + ["run%d_%d" % (k, c)], ["sk0_%d_%d" % (k, c)], scale=top(k, c))
+
+    def last_voice():
+        for c in range(3):
+            act(piece(T.junk, c, 8), T.hs[:, E * c + E - 1:24 * E:3 * E], ACT.Identity, ["hs%d_%d" % (k, c) for k in range(7)] + ["hs_last"],
+                ["hs7_%d" % c], scale=-1.0, bias=-(92 + 28 / 16) / 8, accum_out=T.v7[:, c:c + 1])
 
     def one_round(t):
         tq, tsc, tn = T["tq_%d" % t], T["ts_%d" % t], ["t%d_%d" % (t, c) for c in range(3)]
         for c in range(3):
-            mm(c, 128, piece(tq, c), piece(tsc, c), T.upq[:], T.ups[:], [tn[c], "upq", "ups"])
+            mm(2 * c, 128, piece(tq, c), piece(tsc, c), T.upq[:], T.ups[:], [tn[c], "upq", "ups"])
         for b in range(4):
-            mm(4 + b, C, piece(T.epq, b), piece(T.eps, b), tq[:], tsc[:], tn + ["epq%d" % b])
-        make_later(5)
+            mm(2 * b + 1, C, piece(T.epq, b), piece(T.eps, b), tq[:], tsc[:], tn + ["epq%d" % b])
 
         def unpack(b):
-            act(piece(T.dp, b, C), bank(4 + b, C), ACT.Copy, (), ["dp%d" % b], ["b%d" % (4 + b)])
+            act(piece(T.dp, b, C), bank(2 * b + 1, C), ACT.Copy, (), ["dp%d" % b], ["b%d" % (2 * b + 1)])
 
-        def record(k, c, what):
-            src, top = T.oh[:, 64 * k + 32 + 8 * c:64 * k + 40 + 8 * c], T.run[:, 192 * k + 64 * c + 63:192 * k + 64 * c + 64]
-            code = T.vc[:, 3 * k + c:3 * k + c + 1]
-            if what == 0:
-                act(T.junk[:, 24 * k + 8 * c:24 * k + 8 * c + 8], T.stp[:, 216 * k + 72 * c + 15:216 * k + 72 * c + 72:8], ACT.Identity,
-                    ["stp%d_%d" % (k, c), "jb"], ["vc%d_%d" % (k, c)], bias=T.jb[:, c:c + 1], scale=float(-4 * C), accum_out=code)
-            elif what == 1:
-                act(T.oh[:, 64 * k + 32:64 * k + 64], piece(T.penh, k, 192).indirect(offs(O_HS, 2)), ACT.Copy,
-                    ["penh%d_%d" % (k, q) for q in range(3)] + ["o_hs"], ["ohh%d" % k], scale=-1.0 / BIG)
-            elif what == 2:
-                act(T.sk[:, 16 * c + 8 + k:C:48], src, ACT.Copy, ["ohh%d" % k, "vc%d_%d" % (k, c)], ["sv%d_%d" % (k, c)], scale=code)
-            else:
-                act(T.sk[:, 16 * c + k:C:48], src, ACT.Copy, ["ohh%d" % k, "run%d_%d" % (k, c)], ["sk%d_%d" % (k, c)], scale=top)
+        def replicate():
+            for h in range(8):
+                dma("y", T.win[16 * h:16 * h + 16, :], T.dp[:], ["dp%d" % b for b in range(4)], ["win"], "rep%d" % t)
 
-        unpack(0)
-        lik, fre, todo = ["lik0", "lik1", "lik2"], ["fre0", "fre1", "fre2"], []
-        for k in range(8):
-            run, stp, oh = 192 * k, 216 * k, 64 * k
-            rn = ["run%d_%d" % (k, c) for c in range(3)]
-            sn = ["stp%d_%d" % (k, c) for c in range(3)]
-            top = [T.run[:, run + 64 * c + 63:run + 64 * c + 64] for c in range(3)]
-            for c in range(3):
-                if k:
-                    scan(T.run[:, run + 64 * c:run + 64 * c + 64], piece(T.lik2, c, 64), piece(T.lik2, c, 64), -BIG, ALU.max, ALU.max, [fre[c]], [rn[c]])
-                else:
-                    scan(piece(T.run, c, 64), T.low[:], bank(c, 64), -BIG, ALU.max, ALU.max, ["low"], [rn[c]], ["b%d" % c])
-            for c in range(3):
-                ts(T.stp[:, stp + 72 * c + 8:stp + 72 * c + 72], T.run[:, run + 64 * c:run + 64 * c + 64], top[c], None, ALU.is_ge, None,
-                   [rn[c]], [sn[c]])
-            make_later(2)
-            if k == 7:
-                todo = [(k, c, 0) for c in range(3)] + todo
-                while todo:
-                    record(*todo.pop(0))
-            hs, hn = T.hs if k < 7 else T.hs7, ["hsa", "hsa", "hsb"]
-            scan(hs[:, 0:144], T.wh[:, 0:144], T.stp[:, stp:stp + 144], 0.0, ALU.add, ALU.mult, sn[:2] + ["wh"], ["hsa"])
-            if k < 7:
-                tt(T.oh[:, oh:oh + 26], T.stp[:, stp + 15:stp + 216:8], T.stp[:, stp + 7:stp + 208:8], ALU.subtract, sn, ["ohg%d" % k])
-                act(T.capg[:], T.oh[:, oh:oh + 32].indirect(offs(O_ROW, 12)), ACT.Identity, ["ohg%d" % k, "o_row"], ["capg"],
-                    scale=-(FREE + BIG), bias=FREE)
-            scan(hs[:, 144:216], T.wh[:, 144:216], T.stp[:, stp + 144:stp + 216], 0.0, ALU.add, ALU.mult, sn[2:] + ["wh"], ["hsb"])
-            voice = [hs[:, 72 * c + 71:72 * c + 72] for c in range(3)]
-            if k < 7:
-                pen = [T.penh[:, run + 64 * c:run + 64 * c + 64] for c in range(3)]
+        for k in range(7):
+            for f in (most, step):
                 for c in range(3):
-                    ts(pen[c], T.htab[:], voice[c], -BIG, ALU.is_equal, ALU.mult, [hn[c], "htab"], ["penh%d_%d" % (k, c)])
-                for c in range(3):
-                    if k:
-                        tt(piece(T.lik, c, 64), pen[c], piece(T.lik2, c, 64), ALU.add, [fre[c], "penh%d_%d" % (k, c)], [lik[c]])
-                    else:
-                        tt(piece(T.lik, c, 64), bank(c, 64), pen[c], ALU.add, ["penh%d_%d" % (k, c)], [lik[c]], ["b%d" % c])
-                for c in range(3):
-                    scan(piece(T.lik2, c, 64), piece(T.capg, c, 64), piece(T.lik, c, 64), 0.0, ALU.add, ALU.min, [lik[c], "capg"], [fre[c]])
-                todo += [(k, c, 0) for c in range(3)] + [(k, 0, 1)] + [(k, c, w) for w in (2, 3) for c in range(3)]
-            else:
-                for c in range(3):
-                    ts(T.sk[:, 16 * c + k:C:48], T.htab[:, 0:8], voice[c], top[c], ALU.is_equal, ALU.mult,
-                       [hn[c], "htab", rn[c]], ["sk%d_%d" % (k, c)])
-                for c in range(3):
-                    ts(T.sk[:, 16 * c + 8 + k:C:48], T.htab[:, 0:8], voice[c], T.vc[:, 3 * k + c:3 * k + c + 1], ALU.is_equal, ALU.mult,
-                       [hn[c], "htab", "vc%d_%d" % (k, c)], ["sv%d_%d" % (k, c)])
+                    f(k, c)
             if k == 0:
-                unpack(1)
-                unpack(2)
+                keep_likings()
+            if k < 2:
+                unpack(2 * k)
+                unpack(2 * k + 1)
             if k == 1:
-                unpack(3)
-                for h in range(8):
-                    dma("y", T.win[16 * h:16 * h + 16, :], T.dp[:], ["dp%d" % b for b in range(4)], ["win"], "rep%d" % t)
-            for _ in range(min(len(todo), (0, 8, 12, 12, 12, 12, 12, 0)[k])):
-                record(*todo.pop(0))
+                replicate()
+            weave([None] * 2, later)
+            for f, cs in STEP_ORDER:
+                {"count": ones, "part": part, "pad": pad, "hit": hit, "cap": cap}[f](k, cs)
+            if k == 6:
+                last_voice()
+            for c in range(3):
+                record(k, c)
+            weave([None] * 3, later)
+            if k == 6:
+                for c in range(3):
+                    hit(7, (c,))
+                    record(7, c)
+            for c in range(3):
+                sink(k, c)
             if t == 0 and k in (4, 5):
                 act(piece(T.horn, k - 4, 192), T.h16[:, 32:48].indirect(offs(O_I, 12)), ACT.Copy, ["h16c", "o_i"], ["horn%d" % (k - 4)])
-        done = ["keep8"] + ["%s%d_%d" % (a, k, c) for a in ("sk", "sv") for k in range(8) for c in range(3)]
-        for q in range(2):
-            scan(piece(T.sks, q, 192), piece(T.keep8, q, 192), piece(T.sk, q, 192), 0.0, ALU.mult, ALU.add, done, ["sks%d" % q])
+        for c in range(3):
+            op("v", lambda c=c: V.tensor_reduce(top(7, c), at(T.lik, 1, c), AxisListType.X, ALU.max), ["lik1_%d" % c], ["run7_%d" % c])
+        for c in range(3):
+            ts(T.sk[:, 18 * c + 7:6 * E:54], T.pen[:, 168 + 8 * c, 1:9], top(7, c), None, ALU.mult, None, ["pen7_%d" % c, "run7_%d" % c], ["sk0_7_%d" % c])
+        weave([None] * len(later), later)
+        for b in range(4):
+            scan(piece(T.sks, b, 108), T.keep[:], piece(T.sk, b, 108), 0.0, ALU.mult, ALU.add,
+                 ["keep", "skj"] + ["sk%d_%d_%d" % (w, k, c) for w in range(2) for k in range(8) for c in range(3)], ["sks%d" % b])
 
         yy = []
-        for b in (0, 1, 2, 3):
-            for a in range(4):
-                src, dst = T.sks[32 * a:32 * a + 32, 96 * b + 7:96 * b + 96:8], T.yy[32 * b:32 * b + 32, 12 * a:12 * a + 12]
-                yy.append("yy%d_%d" % (a, b))
-                if (b, a) == (1, 0) or (b >= 2 and (b, a) != (3, 3)):
-                    cp(dst, src, ["sks%d" % (b // 2)], [yy[-1]])
-                else:
-                    act(dst, src, ACT.Copy, ["sks%d" % (b // 2)], [yy[-1]])
+        for n in range(16):
+            b, a = divmod(n, 4)
+            src, dst = T.sks[32 * a:32 * a + 32, 108 * b + 8:108 * b + 108:9], T.yy[32 * b:32 * b + 32, 12 * a:12 * a + 12]
+            yy.append("yy%d_%d" % (a, b))
+            if n >= MOVES_ON_SCALAR:
+                cp(dst, src, ["sks%d" % b], [yy[-1]])
+            else:
+                act(dst, src, ACT.Copy, ["sks%d" % b], [yy[-1]])
         tr(T.zz[:, 0:32], T.yy[:, 0:64:2], yy + ["ypad"], ["zz0"])
         tr(T.zz[:, 32:64], T.yy[:, 0:64:2], yy + ["ypad"], ["zz1"])
-        act(T.xe[:, 128:C], T.yy[:, 0:64].indirect(offs(O_XS + 8, 16)), ACT.Copy, yy + ["ypad", "o_x"], ["xe1"])
-        cp(T.xe[:, 0:128], T.yy[:, 0:64].indirect(offs(O_XS, 8)), yy + ["ypad", "o_x"], ["xe0"])
+        act(T.xe[:, 128:C], T.yy[:, 0:64].indirect(offs(O_XS + 8, 16)), ACT.Copy, yy + ["ypad", "o_xs"], ["xe1"])
+        cp(T.xe[:, 0:128], T.yy[:, 0:64].indirect(offs(O_XS, 8)), yy + ["ypad", "o_xs"], ["xe0"])
         tr(T.yy[:, 64:96], T.zz[:, 16:48], ["zz0", "zz1"], ["ysw"])
         tr(T.srow[:, 0:128], T.xe[:, 0:128], ["xe0"], ["srow0"])
         cp(T.own[:], T.yy[:].indirect(offs(O_OWN, 2)), yy + ["ypad", "ysw", "o_own"], ["own"])
         tr(T.srow[:, 128:C], T.xe[:, 128:C], ["xe1"], ["srow1"])
-        act(T.xv[:], T.yy[:, 0:64].indirect(offs(O_XV, 24)), ACT.Copy, yy + ["ypad", "o_x"], ["xv"])
+        act(T.xv[:], T.yy[:, 0:64].indirect(offs(O_XV, 24)), ACT.Copy, yy + ["ypad", "o_xv"], ["xv"])
         srow = ["srow0", "own", "srow1"]
+
+        def own(m):
+            return T.own[:, (m + back) % 24:(m + back) % 24 + 1]
 
         def slot(k, s, a, b):
             return T.ct[:, 4 * (TB[k] + a) + s:4 * (TB[k] + b):4]
@@ -390,12 +456,12 @@ def rank_program(g, core, T, topo):
 
         def count(k):
             w = 128 if "E" in TILES[k] else 0
-            mm(3, TN[k], T.waq[:, w:w + 128], T.was[:, w:w + 128], T.cq[:, TB[k]:TB[k] + TN[k]], T.cs[:, TB[k]:TB[k] + TN[k]],
+            mm(7, TN[k], T.waq[:, w:w + 128], T.was[:, w:w + 128], T.cq[:, TB[k]:TB[k] + TN[k]], T.cs[:, TB[k]:TB[k] + TN[k]],
                ["cq%d" % k, "waq%d" % (w // 128)], k == 0, k == len(TILES) - 1)
 
         def compare(m):
             k, s = where[m]
-            ts(slot(k, s, 0, 16 * m + 16), T.srow[:, 0:16 * m + 16], T.own[:, m:m + 1], None, ALU.is_lt, None,
+            ts(slot(k, s, 0, 16 * m + 16), T.srow[:, 0:16 * m + 16], own(m), None, ALU.is_lt, None,
                srow[:2 if m <= FIRST else 3], ["ct%d_%d" % (k, s)])
 
         def unbeaten(m):
@@ -407,7 +473,7 @@ def rank_program(g, core, T, topo):
         where = {m: (k, s) for k, tl in enumerate(TILES) for s, m in enumerate(tl)}
         compare(FIRST)
         for n, m in enumerate(ON_SCALAR):
-            act(T.sg[:, C * n:C * n + 16 * m + 16], T.srow[:, 0:16 * m + 16], ACT.Sign, srow, ["sg%d" % n], bias=T.own[:, m:m + 1], scale=-1.0)
+            act(T.sg[:, C * n:C * n + 16 * m + 16], T.srow[:, 0:16 * m + 16], ACT.Sign, srow, ["sg%d" % n], bias=own(m), scale=-1.0)
         for n, m in enumerate(ON_SCALAR):
             k, s = where[m]
             act(slot(k, s, 0, 16 * m), T.sg[:, C * n:C * n + 16 * m], ACT.Relu, ["sg%d" % n], ["ct%d_%d" % (k, s), "won%d" % n],
@@ -438,93 +504,123 @@ def rank_program(g, core, T, topo):
         squeeze(last)
         count(last)
         tr(T.vrow[:], T.xv[:], ["xv"], ["vrow"])
-        scan(T.m1[:], T.horn[:], bank(3, C), 0.0, ALU.mult, ALU.add, ["horn0", "horn1"], ["m1"], ["b3"])
+        scan(T.m1[:], T.horn[:], bank(7, C), 0.0, ALU.mult, ALU.add, ["horn0", "horn1"], ["m1"], ["b7"])
+        gap()
         tt(T.rk[:], T.m1[:, 15:C:16], T.rs[:], ALU.add, ["m1"] + ["rs%d" % m for m in range(24)], ["rk"])
+        gap()
         ts(T.rku[:], T.rk[:], pc(16), None, ALU.mult, None, ["rk", "pf16"], ["rku"])
+        gap()
         cp(T.orow[:].indirect(T.rku[:]), T.vrow[:], ["rku", "vrow"], ["orow"])
-        per = L // 16
-        for q in range(2):
-            scan(piece(T.m2, q, 192), piece(T.horn, q, 192), piece(T.orow, q, 192), 0.0, ALU.mult, ALU.add, ["horn%d" % q, "orow"], ["m2%d" % q])
-        if rank:
-            ts(T.pick[:, 24:24 + per * rank], T.m2[:, 15:L * rank:16], pc(16), None, ALU.mult, None,
-               ["m20", "pf16"] + (["m21"] if L * rank > 192 else []), ["pick1"])
-        ts(T.pick[:, 0:24], T.m2[:, 15:C:16], pc(16), None, ALU.mult, None, ["m20", "m21", "pf16"], ["pick0"])
-
-        def gather(first, n, at, name):
-            for b in range(4):
-                src = T.win[:, C * b:32 * C].indirect(T.pick[:, first:first + n // 16])
-                dst = T.bt[:, 4 * at + b:4 * (at + n):4]
-                if b % 2:
-                    act(dst, src, ACT.Copy, ["win", "pick0", "pick1"], ["%s%d" % (name, b)])
-                else:
-                    cp(dst, src, ["win", "pick0", "pick1"], ["%s%d" % (name, b)])
+        gap()
 
         bq, bs, mq, msc = [T["%s_%d" % (a, t)] for a in ("bq", "bs", "mq", "ms")]
-        away = ["bt%d" % b for b in range(4)]
-        gather(per * (rank + 1), C - L, 0, "bt")
-        quant(bq[:], bs[:], T.bt[:, 0:4 * (C - L)], away, ["b%d_" % t])
+        H = 2 * L
 
-        codes, planes, sent = [], [], 0
-        for d in range(1, n_ranks):
-            peer = (rank + d) % n_ranks
-            rid, pid = topo.addr(T.cores[peer])[:2]
-            eng = topo.engines(core, T.cores[peer])
-            half, quarter = len(eng) // 2, len(eng) // 4
-            first = eng[:half] if d == 1 else eng[half + (d - 2) * quarter:half + (d - 1) * quarter]
-            second = eng[half:] if d == 1 else eng[(d - 2) * quarter:(d - 1) * quarter]
-            there, land = slice(L * (d - 1), L * d), slice(PAD + L * (n_ranks - d), PAD + L * (n_ranks - d + 1))
-            sent += len(first) + len(second)
-            codes.append(RemoteDMATransfer(dst_ids=[DstId(rid=rid, pnc=pid)], dma_engine_mask=sum(1 << e for e in first),
-                                           remote_sem=T.sem["arr%d" % t], src=bq[:, there].bitcast(dt.uint8), dst=mq[:, land].bitcast(dt.uint8)))
-            planes.append(RemoteDMATransfer(dst_ids=[DstId(rid=rid, pnc=pid)], dma_engine_mask=sum(1 << e for e in second),
-                                            remote_sem=T.sem["arr%d" % t], src=bs[:, there], dst=msc[:, land]))
-        op("g", lambda: g.remote_dma_fused(codes, local_sem=T.sem["out%d" % t]), ["b%d_" % t], (), sem="out%d" % t, inc=sent // 2)
-        op("g", lambda: g.remote_dma_fused(planes, local_sem=T.sem["out%d" % t]), ["b%d_" % t], (), sem="out%d" % t, inc=sent // 2)
-        op("g", None, (), ["ma%d" % t], sem="arr%d" % t, inc=sent)
-        gather(per * rank, L, C - L, "bk")
-        quant(mq[:, 0:128], msc[:, 0:128], T.bt[:, 4 * (C - 128):4 * C], away + ["bk%d" % b for b in range(4)], ["mo%d" % t])
-        if t == 0:
-            last_constants()
+        start = (turn + H, turn)
 
-        xs = []
+        def lift(n):
+            for a, col, k in runs(start[n], H):
+                scan(T.m2[:, H * n + a:H * n + a + k], T.horn[:, 0:k], T.orow[:, col:col + k], 0.0, ALU.mult, ALU.add,
+                     ["horn0", "orow"], ["m2%d_%d" % (n, a)])
 
-        def new_state(first, n, skip, name):
-            for b in range(4):
-                mm(b, n, piece(T.wq, b), piece(T.wsc, b), mq[:, first:first + n], msc[:, first:first + n], [name, "w"])
-            for b in range(4):
-                mm(4 + b, n, piece(T.enq, b), piece(T.ens, b), mq[:, first:first + n], msc[:, first:first + n], [name, "enq%d" % b])
-            at = (L * rank + first + skip - PAD) % C
-            cut = min(n, skip + C - at)
-            ts(T.z[:, skip:n], bank(0, n, skip), 0.0, 0.03125, ALU.max, ALU.mult, (), ["z0"], ["b0"])
-            for b in range(1, 4):
-                act(T.z[:, C * b + skip:C * b + n], bank(b, n, skip), ACT.Relu, (), ["z%d" % b], ["b%d" % b], scale=0.03125)
-            for b in range(4):
-                for lo, hi, to in ((skip, cut, at), (cut, n, 0)):
-                    if hi > lo:
-                        xs.append("xs%d_%d" % (b, to))
-                        tt(T.xs[:, 4 * to + b:4 * (to + hi - lo):4], bank(4 + b, hi, lo), T.z[:, C * b + lo:C * b + hi], ALU.add,
-                           ["z%d" % b], [xs[-1]], ["b%d" % (4 + b)])
+        def offsets(n):
+            ts(T.pick[:, 12 * n:12 * n + 12], T.m2[:, H * n + 15:H * n + H:16], pc(16), None, ALU.mult, None,
+               ["m2%d_%d" % (n, a) for a, col, k in runs(start[n], H)] + ["pf16"], ["pick%d" % n])
 
-        new_state(0, 128, PAD, "mo%d" % t)
+        def gather(n, b):
+            src = T.win[:, C * b:32 * C].indirect(T.pick[:, 12 * n:12 * n + 12])
+            dst = T.bt[:, 4 * H * n + b:4 * H * (n + 1):4]
+            if b % 2:
+                act(dst, src, ACT.Copy, ["win", "pick%d" % n], ["bt%d_%d" % (n, b)])
+            else:
+                cp(dst, src, ["win", "pick%d" % n], ["bt%d_%d" % (n, b)])
+
+        def pack(n, q, s, name):
+            quant(q, s, T.bt[:, 4 * H * n:4 * H * (n + 1)], ["bt%d_%d" % (n, b) for b in range(4)], [name])
+
+        def deal(n, q, s, name, moves):
+            for src, dst, cast in ((q, mq, True), (s, msc, False)):
+                trs, sent = [], 0
+                for i, (d, col) in enumerate(moves):
+                    peer = T.cores[(rank + d) % n_ranks]
+                    rid, pid = topo.addr(peer)[:2]
+                    eng = topo.engines(core, peer)
+                    share = len(eng) // len(moves)
+                    a, b = src[:, col:col + L], dst[:, L * (n_ranks + 1 - d):L * (n_ranks + 2 - d)]
+                    if cast:
+                        a, b = a.bitcast(dt.uint8), b.bitcast(dt.uint8)
+                    sent += share
+                    trs.append(RemoteDMATransfer(dst_ids=[DstId(rid=rid, pnc=pid)], remote_sem=T.sem["arr%d_%d" % (n, t)], src=a, dst=b,
+                                                 dma_engine_mask=sum(1 << e for e in eng[share * i:share * (i + 1)])))
+                op("g", lambda trs=trs: g.remote_dma_fused(trs, local_sem=T.sem["out%d" % t]), [name], (), sem="out%d" % t, inc=sent)
+                op("g", None, (), ["ma%d_%d" % (n, t)], sem="arr%d_%d" % (n, t), inc=sent)
+
+        for f in (lift, offsets):
+            f(0)
+            f(1)
+        for n, b in ((0, 0), (0, 1), (0, 2), (0, 3), (1, 0), (1, 1)):
+            gather(n, b)
+        pack(0, bq[:], bs[:], "b%d_" % t)
+        deal(0, bq, bs, "b%d_" % t, [(2, 0), (3, L)])
+        gather(1, 2)
+        gather(1, 3)
+        gap()
+        gap()
+        pack(1, mq[:, 0:H], msc[:, 0:H], "mo%d" % t)
+        deal(1, mq, msc, "mo%d" % t, [(1, L)])
+
+        xs = {}
+
+        def new_state(first, n, keep, to, name):
+            for w, b in PRODUCTS:
+                lq, ls, r = (T.wq, T.wsc, "w") if w else (T.enq, T.ens, "enq%d" % b)
+                k, z, zn = 2 * b + 1 - w, C * b + to, "z%d_%d" % (b, to)
+                mm(k, n, piece(lq, b), piece(ls, b), mq[:, first:first + n], msc[:, first:first + n], name + [r])
+                if w:
+                    act(T.z[:, z:z + keep], bank(k, keep), ACT.Relu, (), [zn], ["b%d" % k], scale=0.03125)
+                    continue
+                for a, col, m in runs(to + (turn if t == R - 1 else 0), keep):
+                    xs.setdefault(to, []).append("xs%d_%d" % (b, col))
+                    tt(T.xs[:, 4 * col + b:4 * (col + m):4], bank(k, a + m, a), T.z[:, z + a:z + a + m], ALU.add, [zn], [xs[to][-1]], ["b%d" % k])
+                if b != 2:
+                    gap()
+
         if t == R - 1:
-            ts(T.ot[:, 0:C], T.orow[:], 1.0 / (4 * C), MAGIC, ALU.mult, ALU.add, ["orow"], ["ot0"])
-            ts(T.ot[:, C:2 * C], T.vrow[:], 1.0 / (4 * C), MAGIC, ALU.mult, ALU.add, ["vrow"], ["ot1"])
-            ts(T.ot[:, 0:C], T.ot[:, 0:C], MAGIC, float(4 * C), ALU.subtract, ALU.mult, ["ot0"], ["ot0"])
-            ts(T.olb[:, C:2 * C], T.ot[:, C:2 * C], MAGIC, None, ALU.subtract, None, ["ot1"], ["ol1"])
-            tt(T.olb[:, 0:C], T.orow[:], T.ot[:, 0:C], ALU.subtract, ["orow", "ot0"], ["ol0"])
-            dma("y", T.ol[:], T.olb[0:128:16, :], ["ol0", "ol1"], (), "sl")
-        new_state(128, C - L, 0, "ma%d" % t)
-        quant_state(t + 1, T.xs, xs)
+            o0, o1, o2 = [piece(T.ot, n, C) for n in range(3)]
+            spare.extend([
+                lambda: ts(o0, T.orow[:], 1.0 / (4 * C), MAGIC, ALU.mult, ALU.add, ["orow"], ["ot0"]),
+                lambda: ts(o1, T.vrow[:], 1.0 / (4 * C), MAGIC, ALU.mult, ALU.add, ["vrow"], ["ot1"]),
+                lambda: ts(o0, o0, MAGIC, float(-4 * C), ALU.subtract, ALU.mult, ["ot0"], ["ot0"]),
+                lambda: ts(T.olb[:, C:2 * C], o1, MAGIC, None, ALU.subtract, None, ["ot1"], ["ol1"])]
+                + [lambda n=n: tt(piece(T.ot, n, H), piece(T.orow, n, H), piece(T.ot, n, H), ALU.add, ["orow", "ot0"], ["ot0"]) for n in range(2)]
+                + [lambda: ts(o2, o0, float(C - turn), float(-C), ALU.is_ge, ALU.mult, ["ot0"], ["ot2"]),
+                   lambda: ts(o1, o0, float(turn), None, ALU.add, None, ["ot0", "ol1"], ["ot1"])]
+                + [lambda n=n: tt(piece(T.olb, n, H), piece(T.ot, 2 + n, H), piece(T.ot, 4 + n, H), ALU.add, ["ot1", "ot2"], ["ol0%d" % n]) for n in range(2)]
+                + [lambda: dma("y", T.ol[:], T.olb[0:128:16, :], ["ol00", "ol01", "ol1"], (), "sl")])
+            gap()
+            gap()
+        new_state(0, 128, L, 0, ["mo%d" % t])
+        mid = 256
+        new_state(H, mid - L, mid - L, L, ["ma0_%d" % t])
+        if t < R - 1:
+            for c in range(2):
+                quant_piece(t + 1, c, T.xs, xs[0] + xs[L])
+        new_state(L + mid, C - mid, C - mid, mid, ["ma0_%d" % t, "ma1_%d" % t])
+        weave([None] * len(spare), spare)
+        for c in range(3) if t == R - 1 else [2]:
+            quant_piece(t + 1, c, T.xs, xs[0] + xs[L] + xs[mid])
 
+    for c in range(3):
+        quant_piece(0, c, T.xin, ["xin%d" % (c // 2)])
     for t in range(R):
         one_round(t)
 
     tq, tsc, tn = T["tq_%d" % R], T["ts_%d" % R], ["t%d_%d" % (R, c) for c in range(3)]
     for c in range(3):
-        mm(c, 128, T.vq[:], T.vs[:], piece(tq, c), piece(tsc, c), [tn[c], "vq"])
+        mm(4 + c, 128, T.vq[:], T.vs[:], piece(tq, c), piece(tsc, c), [tn[c], "vq"])
     for c in range(2):
-        act(piece(T.yo, c), bank(c, 128), ACT.Copy, (), ["yo%d" % c], ["b%d" % c])
-    cp(piece(T.yo, 2), bank(2, 128), (), ["yo2"], ["b2"])
+        act(piece(T.yo, c), bank(4 + c, 128), ACT.Copy, (), ["yo%d" % c], ["b%d" % (4 + c)])
+    cp(piece(T.yo, 2), bank(6, 128), (), ["yo2"], ["b6"])
     dma("y", T.oc[:], tq[:].bitcast(dt.uint8), tn, (), "so")
     dma("s", T.y[:], T.yo[:], ["yo0", "yo1", "yo2"], (), "sy")
     for k in range(4):

@@ -4,37 +4,42 @@ from concourse.mybir import dt, AluOpType, AxisListType, ActivationFunctionType
 ALU = AluOpType
 ACT = ActivationFunctionType
 C, L, R = 384, 96, 3
-E = 72
-BIG = float(2 ** 73)
-FREE = float(2 ** 78)
-SINK = 32.0
-RISE = 2048.0
+H = 2 * L
+HIGH = float(2 ** 72)
+DROP = float(2 ** 74)
+FREE = float(2 ** 76)
+SINK = float(2 ** 81)
+RISE = float(2 ** 86)
 LIFT = float(2 ** 22)
 MAGIC = float(3 * 2 ** 22)
 F32, BF, I32, U16, X4, U8 = "float32", "bfloat16", "int32", "uint16", "float8_e4m3fn_x4", "uint8"
-GROUPS = ((0, 1), (2,))
-ALL = (0, 1, 2)
-STEP_ORDER = [("count", (0,)), ("count", (1,)), ("part", ALL), ("count", (2,)), ("hit", (0,)), ("pad", ALL), ("hit", (1,)), ("hit", (2,)),
-              ("cap", (0,)), ("cap", (1,)), ("cap", (2,))]
-PRODUCTS = [(1, 0), (1, 1), (0, 0), (1, 2), (0, 1), (1, 3), (0, 2), (0, 3)]
-MOVES_ON_SCALAR = 7
+SW, KW = 80, 144
+PART = 32 * 4 * C
+LOW = 7.25
+CAPS = 3
 
-TILES = [[21, 22, 23, "E"], [17, 18, 19, 20], [13, 14, 15, 16], [9, 10, 11, 12], [5, 6, 7, 8], [1, 2, 3, 4], [0]]
+PRODUCTS = [(1, 0), (1, 1), (0, 0), (1, 2), (0, 1), (1, 3), (0, 2), (0, 3)]
+EARLY_BANKS, LAST_BANKS = [0, 2, 1, 4, 3, 6, 5, 7], [1, 3, 5, 7, 6, 1, 3, 5]
+MOVES_ON_SCALAR = 8
+ROW_ON_VECTOR = [0]
+
+TILES = [[21, 22, 23, "E"], [17, 18, 19, 20], [13, 14, 15, 16], [9, 10, 11, 12], [5, 6, 7, 8]]
+ROWS = 5
 ON_SCALAR = [23, 22, 21]
-FIRST = 7
-TN = [max(128, 16 * (max(m for m in t if m != "E") + 1)) for t in TILES]
+TN = [16 * (max(m for m in t if m != "E") + 1) for t in TILES]
 TB = [sum(TN[:k]) for k in range(len(TN))]
 CW = sum(TN)
 O_U, O_XS, O_XV, O_OWN, O_OX, O_I = 0, 8, 32, 56, 58, 82
+CYCLE, WAKE, COPY, FILL, CALL, TRAVEL = 0.83, 200, 2200, 11000, 800, 1200
 
-SCRATCH = {"ps": ("psum", [128, 4096], F32), "pen": ("sbuf", [128, 192, 9], BF)}
+SCRATCH = {"ps": ("psum", [128, 4096], F32), "sks": ("sbuf", [128, 3, KW], F32)}
 for _d, _l in (
-    (BF, dict(xin=4 * C, uin=512, vin=512, xs=4 * C, en=516, ep=516, wall=512, q128=128, g512=512,
-              t128=256, wh=3 * E, keep=108, h16=48, horn=C, stp=21 * E, hs=24 * E, ohg=7 * 24, low=E,
-              cap=21 * E, ct=4 * CW, sg=4 * C, sj=8 * 24 * 23, dp=4 * C, win=32 * C, bt=4 * C)),
-    (F32, dict(z=4 * C, pf=24, tq1=48, htab=64, lik=6 * E, run=24 * E, sk=6 * E, sks=6 * E, junk=24, v7=4,
+    (BF, dict(xin=4 * C, uin=512, vin=512, xs=4 * C, en=516, ep=516, wall=512, q128=128, g512=512, t128=256, htab=64, keep=KW,
+              h16=48, horn=C, stp=21 * SW, hs=24 * SW, ohg=21 * 8, one=24 * 8, low=64, cap=CAPS * C, rows=16 * ROWS * ROWS * 2,
+              ct=4 * CW, sg=3 * C, sj=8 * 24 * 23, dp=4 * C, win=32 * C, bt=4 * C)),
+    (F32, dict(z=4 * C, pf=24, tq1=8, wh=66, lik=3 * C, run=24 * 64, sk=3 * KW, junk=48, v7=6,
                yy=96, zz=64, own=32, xe=C, xv=C, srow=C, vrow=C, rs=24, rs2=4, rk=24, m1=C, m2=C, orow=C, olb=2 * C,
-               ot=3 * C, yo=C)),
+               ot=2 * C, yo=C)),
     (X4, dict(uq=128, upq=128, vq=128, wq=512, enq=512, epq=512, waq=256, cq=CW)),
     (U8, dict(us=128, ups=128, vs=128, wsc=512, ens=512, eps=512, was=256, cs=CW)),
     (I32, dict(pi=8, it=128)),
@@ -43,7 +48,7 @@ for _d, _l in (
     for _n, _w in _l.items():
         SCRATCH[_n] = ("sbuf", [128, _w], _d)
 for _t in range(R + 1):
-    for _n, _w in (("t", C), ("b", 2 * L), ("m", C + L))[:1 if _t == R else 3]:
+    for _n, _w in (("t", C), ("b", H), ("m", C + L))[:1 if _t == R else 3]:
         SCRATCH["%sq_%d" % (_n, _t)] = ("sbuf", [128, _w], X4)
         SCRATCH["%ss_%d" % (_n, _t)] = ("sbuf", [128, _w], U8)
 
@@ -52,127 +57,177 @@ for _t in range(R):
     SEMAPHORES += ["rep%d" % _t, "arr0_%d" % _t, "arr1_%d" % _t, "out%d" % _t]
 
 
+def hazards(ops):
+    wrote, read, held = {}, {}, {}
+    for k, o in enumerate(ops):
+        d, after = set(), set()
+        for a in o["r"]:
+            d.update(wrote.get(a, []))
+        for a in o["w"]:
+            d.update(read.get(a, []))
+            d.update(q for q in wrote.get(a, []) if not (o["sem"] and ops[q]["sem"] == o["sem"]))
+        for a in o["x"]:
+            for q in held.get(a, []):
+                (d if ops[q]["e"] != o["e"] else after).add(q)
+        for a in o["r"]:
+            read.setdefault(a, []).append(k)
+        for a in o["w"]:
+            same = [q for q in wrote.get(a, []) if o["sem"] and ops[q]["sem"] == o["sem"]]
+            wrote[a], read[a] = same + [k], []
+        for a in o["x"]:
+            held[a] = [k]
+        o["d"], o["after"] = d - {k}, after - {k}
+
+
+def issue_order(ops):
+    n = len(ops)
+    users = [[] for _ in ops]
+    for k, o in enumerate(ops):
+        for q in o["d"] | o["after"]:
+            users[q].append(k)
+    chain = [0.0] * n
+    for k in reversed(range(n)):
+        chain[k] = ops[k]["busy"] + ops[k]["late"] + max([WAKE * (k in ops[u]["d"]) + chain[u] for u in users[k]] + [0])
+    missing = [len(o["d"] | o["after"]) for o in ops]
+    ready, free, due, order = {}, {}, [0.0] * n, []
+    for k in range(n):
+        if not missing[k]:
+            ready.setdefault(ops[k]["e"], []).append(k)
+    while len(order) < n:
+        offers = []
+        for e, calls in ready.items():
+            if not calls:
+                continue
+            now = max(free.get(e, 0.0), min(due[k] for k in calls))
+            fits = [k for k in calls if due[k] <= now and not any(
+                now < due[q] < now + ops[k]["busy"] - WAKE / 8 and chain[q] > chain[k] + due[q] - now for q in calls)]
+            k = max(fits or calls, key=lambda q: (chain[q] - (0 if fits else due[q]), -q))
+            offers.append((max(now, due[k]), k))
+        start, k = min(offers)
+        o = ops[k]
+        ready[o["e"]].remove(k)
+        order.append(k)
+        free[o["e"]] = start + o["busy"]
+        for u in users[k]:
+            due[u] = max(due[u], start + o["busy"] + (o["late"] + WAKE if k in ops[u]["d"] else 0))
+            missing[u] -= 1
+            if not missing[u]:
+                ready.setdefault(ops[u]["e"], []).append(u)
+    return order
+
+
+def emit(ops, g, T):
+    hazards(ops)
+    order = issue_order(ops)
+    queue = {"v": g.vector, "s": g.scalar, "t": g.tensor, "g": g, "y": g.sync}
+    place = {k: n for n, k in enumerate(order)}
+    groups, total, waited = {}, {}, {}
+    for k, o in enumerate(ops):
+        if o["sem"]:
+            groups.setdefault(o["sem"], []).append(k)
+            total[o["sem"]] = total.get(o["sem"], 0) + o["inc"]
+    known = {e: {} for e in queue}
+    for k in order:
+        o = ops[k]
+        o["waits"], o["knew"] = [], {}
+        if o["fn"] is None:
+            continue
+        kn = known[o["e"]]
+        for q in sorted(o["d"], key=lambda a: -place[a]):
+            p = ops[q]
+            key, pos = (p["sem"], len(ops)) if p["sem"] else (p["e"], place[q])
+            if kn.get(key, -1) >= pos:
+                continue
+            o["waits"].append(q)
+            p["sig"] = True
+            kn[key] = pos
+            for z in groups[p["sem"]] if p["sem"] else [q]:
+                for a, b in ops[z].get("knew", {}).items():
+                    kn[a] = max(kn.get(a, -1), b)
+        o["knew"] = dict(kn)
+    for k in order:
+        o = ops[k]
+        if not o["sem"] and o.get("sig"):
+            name = "e" + o["e"]
+            total[name] = total.get(name, 0) + 1
+            o["val"] = total[name]
+    for k in order:
+        o = ops[k]
+        if o["fn"] is None:
+            continue
+        for q in o["waits"]:
+            p = ops[q]
+            name, val = (p["sem"], total[p["sem"]]) if p["sem"] else ("e" + p["e"], p["val"])
+            queue[o["e"]].wait_ge(T.sem[name], val)
+            waited[name] = max(waited.get(name, 0), val)
+        ins = o["fn"]()
+        if o["sem"] and not o["sem"].startswith("out"):
+            ins.then_inc(T.sem[o["sem"]], 16)
+        elif o.get("sig") and not o["sem"]:
+            ins.then_inc(T.sem["e" + o["e"]], 1)
+    for name, val in total.items():
+        if waited.get(name, 0) < val:
+            g.wait_ge(T.sem[name], val)
+
+
 def rank_program(g, core, T, topo):
     rank = T.rank_of(core)
     if rank is None:
         return
     n_ranks = len(T.cores)
     turn = L * rank
+    back = (24 - turn // 16) % 24
     ops = []
-
-    def op(eng, fn, r=(), w=(), x=(), sem=None, inc=16):
-        ops.append({"e": eng, "fn": fn, "r": list(r), "w": list(w), "x": list(x), "sem": sem, "inc": inc})
-
-    def emit():
-        queue = {"v": g.vector, "s": g.scalar, "t": g.tensor, "g": g, "y": g.sync}
-        wrote, read, held = {}, {}, {}
-        for k, o in enumerate(ops):
-            d = set()
-            for a in o["r"]:
-                d.update(wrote.get(a, []))
-            for a in o["w"]:
-                d.update(read.get(a, []))
-                d.update(q for q in wrote.get(a, []) if not (o["sem"] and ops[q]["sem"] == o["sem"]))
-            for a in o["x"]:
-                d.update(q for q in held.get(a, []) if ops[q]["e"] != o["e"])
-            for a in o["r"]:
-                read.setdefault(a, []).append(k)
-            for a in o["w"]:
-                same = [q for q in wrote.get(a, []) if o["sem"] and ops[q]["sem"] == o["sem"]]
-                wrote[a], read[a] = same + [k], []
-            for a in o["x"]:
-                held[a] = [k]
-            d.discard(k)
-            o["d"] = d
-        known = {e: {} for e in queue}
-        for k, o in enumerate(ops):
-            o["key"] = o["sem"] or o["e"]
-            o["waits"] = []
-            if o["fn"] is None:
-                o["knew"] = {}
-                continue
-            kn = known[o["e"]]
-            for q in sorted(o["d"], reverse=True):
-                p = ops[q]
-                pos = len(ops) if p["sem"] else q
-                if kn.get(p["key"], -1) >= pos:
-                    continue
-                o["waits"].append(q)
-                p["sig"] = True
-                kn[p["key"]] = pos
-                group = [z for z in ops[:k] if z["sem"] == p["sem"]] if p["sem"] else [p]
-                for z in group:
-                    for a, b in z["knew"].items():
-                        if kn.get(a, -1) < b:
-                            kn[a] = b
-            o["knew"] = dict(kn)
-        total, waited = {}, {}
-        for o in ops:
-            if o["sem"]:
-                total[o["sem"]] = total.get(o["sem"], 0) + o["inc"]
-        for o in ops:
-            if not o["sem"] and o.get("sig"):
-                name = "e" + o["e"]
-                total[name] = total.get(name, 0) + 1
-                o["val"] = total[name]
-        for o in ops:
-            if o["fn"] is None:
-                continue
-            for q in o["waits"]:
-                p = ops[q]
-                name, val = (p["sem"], total[p["sem"]]) if p["sem"] else ("e" + p["e"], p["val"])
-                queue[o["e"]].wait_ge(T.sem[name], val)
-                waited[name] = max(waited.get(name, 0), val)
-            ins = o["fn"]()
-            if o["sem"] and not o["sem"].startswith("out"):
-                ins.then_inc(T.sem[o["sem"]], 16)
-            elif o.get("sig") and not o["sem"]:
-                ins.then_inc(T.sem["e" + o["e"]], 1)
-        for name, val in total.items():
-            if waited.get(name, 0) < val:
-                g.wait_ge(T.sem[name], val)
-
     V, S = g.vector, g.scalar
 
-    def ts(out, in0, s1, s2, o0, o1, r, w, x=()):
+    def op(eng, fn, r=(), w=(), x=(), n=64, sem=None, inc=16, late=0):
+        ops.append({"e": eng, "fn": fn, "r": list(r), "w": list(w), "x": list(x), "sem": sem, "inc": inc,
+                    "busy": CYCLE * max(n, 64), "late": late})
+
+    def ts(out, in0, s1, s2, o0, o1, r, w, x=(), n=64):
         if o1 is None:
-            op("v", lambda: V.tensor_scalar(out, in0, s1, None, o0), r, w, x)
+            op("v", lambda: V.tensor_scalar(out, in0, s1, None, o0), r, w, x, n)
         else:
-            op("v", lambda: V.tensor_scalar(out, in0, s1, s2, o0, o1), r, w, x)
+            op("v", lambda: V.tensor_scalar(out, in0, s1, s2, o0, o1), r, w, x, n)
 
-    def tt(out, a, b, o, r, w, x=()):
-        op("v", lambda: V.tensor_tensor(out, a, b, o), r, w, x)
+    def tt(out, a, b, o, r, w, x=(), n=64):
+        op("v", lambda: V.tensor_tensor(out, a, b, o), r, w, x, n)
 
-    def cp(out, a, r, w, x=()):
-        op("v", lambda: V.tensor_copy(out, a), r, w, x)
+    def cp(out, a, r, w, x=(), n=64):
+        op("v", lambda: V.tensor_copy(out, a), r, w, x, n)
 
-    def ms(ap, c, w):
-        op("v", lambda: V.memset(ap, c), (), w)
+    def ms(ap, c, w, n=64):
+        op("v", lambda: V.memset(ap, c), (), w, (), n)
 
-    def scan(out, d0, d1, init, o0, o1, r, w, x=()):
-        op("v", lambda: V.tensor_tensor_scan(out, d0, d1, init, o0, o1), r, w, x)
+    def scan(out, d0, d1, init, o0, o1, r, w, x=(), n=64):
+        op("v", lambda: V.tensor_tensor_scan(out, d0, d1, init, o0, o1), r, w, x, n)
 
-    def tr(out, a, r, w):
-        op("v", lambda: V.transpose(out, a), r, w)
+    def tr(out, a, r, w, n=64):
+        op("v", lambda: V.transpose(out, a), r, w, (), n)
 
-    def quant(q, s, a, r, w):
-        op("v", lambda: V.quantize_mx(q, s, a), r, w)
+    def quant(q, s, a, r, w, n=128):
+        op("v", lambda: V.quantize_mx(q, s, a), r, w, (), n + 16)
 
-    def act(out, a, f, r, w, x=(), **kw):
-        op("s", lambda: S.activation(out, a, f, **kw), r, w, x)
+    def act(out, a, f, r, w, x=(), n=64, **kw):
+        op("s", lambda: S.activation(out, a, f, **kw), r, w, x, n)
 
     def mm(bank, n, lq, ls, rq, rs_, r, start=True, stop=True):
-        op("t", lambda: g.tensor.matmul_mx(T.ps[:, 512 * bank:512 * bank + n], lq, ls, rq, rs_, start, stop), r, (), ["b%d" % bank])
+        op("t", lambda: g.tensor.matmul_mx(T.ps[:, 512 * bank:512 * bank + n], lq, ls, rq, rs_, start, stop), r, (), ["b%d" % bank],
+           (n + 16) * 5 // 4)
 
-    def iota(out, pat, base, ch, w, small=False):
+    def iota(out, pat, base, ch, w, small=True):
+        n = 160 + 2 * pat[0][1] * (pat[1][1] if len(pat) > 1 else 1) * (pat[2][1] if len(pat) > 2 else 1)
         if small:
-            op("g", lambda: g.iota(out, pat, base, ch, allow_small_or_imprecise_dtypes=True), (), w)
+            op("g", lambda: g.iota(out, pat, base, ch, allow_small_or_imprecise_dtypes=True), (), w, (), n)
         else:
-            op("g", lambda: g.iota(out, pat, base, ch), (), w)
+            op("g", lambda: g.iota(out, pat, base, ch), (), w, (), n)
 
-    def dma(eng, out, a, r, w, sem):
-        q = {"y": g.sync, "s": g.scalar, "g": g}[eng]
-        op(eng, lambda: q.dma_start(out, a), r, w, sem=sem)
+    def dma(eng, out, a, r, w, sem, late=COPY):
+        q = {"y": g.sync, "s": g.scalar}[eng]
+        op(eng, lambda: q.dma_start(out, a), r, w, sem=sem, late=late)
+
+    def gathered(n):
+        return 70 + n * 3 // 2
 
     def offs(a, k):
         return T.off[:, a:a + k]
@@ -183,431 +238,299 @@ def rank_program(g, core, T, topo):
     def piece(buf, c, w=128):
         return buf[:, w * c:w * c + w]
 
-    def pc(k):
-        return T.pf[:, k:k + 1]
+    def col(buf, k):
+        return buf[:, k:k + 1]
 
-    def tq1(k):
-        return T.tq1[:, 8 * k:8 * k + 8]
+    def pc(k):
+        return col(T.pf, k)
 
     def runs(first, n):
         first %= C
         cut = min(n, C - first)
         return [(0, first, cut)] + ([(cut, 0, n - cut)] if cut < n else [])
 
-    def weave(main, fill):
-        for f in main:
-            if f is None:
-                if fill:
-                    fill.pop(0)()
-            else:
-                f()
-
     dma("s", T.uin[:], T.u[:], (), ["uin"], "lu")
-    for n, grp in enumerate(GROUPS):
-        for at, col, k in runs(turn + 128 * grp[0], 128 * len(grp)):
-            at += 128 * grp[0]
-            dma("y", T.xin[:, 4 * at:4 * (at + k)], T.x[:, 4 * col:4 * (col + k)], (), ["xin%d" % n], "lx%d" % n)
-    dma("y", T.wq[:].bitcast(dt.uint8), T.wc[:], (), ["w"], "lw")
-    dma("y", T.wsc[:], T.ws[:], (), ["w"], "lw")
-    dma("y", T.vin[:], T.v[:], (), ["vin"], "lv")
+    for n, (first, k) in enumerate(((0, 256), (256, 128))):
+        for a, j, m in runs(turn + first, k):
+            dma("y", T.xin[:, 4 * (first + a):4 * (first + a + m)], T.x[:, 4 * j:4 * (j + m)], (), ["xin%d" % n], "lx%d" % n, COPY + 600 * (n + 1))
+    dma("y", T.wq[:].bitcast(dt.uint8), T.wc[:], ["xin1"], ["w"], "lw")
+    dma("y", T.wsc[:], T.ws[:], ["xin1"], ["w"], "lw")
+    dma("y", T.vin[:], T.v[:], ["xin1"], ["vin"], "lv")
 
-    iota(T.pi[:, 0:1], [[0, 1]], 0, 1, ["p"])
-    iota(T.it[:, 0:8], [[16, 8]], -5, 0, ["it0"])
-    iota(T.q128[:], [[1, 128]], 0, 0, ["q128"], True)
-    iota(T.htab[:], [[0, 8], [-1, 8]], int(MAGIC) - 8, 0, ["htab"], True)
-    iota(T.sk[:, 17:6 * E:18], [[64 * C, 8], [128, 3]], 4 * C * 7 - 64 * C * 8, 1, ["skj"], True)
-    iota(T.it[:, 8:56], [[0, 2], [1, 24]], 0, 0, ["it7"])
-    for q in range(2):
-        iota(T.it[:, 56 + 24 * q:80 + 24 * q], [[2, 3], [12, 4], [6, 2]], 0, 0, ["it4%d" % q])
-    iota(T.it[:, 104:106], [[2, 2]], 0, 0, ["it6"])
-    iota(T.g512[:], [[1, 8], [0, 64]], 0, 0, ["g512"], True)
-    for k, t in enumerate(TILES):
-        lo = 0 if len(t) < 4 else 16 * (min(m for m in t if m != "E") + 1)
-        iota(T.ct[:, 4 * (TB[k] + lo):4 * (TB[k] + TN[k])], [[0, 4 * (TN[k] - lo)]], 0, 0, ["ct%d_%d" % (k, s) for s in range(4)], True)
-
-    ms(T.ep[:], 0.0, ["ep"])
     P_I, P_G, P_I8, P_A, P_F, P_E = range(1, 7)
+    every = [(k, c) for k in range(7) for c in range(3)]
+    iota(T.pi[:, 0:1], [[0, 1]], 0, 1, ["p"], False)
+    iota(T.it[:, 0:8], [[0, 2], [32, 4]], 0, 0, ["it0"], False)
+    iota(T.q128[:], [[1, 128]], 0, 0, ["q128"])
+    iota(T.htab[:], [[0, 8], [-1, 8]], 136, 0, ["htab"])
+    iota(T.htab[:, 0:64:8], [[0, 8]], 128, 0, ["htab"])
+    iota(T.stp[:, 7:21 * SW:SW], [[0, 21]], 0, 0, ["stp_a"])
+    for e in (72, 73):
+        iota(T.stp[:, e:21 * SW:SW], [[0, 21]], 1, 0, ["stp_%d" % e])
+    for h in range(8):
+        rest = 16 - LOW + (8 - h if h else 0) - (7 if h else 8) / 32
+        iota(T.sk[:, 18 * h + 17:3 * KW:KW], [[128, 3]], -int(PART * rest), 1, ["skj%d" % h])
+    iota(T.it[:, 8:56], [[0, 2], [1, 24]], 0, 0, ["it7"], False)
+    iota(T.it[:, 104:106], [[4, 2]], 0, 0, ["it6"], False)
+    for q in range(2):
+        iota(T.it[:, 56 + 24 * q:80 + 24 * q], [[4, 3], [12, 4], [2, 2]], 0, 0, ["it4%d" % q], False)
+    iota(T.g512[:], [[1, 8], [0, 64]], 0, 0, ["g512"])
+    iota(T.keep[:], [[0, KW]], 1, 0, ["keep"])
+    iota(T.keep[:, 0:KW:9], [[0, 16]], 0, 0, ["keep"])
+    iota(T.keep[:, 17:KW:18], [[0, 8]], PART, 0, ["keep"])
+    iota(T.yy[:, 48:64], [[0, 16]], 0, 0, ["ypad"])
+    iota(T.sk[:, 8:3 * KW:18], [[0, 24]], 0, 0, ["skz"])
+    iota(T.hs[:, 21 * SW:24 * SW], [[0, 3 * SW]], 0, 0, ["hs_last"])
+    iota(T.en[:], [[0, 516]], 0, 0, ["en"])
+    for k, t in enumerate(TILES):
+        lo = 16 * (min(m for m in t if m != "E") + 1)
+        iota(T.ct[:, 4 * (TB[k] + lo):4 * (TB[k] + TN[k])], [[0, 4 * (TN[k] - lo)]], 0, 0, ["ct%d_%d" % (k, s) for s in range(4)])
 
-    def digit(col, sh, mask):
-        ts(T.pi[:, col:col + 1], T.pi[:, 0:1], sh, mask, ALU.logical_shift_right, ALU.bitwise_and, ["p"], ["pi%d" % col])
-
-    def unpacker(b):
-        quant(piece(T.epq, b), piece(T.eps, b), T.ep[:, 3 - b:515 - b], ["ep"], ["epq%d" % b])
-
-    for col, sh, mask in ((P_I, 0, 15), (P_G, 4, 7), (P_I8, 3, 1), (P_A, 1, 3)):
-        digit(col, sh, mask)
-    cp(T.pf[:, 0:3], T.pi[:, 0:3], ["p", "pi1", "pi2"], ["pf0"])
-    digit(P_F, 0, 1)
-    digit(P_E, 4, 1)
-    ts(tq1(1), T.it[:, 0:8], pc(P_I), 1.0 / 9, ALU.add, ALU.mult, ["pf0", "it0"], ["ub"])
-    ts(pc(10), pc(P_I), 8.0, pc(P_G), ALU.mult, ALU.add, ["pf0"], ["pf10"])
-    ts(tq1(0), T.it[:, 0:8], pc(P_I), 4.0, ALU.add, ALU.add, ["pf0", "it0"], ["ua"])
-    ts(tq1(2), tq1(1), MAGIC, MAGIC, ALU.add, ALU.subtract, ["ub"], ["uc"])
-    ts(T.ep[:, 3:515:4], T.q128[:], pc(10), None, ALU.is_equal, None, ["pf10", "q128", "ep"], ["ep"])
-    ms(T.wh[:], 1.0, ["wh"])
-    ts(tq1(3), tq1(2), 9.0, 7.0, ALU.mult, ALU.add, ["uc"], ["ud"])
-    ts(tq1(4), tq1(2), 7.0, None, ALU.mult, None, ["uc"], ["ue"])
-    ms(T.low[:], -BIG, ["low"])
-    tt(tq1(3), tq1(3), tq1(0), ALU.min, ["ud", "ua"], ["ud"])
-    unpacker(0)
-    tt(tq1(4), tq1(4), tq1(3), ALU.add, ["ud", "ue"], ["ue"])
-    unpacker(1)
-    ts(offs(O_U, 8), tq1(4), 127.0, 0.0, ALU.min, ALU.max, ["ue"], ["o_u"])
-    cp(T.pf[:, 3:7], T.pi[:, 3:7], ["pf0"] + ["pi%d" % c for c in range(3, 7)], ["pf"])
-    ms(T.wh[:, 0:3 * E:9], -8.0625, ["wh"])
-    ms(T.stp[:, 0:21 * E:E], 0.0, ["stp%d_%d" % (k, c) for k in range(7) for c in range(3)])
-    unpacker(2)
-    ms(T.wh[:, E - 1:3 * E:E], -15.0, ["wh"])
+    ms(T.ep[:], 0.0, ["ep"], 258)
+    ms(T.low[:], -HIGH, ["low"])
+    ms(T.wh[:, 0:64], 1.0, ["wh"])
+    ms(T.wh[:, 0:64:8], -7 - 1 / 32, ["wh"])
+    ms(T.wh[:, 64:65], -LOW, ["wh64"])
+    ms(T.wh[:, 65:66], 128 + LOW, ["wh65"])
+    ms(T.lik[:, 0:C:2], HIGH, ["pads"], 192)
+    for k in range(CAPS):
+        ms(T.cap[:, C * k:C * k + C:2], FREE, ["cap%d_%d%s" % (k, c, a) for c in range(3) for a in ("", "p")], 96)
+    for k, sh, mask in ((P_I, 0, 15), (P_G, 4, 7), (P_I8, 3, 1), (P_A, 1, 3), (P_F, 0, 1), (P_E, 4, 1)):
+        ts(col(T.pi, k), T.pi[:, 0:1], sh, mask, ALU.logical_shift_right, ALU.bitwise_and, ["p"], ["pi%d" % k])
+    cp(T.pf[:, 0:7], T.pi[:, 0:7], ["p"] + ["pi%d" % k for k in range(1, 7)], ["pf"])
+    ts(pc(8), pc(P_I8), 8.0, pc(P_I), ALU.mult, ALU.add, ["pf"], ["pf8"])
+    ts(pc(10), pc(P_I), 8.0, pc(P_G), ALU.mult, ALU.add, ["pf"], ["pf10"])
+    ts(offs(O_U, 8), T.it[:, 0:8], pc(8), None, ALU.add, None, ["pf8", "it0"], ["o_u"])
     quant(T.uq[:], T.us[:], T.uin[:], ["uin"], ["uq"])
-    unpacker(3)
-    op("v", lambda: V.tensor_copy(T.upq[:].bitcast(dt.uint32), T.uq[:].bitcast(dt.uint32).indirect(offs(O_U, 8))), ["uq", "o_u"], ["upq"])
-    op("s", lambda: S.activation(T.ups[:], T.us[:].indirect(offs(O_U, 8)), ACT.Copy), ["uq", "o_u"], ["ups"])
-
-    back = (24 - turn // 16) % 24
-    later = [
-        lambda: ts(pc(15), pc(P_I), 15.0, LIFT, ALU.not_equal, ALU.mult, ["pf"], ["pf15"]),
-        lambda: act(pc(11), pc(P_A), ACT.Identity, ["pf"], ["pf11"], scale=6.0, bias=pc(P_I8)),
-        lambda: act(pc(14), pc(P_G), ACT.Identity, ["pf"], ["pf14"], scale=16.0, bias=15.0),
-        lambda: act(pc(17), pc(P_I), ACT.Identity, ["pf"], ["pf17"], bias=1.0),
-        lambda: act(pc(12), pc(P_E), ACT.Identity, ["pf", "pf11"], ["pf12"], scale=3.0, bias=pc(11)),
-        lambda: ts(pc(18), pc(15), 1.0, None, ALU.max, None, ["pf15"], ["pf18"]),
-        lambda: ts(T.h16[:, 0:16], T.q128[:, 0:16], pc(P_I), None, ALU.not_equal, None, ["pf", "q128"], ["h16a"]),
-        lambda: ts(T.h16[:, 16:32], T.q128[:, 0:16], pc(17), LIFT, ALU.is_equal, ALU.mult, ["pf17", "q128"], ["h16b"]),
-        lambda: ts(pc(13), pc(P_F), pc(P_E), None, ALU.is_equal, None, ["pf"], ["pf13"]),
-        lambda: tt(T.h16[:, 32:48], T.h16[:, 0:16], T.h16[:, 16:32], ALU.max, ["h16a", "h16b"], ["h16c"]),
-        lambda: ts(offs(O_I, 24), T.it[:, 8:32], 0.0, pc(P_I), ALU.mult, ALU.add, ["it7", "pf"], ["o_i"]),
-        lambda: ts(pc(16), pc(P_I), 15.0, 1.0 / LIFT, ALU.is_equal, ALU.max, ["pf"], ["pf16"]),
-        lambda: ts(T.t128[:, 0:128], T.q128[:], pc(0), None, ALU.is_gt, None, ["pf", "q128"], ["t128a"]),
-        lambda: ts(T.t128[:, 128:256], T.q128[:], pc(14), None, ALU.is_le, None, ["pf14", "q128"], ["t128b"]),
-        lambda: ts(T.tq1[:, 40:42], T.it[:, 104:106], pc(12), None, ALU.add, None, ["pf12", "it6"], ["tq1a"]),
-        lambda: cp(offs(O_XS, 24), T.it[:, 56 + back:80 + back], ["it40", "it41"], ["o_xs"]),
-        lambda: ts(T.wall[:], T.g512[:], pc(P_G), None, ALU.is_equal, None, ["pf", "g512"], ["wall"]),
-        lambda: ts(T.tq1[:, 42:44], T.tq1[:, 40:42], 64.0, pc(13), ALU.subtract, ALU.mult, ["tq1a", "pf13"], ["tq1b"]),
-        lambda: quant(T.waq[:, 0:128], T.was[:, 0:128], T.wall[:], ["wall"], ["waq0"]),
-        lambda: tt(T.tq1[:, 44:46], T.tq1[:, 40:42], T.tq1[:, 42:44], ALU.add, ["tq1a", "tq1b"], ["tq1c"]),
-        lambda: tt(T.wall[:, 3:512:4], T.t128[:, 0:128], T.t128[:, 128:256], ALU.mult, ["t128a", "t128b"], ["wall"]),
-        lambda: ts(offs(O_OWN, 2), T.tq1[:, 44:46], 64.0, None, ALU.add, None, ["tq1c"], ["o_own"]),
-        lambda: quant(T.waq[:, 128:256], T.was[:, 128:256], T.wall[:], ["wall"], ["waq1"]),
-        lambda: cp(offs(O_OX, 24), T.it[:, 8 + back:32 + back], ["it7"], ["o_ox"]),
-        lambda: ts(offs(O_XV, 24), T.it[:, 56 + back:80 + back], 1.0, None, ALU.add, None, ["it40", "it41"], ["o_xv"]),
-        lambda: ms(T.keep[:], 1.0, ["keep"]),
-        lambda: ms(T.yy[:, 48:64], 0.0, ["ypad"]),
-        lambda: ms(T.keep[:, 0:108:9], 0.0, ["keep"]),
-        lambda: ms(T.sk[:, 8:6 * E:18], 0.0, ["skj"]),
-        lambda: ms(T.hs[:, 21 * E:24 * E], 0.0, ["hs_last"]),
-        lambda: ms(T.keep[:, 17:108:18], 64.0 * C, ["keep"]),
-        lambda: ms(T.rs[:, 0:1], 0.0, ["rs0"]),
-        lambda: act(pc(19), pc(18), ACT.Copy, ["pf18"], ["pf19"], scale=-1.0),
-    ] + [lambda n=n, m=m: act(pc(20 + n), pc(18), ACT.Copy, ["pf18"], ["pf%d" % (20 + n)], scale=16.0 * m) for n, m in enumerate(ON_SCALAR)]
-    spare = [lambda: ms(T.en[:], 0.0, ["en"]),
-             lambda: ts(T.en[:, 3:515:4], T.q128[:], pc(0), None, ALU.is_equal, None, ["pf", "q128", "en"], ["en"])]
-    spare += [lambda b=b: quant(piece(T.enq, b), piece(T.ens, b), T.en[:, 3 - b:515 - b], ["en"], ["enq%d" % b]) for b in range(4)]
-    spare += [lambda: quant(T.vq[:], T.vs[:], T.vin[:], ["vin"], ["vq"])]
-
-    def gap():
-        weave([None], spare)
+    op("v", lambda: V.tensor_copy(T.upq[:].bitcast(dt.uint32), T.uq[:].bitcast(dt.uint32).indirect(offs(O_U, 8))), ["uq", "o_u"], ["upq"], (), gathered(128))
+    op("s", lambda: S.activation(T.ups[:], T.us[:].indirect(offs(O_U, 8)), ACT.Copy), ["uq", "o_u"], ["ups"], (), gathered(128))
+    for e, q, s, at, name in ((T.ep, T.epq, T.eps, 10, "ep"), (T.en, T.enq, T.ens, 0, "en")):
+        ts(e[:, 3:515:4], T.q128[:], pc(at), None, ALU.is_equal, None, ["pf", "pf10", "q128", name], [name])
+        for b in range(4):
+            quant(piece(q, b), piece(s, b), e[:, 3 - b:515 - b], [name], ["%sq%d" % (name, b)])
+    quant(T.vq[:], T.vs[:], T.vin[:], ["vin"], ["vq"])
+    act(pc(17), pc(P_I), ACT.Identity, ["pf"], ["pf17"], bias=1.0)
+    act(pc(14), pc(P_G), ACT.Identity, ["pf"], ["pf14"], scale=16.0, bias=15.0)
+    act(pc(11), pc(P_A), ACT.Identity, ["pf"], ["pf11"], scale=3.0, bias=pc(P_I8))
+    act(pc(12), pc(11), ACT.Identity, ["pf", "pf11"], ["pf12"], scale=2.0, bias=pc(P_E))
+    ts(pc(15), pc(P_I), 15.0, LIFT, ALU.not_equal, ALU.mult, ["pf"], ["pf15"])
+    ts(pc(18), pc(15), 1.0, None, ALU.max, None, ["pf15"], ["pf18"])
+    ts(pc(16), pc(P_I), 15.0, 1.0 / LIFT, ALU.is_equal, ALU.max, ["pf"], ["pf16"])
+    ts(pc(13), pc(P_F), pc(P_E), None, ALU.is_equal, None, ["pf"], ["pf13"])
+    act(pc(19), pc(18), ACT.Copy, ["pf18"], ["pf19"], scale=-1.0)
+    for n, m in enumerate(ON_SCALAR):
+        act(pc(20 + n), pc(18), ACT.Copy, ["pf18"], ["pf%d" % (20 + n)], scale=16.0 * m)
+    ts(T.h16[:, 0:16], T.q128[:, 0:16], pc(P_I), None, ALU.not_equal, None, ["pf", "q128"], ["h16a"])
+    ts(T.h16[:, 16:32], T.q128[:, 0:16], pc(17), LIFT, ALU.is_equal, ALU.mult, ["pf17", "q128"], ["h16b"])
+    tt(T.h16[:, 32:48], T.h16[:, 0:16], T.h16[:, 16:32], ALU.max, ["h16a", "h16b"], ["h16c"])
+    ts(offs(O_I, 24), T.it[:, 8:32], 0.0, pc(P_I), ALU.mult, ALU.add, ["it7", "pf"], ["o_i"])
+    for q in range(4):
+        act(piece(T.horn, q, L), T.h16[:, 32:48].indirect(offs(O_I, 6)), ACT.Copy, ["h16c", "o_i"], ["horn%d" % q], n=gathered(L))
+    horn = ["horn%d" % q for q in range(4)]
+    ts(T.t128[:, 0:128], T.q128[:], pc(0), None, ALU.is_gt, None, ["pf", "q128"], ["t128a"])
+    ts(T.t128[:, 128:256], T.q128[:], pc(14), None, ALU.is_le, None, ["pf14", "q128"], ["t128b"])
+    for q in range(2):
+        ts(piece(T.wall, q, 256), piece(T.g512, q, 256), pc(P_G), None, ALU.is_equal, None, ["pf", "g512"], ["wall%d" % q], n=128)
+    quant(T.waq[:, 0:128], T.was[:, 0:128], T.wall[:], ["wall0", "wall1"], ["waq0"])
+    for q in range(2):
+        tt(T.wall[:, 256 * q + 3:256 * q + 256:4], piece(T.t128, q, 64), piece(T.t128, 2 + q, 64), ALU.mult, ["t128a", "t128b"], ["wall%d" % q], n=128)
+    quant(T.waq[:, 128:256], T.was[:, 128:256], T.wall[:], ["wall0", "wall1"], ["waq1"])
+    ts(T.tq1[:, 0:2], T.it[:, 104:106], pc(12), None, ALU.add, None, ["pf12", "it6"], ["tq1a"])
+    ts(T.tq1[:, 2:4], T.tq1[:, 0:2], 64.0, pc(13), ALU.subtract, ALU.mult, ["tq1a", "pf13"], ["tq1b"])
+    tt(T.tq1[:, 4:6], T.tq1[:, 0:2], T.tq1[:, 2:4], ALU.add, ["tq1a", "tq1b"], ["tq1c"])
+    ts(offs(O_OWN, 2), T.tq1[:, 4:6], 64.0, None, ALU.add, None, ["tq1c"], ["o_own"])
+    cp(offs(O_XS, 24), T.it[:, 56 + back:80 + back], ["it40", "it41"], ["o_xs"])
+    ts(offs(O_XV, 24), T.it[:, 56 + back:80 + back], 1.0, None, ALU.add, None, ["it40", "it41"], ["o_xv"])
+    cp(offs(O_OX, 24), T.it[:, 8 + back:32 + back], ["it7"], ["o_ox"])
 
     def quant_piece(t, c, tile, r):
-        quant(piece(T["tq_%d" % t], c), piece(T["ts_%d" % t], c), piece(tile, c, 512), r, ["t%d_%d" % (t, c)])
+        tq, tsc, name = piece(T["tq_%d" % t], c), piece(T["ts_%d" % t], c), "t%d_%d" % (t, c)
+        quant(tq, tsc, piece(tile, c, 512), r, [name])
+        if t < R:
+            mm(2 * c, 128, tq, tsc, T.upq[:], T.ups[:], [name, "upq", "ups"])
 
-    def at(buf, k, c, n=1):
-        return buf[:, 3 * E * k + E * c:3 * E * k + E * (c + n)]
+    def match(c):
+        def likings(k):
+            n = 0 if k == 0 else 1 + k % 2
+            return piece(T.lik, 3 * n + c), T.lik[:, C * n + 128 * c + 1:C * n + 128 * c + 128:2], "lik%d_%d" % (n, c)
 
-    def names(a, k, cs):
-        return ["%s%d_%d" % (a, k, c) for c in cs]
+        def record(k, top, count, r):
+            a, one = KW * c + k, piece(T.one, 3 * k + c, 8)
+            act(T.sk[:, a + 9:KW * c + KW:18], one, ACT.Relu, r + ["one%d_%d" % (k, c)], ["sk1_%d_%d" % (k, c)], scale=16.0, bias=count)
+            if top is not None:
+                act(T.sk[:, a:KW * c + KW:18], one, ACT.Copy, r + ["one%d_%d" % (k, c)], ["sk0_%d_%d" % (k, c)], scale=top)
 
-    def top(k, c):
-        return T.run[:, 3 * E * k + E * c + E - 1:3 * E * k + E * c + E]
-
-    def voice(k, c):
-        return T.hs[:, 3 * E * k + E * c + E - 1:3 * E * k + E * c + E] if k < 7 else T.v7[:, c:c + 1]
-
-    def most(k, c):
-        if k:
-            scan(at(T.run, k, c), T.low[:], at(T.lik, k % 2, c), -BIG, ALU.max, ALU.max, ["low", "lik%d_%d" % (k % 2, c)], ["run%d_%d" % (k, c)])
-        else:
-            scan(T.run[:, E * c + 1:E * c + E], T.low[:, 1:E], bank(2 * c, E, 1), -BIG, ALU.max, ALU.max, ["low"], ["run0_%d" % c], ["b%d" % (2 * c)])
-
-    def keep_likings():
-        for c in range(3):
-            act(at(T.lik, 0, c), bank(2 * c, E), ACT.Copy, (), ["lik0_%d" % c], ["b%d" % (2 * c)])
-        act(T.lik[:, 0:3 * E:9], T.low[:, 0:24], ACT.Copy, ["low"], names("lik", 0, range(3)))
-
-    def step(k, c):
-        a = 3 * E * k + E * c
-        ts(T.stp[:, a + 1:a + E], T.run[:, a + 1:a + E], top(k, c), None, ALU.is_ge, None, ["run%d_%d" % (k, c)], ["stp%d_%d" % (k, c)])
-
-    def ones(k, cs):
-        scan(at(T.hs, k, cs[0], len(cs)), T.wh[:, 0:len(cs) * E], at(T.stp, k, cs[0], len(cs)), 0.0, ALU.add, ALU.mult,
-             names("stp", k, cs) + ["wh"], names("hs", k, cs))
-
-    def part(k, cs):
-        a = 3 * E * k
-        tt(piece(T.ohg, k, 24), T.stp[:, a + 8:a + 3 * E:9], T.stp[:, a:a + 3 * E:9], ALU.subtract, names("stp", k, cs), ["ohg%d" % k])
-
-    def pad(k, cs):
-        ts(T.pen[:, 24 * k:24 * k + 24, 0], piece(T.ohg, k, 24), RISE + SINK, RISE, ALU.mult, ALU.subtract, ["ohg%d" % k], ["pad%d" % k])
-
-    def hit(k, cs):
-        c = cs[0]
-        row, rows = 24 * k + 8 * c, 8 if k < 7 else 1
-        ts(T.pen[:, row:row + rows, 1:9], T.htab[:, 0:8 * rows], voice(k, c), MAGIC, ALU.subtract, ALU.is_equal,
-           ["hs%d_%d" % (k, c), "htab"], ["pen%d_%d" % (k, c)])
-
-    def cap(k, cs):
-        row = 24 * k + 8 * cs[0]
-        ts(at(T.cap, k, cs[0], len(cs)), T.pen[:, row:row + 8 * len(cs), :], -(FREE + BIG), FREE, ALU.mult, ALU.add,
-           names("pen", k, cs) + ["pad%d" % k], names("cap", k, cs))
-
-    def sink(k, c):
-        scan(at(T.lik, (k + 1) % 2, c), at(T.cap, k, c), at(T.lik, k % 2, c), 0.0, ALU.add, ALU.min,
-             ["cap%d_%d" % (k, c), "lik%d_%d" % (k % 2, c)], ["lik%d_%d" % ((k + 1) % 2, c)])
-
-    def record(k, c):
-        one, r, a = T.pen[:, 24 * k + 8 * c, 1:9], ["pen%d_%d" % (k, c)], 18 * c + k
-        act(T.sk[:, a + 9:6 * E:54], one, ACT.Relu, r + ["hs%d_%d" % (k, c)], ["sk1_%d_%d" % (k, c)], scale=16.0, bias=voice(k, c))
-        if k < 7:
-            act(T.sk[:, a:6 * E:54], one, ACT.Copy, r + ["run%d_%d" % (k, c)], ["sk0_%d_%d" % (k, c)], scale=top(k, c))
-
-    def last_voice():
-        for c in range(3):
-            act(piece(T.junk, c, 8), T.hs[:, E * c + E - 1:24 * E:3 * E], ACT.Identity, ["hs%d_%d" % (k, c) for k in range(7)] + ["hs_last"],
-                ["hs7_%d" % c], scale=-1.0, bias=-(92 + 28 / 16) / 8, accum_out=T.v7[:, c:c + 1])
+        for k in range(7):
+            n, tag = 3 * k + c, "%d_%d" % (k, c)
+            run, top, s, cap = piece(T.run, n, 64), col(T.run, 64 * n + 63), SW * n, C * (k % CAPS) + 128 * c
+            caps = "cap%d_%d" % (k % CAPS, c)
+            whole, entries, lik = likings(k)
+            if k:
+                scan(run, T.low[:], entries, -HIGH, ALU.max, ALU.max, ["low", lik], ["run" + tag])
+            else:
+                scan(run, T.low[:], bank(2 * c, 64), -HIGH, ALU.max, ALU.max, ["low"], ["run" + tag], ["b%d" % (2 * c)])
+                act(entries, bank(2 * c, 64), ACT.Copy, ["pads"], [lik], ["b%d" % (2 * c)])
+            ts(T.stp[:, s + 8:s + 72], run, top, None, ALU.is_ge, None, ["run" + tag], ["stp" + tag])
+            tt(piece(T.ohg, n, 8), T.stp[:, s + 15:s + 72:8], T.stp[:, s + 7:s + 64:8], ALU.subtract, ["stp" + tag, "stp_a"], ["ohg" + tag])
+            act(T.cap[:, cap:cap + 128:16], piece(T.ohg, n, 8), ACT.Identity, ["ohg" + tag], [caps + "p"], scale=-(RISE + SINK), bias=RISE)
+            scan(T.hs[:, s:s + 66], T.wh[:], T.stp[:, s + 8:s + 74], 0.0, ALU.add, ALU.mult,
+                 ["stp" + tag, "stp_72", "stp_73", "wh", "wh64", "wh65"], ["hs" + tag])
+            ts(T.cap[:, cap + 1:cap + 128:2], T.htab[:], col(T.hs, s + 65), -DROP, ALU.is_equal, ALU.mult, ["hs" + tag, "htab"], [caps])
+            act(piece(T.one, n, 8), T.cap[:, cap + 1:cap + 16:2], ACT.Copy, [caps], ["one" + tag], scale=-1.0 / DROP)
+            record(k, top, col(T.hs, s + 64), ["run" + tag, "hs" + tag])
+            scan(likings(k + 1)[0], T.cap[:, cap:cap + 128], whole, 0.0, ALU.add, ALU.min, [caps, caps + "p", lik], [likings(k + 1)[2]], n=128)
+        counts, top = ["hs%d_%d" % (k, c) for k in range(7)] + ["hs_last"], col(T.run, 64 * (21 + c) + 63)
+        for w, total in enumerate((28 - 29 / 32 - 8 * LOW, 8 * 128 + 28)):
+            act(piece(T.junk, 2 * c + w, 8), T.hs[:, SW * c + 64 + w:24 * SW:3 * SW], ACT.Identity, counts, ["v7_%d_%d" % (w, c)],
+                scale=-1.0, bias=total / 8, accum_out=col(T.v7, 2 * c + w))
+        ts(piece(T.one, 21 + c, 8), T.htab[:, 0:8], col(T.v7, 2 * c + 1), None, ALU.is_equal, None, ["v7_1_%d" % c, "htab"], ["one7_%d" % c])
+        record(7, None, col(T.v7, 2 * c), ["v7_0_%d" % c])
+        op("v", lambda: V.tensor_reduce(top, likings(7)[1], AxisListType.X, ALU.max), [likings(7)[2]], ["run7_%d" % c])
+        ts(T.sk[:, KW * c + 7:KW * c + KW:18], piece(T.one, 21 + c, 8), top, None, ALU.mult, None, ["one7_%d" % c, "run7_%d" % c], ["sk0_7_%d" % c])
+        scan(T.sks[:, c, :], T.keep[:], piece(T.sk, c, KW), 0.0, ALU.mult, ALU.add,
+             ["keep", "skz"] + ["skj%d" % h for h in range(8)] + ["sk%d_%d_%d" % (w, k, c) for w in range(2) for k in range(8)], ["sks%d" % c], n=KW)
 
     def one_round(t):
         tq, tsc, tn = T["tq_%d" % t], T["ts_%d" % t], ["t%d_%d" % (t, c) for c in range(3)]
         for c in range(3):
-            mm(2 * c, 128, piece(tq, c), piece(tsc, c), T.upq[:], T.ups[:], [tn[c], "upq", "ups"])
+            match(c)
         for b in range(4):
             mm(2 * b + 1, C, piece(T.epq, b), piece(T.eps, b), tq[:], tsc[:], tn + ["epq%d" % b])
-
-        def unpack(b):
-            act(piece(T.dp, b, C), bank(2 * b + 1, C), ACT.Copy, (), ["dp%d" % b], ["b%d" % (2 * b + 1)])
-
-        def replicate():
-            for h in range(8):
-                dma("y", T.win[16 * h:16 * h + 16, :], T.dp[:], ["dp%d" % b for b in range(4)], ["win"], "rep%d" % t)
-
-        for k in range(7):
-            for f in (most, step):
-                for c in range(3):
-                    f(k, c)
-            if k == 0:
-                keep_likings()
-            if k < 2:
-                unpack(2 * k)
-                unpack(2 * k + 1)
-            if k == 1:
-                replicate()
-            weave([None] * 2, later)
-            for f, cs in STEP_ORDER:
-                {"count": ones, "part": part, "pad": pad, "hit": hit, "cap": cap}[f](k, cs)
-            if k == 6:
-                last_voice()
             for c in range(3):
-                record(k, c)
-            weave([None] * 3, later)
-            if k == 6:
-                for c in range(3):
-                    hit(7, (c,))
-                    record(7, c)
-            for c in range(3):
-                sink(k, c)
-            if t == 0 and k in (4, 5):
-                act(piece(T.horn, k - 4, 192), T.h16[:, 32:48].indirect(offs(O_I, 12)), ACT.Copy, ["h16c", "o_i"], ["horn%d" % (k - 4)])
-        for c in range(3):
-            op("v", lambda c=c: V.tensor_reduce(top(7, c), at(T.lik, 1, c), AxisListType.X, ALU.max), ["lik1_%d" % c], ["run7_%d" % c])
-        for c in range(3):
-            ts(T.sk[:, 18 * c + 7:6 * E:54], T.pen[:, 168 + 8 * c, 1:9], top(7, c), None, ALU.mult, None, ["pen7_%d" % c, "run7_%d" % c], ["sk0_7_%d" % c])
-        weave([None] * len(later), later)
-        for b in range(4):
-            scan(piece(T.sks, b, 108), T.keep[:], piece(T.sk, b, 108), 0.0, ALU.mult, ALU.add,
-                 ["keep", "skj"] + ["sk%d_%d_%d" % (w, k, c) for w in range(2) for k in range(8) for c in range(3)], ["sks%d" % b])
+                act(piece(T.dp, 3 * b + c), bank(2 * b + 1, 128 * c + 128, 128 * c), ACT.Copy, (), ["dp%d_%d" % (b, c)], ["b%d" % (2 * b + 1)], n=128)
+        for h in range(8):
+            dma("y", T.win[16 * h:16 * h + 16, :], T.dp[:], ["dp%d_%d" % (b, c) for b in range(4) for c in range(3)], ["win"], "rep%d" % t, FILL)
 
-        yy = []
+        yy = ["ypad"]
         for n in range(16):
             b, a = divmod(n, 4)
-            src, dst = T.sks[32 * a:32 * a + 32, 108 * b + 8:108 * b + 108:9], T.yy[32 * b:32 * b + 32, 12 * a:12 * a + 12]
+            src, dst = T.sks[32 * a:32 * a + 32, :, 36 * b + 8:36 * b + 36:9], T.yy[32 * b:32 * b + 32, 12 * a:12 * a + 12]
             yy.append("yy%d_%d" % (a, b))
             if n >= MOVES_ON_SCALAR:
-                cp(dst, src, ["sks%d" % b], [yy[-1]])
+                cp(dst, src, ["sks0", "sks1", "sks2"], [yy[-1]])
             else:
-                act(dst, src, ACT.Copy, ["sks%d" % b], [yy[-1]])
-        tr(T.zz[:, 0:32], T.yy[:, 0:64:2], yy + ["ypad"], ["zz0"])
-        tr(T.zz[:, 32:64], T.yy[:, 0:64:2], yy + ["ypad"], ["zz1"])
-        act(T.xe[:, 128:C], T.yy[:, 0:64].indirect(offs(O_XS + 8, 16)), ACT.Copy, yy + ["ypad", "o_xs"], ["xe1"])
-        cp(T.xe[:, 0:128], T.yy[:, 0:64].indirect(offs(O_XS, 8)), yy + ["ypad", "o_xs"], ["xe0"])
+                act(dst, src, ACT.Copy, ["sks0", "sks1", "sks2"], [yy[-1]])
+        tr(T.zz[:, 0:32], T.yy[:, 0:64:2], yy, ["zz0"])
+        tr(T.zz[:, 32:64], T.yy[:, 0:64:2], yy, ["zz1"])
         tr(T.yy[:, 64:96], T.zz[:, 16:48], ["zz0", "zz1"], ["ysw"])
-        tr(T.srow[:, 0:128], T.xe[:, 0:128], ["xe0"], ["srow0"])
-        cp(T.own[:], T.yy[:].indirect(offs(O_OWN, 2)), yy + ["ypad", "ysw", "o_own"], ["own"])
-        tr(T.srow[:, 128:C], T.xe[:, 128:C], ["xe1"], ["srow1"])
-        act(T.xv[:], T.yy[:, 0:64].indirect(offs(O_XV, 24)), ACT.Copy, yy + ["ypad", "o_xv"], ["xv"])
-        srow = ["srow0", "own", "srow1"]
+        cp(T.own[:], T.yy[:].indirect(offs(O_OWN, 2)), yy + ["ysw", "o_own"], ["own"], n=gathered(32))
+        for c in range(3):
+            if c in ROW_ON_VECTOR:
+                cp(piece(T.xe, c), T.yy[:, 0:64].indirect(offs(O_XS + 8 * c, 8)), yy + ["o_xs"], ["xe%d" % c], n=gathered(128))
+            else:
+                act(piece(T.xe, c), T.yy[:, 0:64].indirect(offs(O_XS + 8 * c, 8)), ACT.Copy, yy + ["o_xs"], ["xe%d" % c], n=gathered(128))
+            tr(piece(T.srow, c), piece(T.xe, c), ["xe%d" % c], ["srow%d" % c], 128)
+        act(T.xv[:], T.yy[:, 0:64].indirect(offs(O_XV, 24)), ACT.Copy, yy + ["o_xv"], ["xv"], n=gathered(C))
+        vrow = ["vrow%d" % n for n in range(4)]
+        for n in range(4):
+            tr(piece(T.vrow, n, L), piece(T.xv, n, L), ["xv"], [vrow[n]], L)
 
         def own(m):
-            return T.own[:, (m + back) % 24:(m + back) % 24 + 1]
+            return col(T.own, (m + back) % 24)
 
         def slot(k, s, a, b):
             return T.ct[:, 4 * (TB[k] + a) + s:4 * (TB[k] + b):4]
 
-        def squeeze(k):
-            quant(T.cq[:, TB[k]:TB[k] + TN[k]], T.cs[:, TB[k]:TB[k] + TN[k]], T.ct[:, 4 * TB[k]:4 * (TB[k] + TN[k])],
-                  ["ct%d_%d" % (k, s) for s in range(4)] + ["cd%d" % m for m in TILES[k] if m in ON_SCALAR], ["cq%d" % k])
-
-        def count(k):
-            w = 128 if "E" in TILES[k] else 0
-            mm(7, TN[k], T.waq[:, w:w + 128], T.was[:, w:w + 128], T.cq[:, TB[k]:TB[k] + TN[k]], T.cs[:, TB[k]:TB[k] + TN[k]],
-               ["cq%d" % k, "waq%d" % (w // 128)], k == 0, k == len(TILES) - 1)
-
-        def compare(m):
-            k, s = where[m]
-            ts(slot(k, s, 0, 16 * m + 16), T.srow[:, 0:16 * m + 16], own(m), None, ALU.is_lt, None,
-               srow[:2 if m <= FIRST else 3], ["ct%d_%d" % (k, s)])
-
-        def unbeaten(m):
-            k, s = where[m]
+        for k, tile in enumerate(TILES):
+            parts = ["ct%d_%d" % (k, s) for s in range(4)]
+            for s, m in enumerate(tile):
+                if m == "E":
+                    tt(slot(k, s, 0, C), T.own[:].indirect(offs(O_OX, 24)), T.srow[:], ALU.is_equal, ["own", "srow0", "srow1", "srow2", "o_ox"], [parts[s]],
+                       n=gathered(C))
+                    continue
+                n, srow = 16 * m, ["own"] + ["srow%d" % c for c in range(m // 8 + 1)]
+                if m in ON_SCALAR:
+                    e = ON_SCALAR.index(m)
+                    sg = C * e
+                    act(T.sg[:, sg:sg + n + 16], T.srow[:, 0:n + 16], ACT.Sign, srow, ["sg%d" % e], n=n + 16, bias=own(m), scale=-1.0)
+                    act(slot(k, s, 0, n), T.sg[:, sg:sg + n], ACT.Relu, ["sg%d" % e], [parts[s], "won%d" % e], n=n + 24, accum_out=col(T.rs2, e))
+                    act(slot(k, s, n, n + 16), T.sg[:, sg + n:sg + n + 16], ACT.Relu, ["sg%d" % e], ["cd%d" % m])
+                    act(col(T.rs, m), col(T.rs2, e), ACT.Identity, ["won%d" % e, "pf19", "pf%d" % (20 + e)], ["rs%d" % m], scale=pc(19), bias=pc(20 + e))
+                    parts.append("cd%d" % m)
+                else:
+                    ts(slot(k, s, 0, n + 16), T.srow[:, 0:n + 16], own(m), None, ALU.is_lt, None, srow, [parts[s]], n=n + 16)
+                    act(T.sj[:, 8 * m * (m - 1):8 * m * (m + 1)], slot(k, s, 0, n), ACT.Identity, [parts[s], "pf18", "pf19"], ["rs%d" % m],
+                        n=n + 24, scale=pc(19), bias=pc(18), accum_out=col(T.rs, m))
+            w, cq, cs = 128 if "E" in tile else 0, T.cq[:, TB[k]:TB[k] + TN[k]], T.cs[:, TB[k]:TB[k] + TN[k]]
+            quant(cq, cs, T.ct[:, 4 * TB[k]:4 * (TB[k] + TN[k])], parts, ["cq%d" % k], TN[k])
+            mm(6, TN[k], T.waq[:, w:w + 128], T.was[:, w:w + 128], cq, cs, ["cq%d" % k, "waq%d" % (w // 128)], k == 0, k == len(TILES) - 1)
+        for m in range(ROWS):
+            a, n = 32 * ROWS * m, 16 * ROWS
             if m:
-                act(T.sj[:, 8 * m * (m - 1):8 * m * (m + 1)], slot(k, s, 0, 16 * m), ACT.Identity, ["ct%d_%d" % (k, s), "pf18", "pf19"],
-                    ["rs%d" % m], scale=pc(19), bias=pc(18), accum_out=T.rs[:, m:m + 1])
-
-        where = {m: (k, s) for k, tl in enumerate(TILES) for s, m in enumerate(tl)}
-        compare(FIRST)
-        for n, m in enumerate(ON_SCALAR):
-            act(T.sg[:, C * n:C * n + 16 * m + 16], T.srow[:, 0:16 * m + 16], ACT.Sign, srow, ["sg%d" % n], bias=own(m), scale=-1.0)
-        for n, m in enumerate(ON_SCALAR):
-            k, s = where[m]
-            act(slot(k, s, 0, 16 * m), T.sg[:, C * n:C * n + 16 * m], ACT.Relu, ["sg%d" % n], ["ct%d_%d" % (k, s), "won%d" % n],
-                accum_out=T.rs2[:, n:n + 1])
-            act(slot(k, s, 16 * m, 16 * m + 16), T.sg[:, C * n + 16 * m:C * n + 16 * m + 16], ACT.Relu, ["sg%d" % n], ["cd%d" % m])
-        unbeaten(FIRST)
-        for n, m in enumerate(ON_SCALAR):
-            act(T.rs[:, m:m + 1], T.rs2[:, n:n + 1], ACT.Identity, ["won%d" % n, "pf19", "pf%d" % (20 + n)], ["rs%d" % m],
-                scale=pc(19), bias=pc(20 + n))
-        ke, se = where["E"]
-        for m in reversed(TILES[1]):
-            compare(m)
-            unbeaten(m)
-        tt(slot(ke, se, 0, C), T.own[:].indirect(offs(O_OX, 24)), T.srow[:], ALU.is_equal, srow + ["o_ox"], ["ct%d_%d" % (ke, se)])
-        squeeze(1)
-        last = len(TILES) - 1
-        for k in range(2, last + 1):
-            for n, m in enumerate(m for m in reversed(TILES[k]) if m != FIRST):
-                compare(m)
-                unbeaten(m)
-                if n == 0 and k > 2:
-                    squeeze(k - 1)
-                    if k == 3:
-                        squeeze(0)
-                        count(0)
-                        count(1)
-                    count(k - 1)
-        squeeze(last)
-        count(last)
-        tr(T.vrow[:], T.xv[:], ["xv"], ["vrow"])
-        scan(T.m1[:], T.horn[:], bank(7, C), 0.0, ALU.mult, ALU.add, ["horn0", "horn1"], ["m1"], ["b7"])
-        gap()
+                ts(T.rows[:, a:a + 16 * m], T.srow[:, 0:16 * m], own(m), None, ALU.is_ge, None, ["own", "srow0"], ["ge%d" % m])
+            ts(T.rows[:, a + 16 * m:a + n], T.srow[:, 16 * m:n], own(m), None, ALU.is_gt, None, ["own", "srow0"], ["gt%d" % m], n=n - 16 * m)
+            act(T.rows[:, a + n:a + 2 * n], T.rows[:, a:a + n], ACT.Copy, ["ge%d" % m, "gt%d" % m, "pf18"], ["rs%d" % m], n=n + 24,
+                scale=pc(18), accum_out=col(T.rs, m))
+        scan(T.m1[:], T.horn[:], bank(6, C), 0.0, ALU.mult, ALU.add, horn, ["m1"], ["b6"], n=C)
         tt(T.rk[:], T.m1[:, 15:C:16], T.rs[:], ALU.add, ["m1"] + ["rs%d" % m for m in range(24)], ["rk"])
-        gap()
         ts(T.rku[:], T.rk[:], pc(16), None, ALU.mult, None, ["rk", "pf16"], ["rku"])
-        gap()
-        cp(T.orow[:].indirect(T.rku[:]), T.vrow[:], ["rku", "vrow"], ["orow"])
-        gap()
+        cp(T.orow[:].indirect(T.rku[:]), T.vrow[:], ["rku"] + vrow, ["orow"], n=4 * C)
+        if t == R - 1:
+            o0, o1 = piece(T.ot, 0, C), piece(T.ot, 1, C)
+            act(o1, T.vrow[:], ACT.Identity, vrow, ["ot1"], n=C, scale=1.0 / (4 * C), bias=MAGIC)
+            act(T.olb[:, C:2 * C], o1, ACT.Identity, ["ot1"], ["ol1"], n=C, bias=-MAGIC)
+            act(o0, T.orow[:], ACT.Identity, ["orow"], ["ot0"], n=C, scale=1.0 / C, bias=(turn - (C - 1) / 2) / C)
+            ts(o0, o0, MAGIC, MAGIC, ALU.add, ALU.subtract, ["ot0"], ["ot0"], n=C)
+            act(o0, o0, ACT.Identity, ["ot0"], ["ot0"], n=C, scale=float(-C), bias=float(turn))
+            for n in range(4):
+                tt(piece(T.olb, n, L), piece(T.orow, n, L), piece(T.ot, n, L), ALU.add, ["orow", "ot0"], ["ol0%d" % n], n=H)
+            dma("y", T.ol[:], T.olb[0:128:16, :], ["ol0%d" % n for n in range(4)] + ["ol1"], (), "sl")
 
         bq, bs, mq, msc = [T["%s_%d" % (a, t)] for a in ("bq", "bs", "mq", "ms")]
-        H = 2 * L
-
-        start = (turn + H, turn)
-
-        def lift(n):
-            for a, col, k in runs(start[n], H):
-                scan(T.m2[:, H * n + a:H * n + a + k], T.horn[:, 0:k], T.orow[:, col:col + k], 0.0, ALU.mult, ALU.add,
-                     ["horn0", "orow"], ["m2%d_%d" % (n, a)])
-
-        def offsets(n):
-            ts(T.pick[:, 12 * n:12 * n + 12], T.m2[:, H * n + 15:H * n + H:16], pc(16), None, ALU.mult, None,
-               ["m2%d_%d" % (n, a) for a, col, k in runs(start[n], H)] + ["pf16"], ["pick%d" % n])
-
-        def gather(n, b):
-            src = T.win[:, C * b:32 * C].indirect(T.pick[:, 12 * n:12 * n + 12])
-            dst = T.bt[:, 4 * H * n + b:4 * H * (n + 1):4]
-            if b % 2:
-                act(dst, src, ACT.Copy, ["win", "pick%d" % n], ["bt%d_%d" % (n, b)])
-            else:
-                cp(dst, src, ["win", "pick%d" % n], ["bt%d_%d" % (n, b)])
-
-        def pack(n, q, s, name):
-            quant(q, s, T.bt[:, 4 * H * n:4 * H * (n + 1)], ["bt%d_%d" % (n, b) for b in range(4)], [name])
-
-        def deal(n, q, s, name, moves):
-            for src, dst, cast in ((q, mq, True), (s, msc, False)):
+        halves = ((turn + H, bq, bs, "b%d_" % t, ((2, 0), (3, L))), (turn, mq, msc, "mo%d" % t, ((1, L),)))
+        for n, (first, q, s, name, moves) in enumerate(halves):
+            for a, j, k in runs(first, H):
+                scan(T.m2[:, H * n + a:H * n + a + k], T.horn[:, 0:k], T.orow[:, j:j + k], 0.0, ALU.mult, ALU.add, horn + ["orow"], ["m2%d_%d" % (n, a)], n=k)
+            pick = T.pick[:, 12 * n:12 * n + 12]
+            ts(pick, T.m2[:, H * n + 15:H * n + H:16], pc(16), None, ALU.mult, None,
+               ["m2%d_%d" % (n, a) for a, j, k in runs(first, H)] + ["pf16"], ["pick%d" % n])
+            for b in range(4):
+                src, dst = T.win[:, C * b:32 * C].indirect(pick), T.bt[:, 4 * H * n + b:4 * H * (n + 1):4]
+                if b % 2:
+                    act(dst, src, ACT.Copy, ["win", "pick%d" % n], ["bt%d_%d" % (n, b)], n=gathered(H))
+                else:
+                    cp(dst, src, ["win", "pick%d" % n], ["bt%d_%d" % (n, b)], n=gathered(H))
+            quant(q[:, 0:H], s[:, 0:H], T.bt[:, 4 * H * n:4 * H * (n + 1)], ["bt%d_%d" % (n, b) for b in range(4)], [name], H)
+            for src, dst in ((q, mq), (s, msc)):
                 trs, sent = [], 0
-                for i, (d, col) in enumerate(moves):
-                    peer = T.cores[(rank + d) % n_ranks]
+                for i, (ahead, j) in enumerate(moves):
+                    peer = T.cores[(rank + ahead) % n_ranks]
                     rid, pid = topo.addr(peer)[:2]
                     eng = topo.engines(core, peer)
                     share = len(eng) // len(moves)
-                    a, b = src[:, col:col + L], dst[:, L * (n_ranks + 1 - d):L * (n_ranks + 2 - d)]
-                    if cast:
+                    a, b = src[:, j:j + L], dst[:, L * (n_ranks + 1 - ahead):L * (n_ranks + 2 - ahead)]
+                    if dst is mq:
                         a, b = a.bitcast(dt.uint8), b.bitcast(dt.uint8)
                     sent += share
                     trs.append(RemoteDMATransfer(dst_ids=[DstId(rid=rid, pnc=pid)], remote_sem=T.sem["arr%d_%d" % (n, t)], src=a, dst=b,
                                                  dma_engine_mask=sum(1 << e for e in eng[share * i:share * (i + 1)])))
-                op("g", lambda trs=trs: g.remote_dma_fused(trs, local_sem=T.sem["out%d" % t]), [name], (), sem="out%d" % t, inc=sent)
-                op("g", None, (), ["ma%d_%d" % (n, t)], sem="arr%d_%d" % (n, t), inc=sent)
-
-        for f in (lift, offsets):
-            f(0)
-            f(1)
-        for n, b in ((0, 0), (0, 1), (0, 2), (0, 3), (1, 0), (1, 1)):
-            gather(n, b)
-        pack(0, bq[:], bs[:], "b%d_" % t)
-        deal(0, bq, bs, "b%d_" % t, [(2, 0), (3, L)])
-        gather(1, 2)
-        gather(1, 3)
-        gap()
-        gap()
-        pack(1, mq[:, 0:H], msc[:, 0:H], "mo%d" % t)
-        deal(1, mq, msc, "mo%d" % t, [(1, L)])
+                call = "call%d_%d_%d" % (n, t, dst is mq)
+                op("g", lambda trs=trs: g.remote_dma_fused(trs, local_sem=T.sem["out%d" % t]), [name], [call], ["calls"], CALL / CYCLE, "out%d" % t, sent)
+                op("far", None, [call], ["ma%d_%d" % (n, t)], (), 64, "arr%d_%d" % (n, t), sent, TRAVEL)
 
         xs = {}
 
-        def new_state(first, n, keep, to, name):
-            for w, b in PRODUCTS:
+        def new_state(first, n, keep, to, banks, name):
+            for (w, b), k in zip(PRODUCTS, banks):
                 lq, ls, r = (T.wq, T.wsc, "w") if w else (T.enq, T.ens, "enq%d" % b)
-                k, z, zn = 2 * b + 1 - w, C * b + to, "z%d_%d" % (b, to)
+                z, zn = C * b + to, "z%d_%d" % (b, to)
                 mm(k, n, piece(lq, b), piece(ls, b), mq[:, first:first + n], msc[:, first:first + n], name + [r])
                 if w:
-                    act(T.z[:, z:z + keep], bank(k, keep), ACT.Relu, (), [zn], ["b%d" % k], scale=0.03125)
+                    act(T.z[:, z:z + keep], bank(k, keep), ACT.Relu, (), [zn], ["b%d" % k], n=keep, scale=0.03125)
                     continue
-                for a, col, m in runs(to + (turn if t == R - 1 else 0), keep):
-                    xs.setdefault(to, []).append("xs%d_%d" % (b, col))
-                    tt(T.xs[:, 4 * col + b:4 * (col + m):4], bank(k, a + m, a), T.z[:, z + a:z + a + m], ALU.add, [zn], [xs[to][-1]], ["b%d" % k])
-                if b != 2:
-                    gap()
+                for a, j, m in runs(to + (turn if t == R - 1 else 0), keep):
+                    xs.setdefault(to, []).append("xs%d_%d" % (b, j))
+                    tt(T.xs[:, 4 * j + b:4 * (j + m):4], bank(k, a + m, a), T.z[:, z + a:z + a + m], ALU.add, [zn], [xs[to][-1]], ["b%d" % k], n=m)
 
-        if t == R - 1:
-            o0, o1, o2 = [piece(T.ot, n, C) for n in range(3)]
-            spare.extend([
-                lambda: ts(o0, T.orow[:], 1.0 / (4 * C), MAGIC, ALU.mult, ALU.add, ["orow"], ["ot0"]),
-                lambda: ts(o1, T.vrow[:], 1.0 / (4 * C), MAGIC, ALU.mult, ALU.add, ["vrow"], ["ot1"]),
-                lambda: ts(o0, o0, MAGIC, float(-4 * C), ALU.subtract, ALU.mult, ["ot0"], ["ot0"]),
-                lambda: ts(T.olb[:, C:2 * C], o1, MAGIC, None, ALU.subtract, None, ["ot1"], ["ol1"])]
-                + [lambda n=n: tt(piece(T.ot, n, H), piece(T.orow, n, H), piece(T.ot, n, H), ALU.add, ["orow", "ot0"], ["ot0"]) for n in range(2)]
-                + [lambda: ts(o2, o0, float(C - turn), float(-C), ALU.is_ge, ALU.mult, ["ot0"], ["ot2"]),
-                   lambda: ts(o1, o0, float(turn), None, ALU.add, None, ["ot0", "ol1"], ["ot1"])]
-                + [lambda n=n: tt(piece(T.olb, n, H), piece(T.ot, 2 + n, H), piece(T.ot, 4 + n, H), ALU.add, ["ot1", "ot2"], ["ol0%d" % n]) for n in range(2)]
-                + [lambda: dma("y", T.ol[:], T.olb[0:128:16, :], ["ol00", "ol01", "ol1"], (), "sl")])
-            gap()
-            gap()
-        new_state(0, 128, L, 0, ["mo%d" % t])
         mid = 256
-        new_state(H, mid - L, mid - L, L, ["ma0_%d" % t])
-        if t < R - 1:
-            for c in range(2):
+        late = {(j + e) // 128 for a, j, k in runs(mid + (turn if t == R - 1 else 0), C - mid) for e in (0, k - 1)}
+        new_state(0, 128, L, 0, EARLY_BANKS, ["mo%d" % t])
+        new_state(H, mid - L, mid - L, L, EARLY_BANKS, ["ma0_%d" % t])
+        for c in range(3):
+            if c not in late:
                 quant_piece(t + 1, c, T.xs, xs[0] + xs[L])
-        new_state(L + mid, C - mid, C - mid, mid, ["ma0_%d" % t, "ma1_%d" % t])
-        weave([None] * len(spare), spare)
-        for c in range(3) if t == R - 1 else [2]:
+        new_state(L + mid, C - mid, C - mid, mid, LAST_BANKS, ["ma0_%d" % t, "ma1_%d" % t])
+        for c in sorted(late):
             quant_piece(t + 1, c, T.xs, xs[0] + xs[L] + xs[mid])
 
     for c in range(3):
@@ -617,12 +540,13 @@ def rank_program(g, core, T, topo):
 
     tq, tsc, tn = T["tq_%d" % R], T["ts_%d" % R], ["t%d_%d" % (R, c) for c in range(3)]
     for c in range(3):
-        mm(4 + c, 128, T.vq[:], T.vs[:], piece(tq, c), piece(tsc, c), [tn[c], "vq"])
-    for c in range(2):
-        act(piece(T.yo, c), bank(4 + c, 128), ACT.Copy, (), ["yo%d" % c], ["b%d" % (4 + c)])
-    cp(piece(T.yo, 2), bank(6, 128), (), ["yo2"], ["b6"])
+        mm(2 * c, 128, T.vq[:], T.vs[:], piece(tq, c), piece(tsc, c), [tn[c], "vq"])
+        if c % 2:
+            act(piece(T.yo, c), bank(2 * c, 128), ACT.Copy, (), ["yo%d" % c], ["b%d" % (2 * c)], n=128)
+        else:
+            cp(piece(T.yo, c), bank(2 * c, 128), (), ["yo%d" % c], ["b%d" % (2 * c)], n=128)
     dma("y", T.oc[:], tq[:].bitcast(dt.uint8), tn, (), "so")
     dma("s", T.y[:], T.yo[:], ["yo0", "yo1", "yo2"], (), "sy")
     for k in range(4):
         dma("y" if k < 3 else "s", T.osc[4 * k:4 * k + 4, :], tsc[32 * k:32 * k + 4, :], tn, (), "so")
-    emit()
+    emit(ops, g, T)

from concourse.bass import DstId, RemoteDMATransfer
from concourse.mybir import dt, AluOpType, AxisListType, ActivationFunctionType

ALU = AluOpType
ACT = ActivationFunctionType
C, L, R = 384, 96, 3
H = 2 * L
HIGH = float(2 ** 72)
DROP = float(2 ** 74)
FREE = float(2 ** 76)
SINK = float(2 ** 81)
RISE = float(2 ** 86)
LIFT = float(2 ** 22)
MAGIC = float(3 * 2 ** 22)
F32, BF, I32, U16, X4, U8 = "float32", "bfloat16", "int32", "uint16", "float8_e4m3fn_x4", "uint8"
SW, KW = 80, 144
PART = 32 * 4 * C
LOW = 7.25
CAPS = 3

PRODUCTS = [(1, 0), (1, 1), (0, 0), (1, 2), (0, 1), (1, 3), (0, 2), (0, 3)]
EARLY_BANKS, LAST_BANKS = [0, 2, 1, 4, 3, 6, 5, 7], [1, 3, 5, 7, 6, 1, 3, 5]
MOVES_ON_SCALAR = 8
ROW_ON_VECTOR = [0]

TILES = [[21, 22, 23, "E"], [17, 18, 19, 20], [13, 14, 15, 16], [9, 10, 11, 12], [5, 6, 7, 8]]
ROWS = 5
ON_SCALAR = [23, 22, 21]
TN = [16 * (max(m for m in t if m != "E") + 1) for t in TILES]
TB = [sum(TN[:k]) for k in range(len(TN))]
CW = sum(TN)
O_U, O_XS, O_XV, O_OWN, O_OX, O_I = 0, 8, 32, 56, 58, 82
CYCLE, WAKE, COPY, FILL, CALL, TRAVEL = 0.83, 200, 2200, 11000, 800, 1200

SCRATCH = {"ps": ("psum", [128, 4096], F32), "sks": ("sbuf", [128, 3, KW], F32)}
for _d, _l in (
    (BF, dict(xin=4 * C, uin=512, vin=512, xs=4 * C, en=516, ep=516, wall=512, q128=128, g512=512, t128=256, htab=64, keep=KW,
              h16=48, horn=C, stp=21 * SW, hs=24 * SW, ohg=21 * 8, one=24 * 8, low=64, cap=CAPS * C, rows=16 * ROWS * ROWS * 2,
              ct=4 * CW, sg=3 * C, sj=8 * 24 * 23, dp=4 * C, win=32 * C, bt=4 * C)),
    (F32, dict(z=4 * C, pf=24, tq1=8, wh=66, lik=3 * C, run=24 * 64, sk=3 * KW, junk=48, v7=6,
               yy=96, zz=64, own=32, xe=C, xv=C, srow=C, vrow=C, rs=24, rs2=4, rk=24, m1=C, m2=C, orow=C, olb=2 * C,
               ot=2 * C, yo=C)),
    (X4, dict(uq=128, upq=128, vq=128, wq=512, enq=512, epq=512, waq=256, cq=CW)),
    (U8, dict(us=128, ups=128, vs=128, wsc=512, ens=512, eps=512, was=256, cs=CW)),
    (I32, dict(pi=8, it=128)),
    (U16, dict(off=108, rku=24, pick=24)),
):
    for _n, _w in _l.items():
        SCRATCH[_n] = ("sbuf", [128, _w], _d)
for _t in range(R + 1):
    for _n, _w in (("t", C), ("b", H), ("m", C + L))[:1 if _t == R else 3]:
        SCRATCH["%sq_%d" % (_n, _t)] = ("sbuf", [128, _w], X4)
        SCRATCH["%ss_%d" % (_n, _t)] = ("sbuf", [128, _w], U8)

SEMAPHORES = ["ev", "es", "et", "eg", "lx0", "lx1", "lu", "lv", "lw", "so", "sy", "sl"]
for _t in range(R):
    SEMAPHORES += ["rep%d" % _t, "arr0_%d" % _t, "arr1_%d" % _t, "out%d" % _t]


def hazards(ops):
    wrote, read, held = {}, {}, {}
    for k, o in enumerate(ops):
        d, after = set(), set()
        for a in o["r"]:
            d.update(wrote.get(a, []))
        for a in o["w"]:
            d.update(read.get(a, []))
            d.update(q for q in wrote.get(a, []) if not (o["sem"] and ops[q]["sem"] == o["sem"]))
        for a in o["x"]:
            for q in held.get(a, []):
                (d if ops[q]["e"] != o["e"] else after).add(q)
        for a in o["r"]:
            read.setdefault(a, []).append(k)
        for a in o["w"]:
            same = [q for q in wrote.get(a, []) if o["sem"] and ops[q]["sem"] == o["sem"]]
            wrote[a], read[a] = same + [k], []
        for a in o["x"]:
            held[a] = [k]
        o["d"], o["after"] = d - {k}, after - {k}


def issue_order(ops):
    n = len(ops)
    users = [[] for _ in ops]
    for k, o in enumerate(ops):
        for q in o["d"] | o["after"]:
            users[q].append(k)
    chain = [0.0] * n
    for k in reversed(range(n)):
        chain[k] = ops[k]["busy"] + ops[k]["late"] + max([WAKE * (k in ops[u]["d"]) + chain[u] for u in users[k]] + [0])
    missing = [len(o["d"] | o["after"]) for o in ops]
    ready, free, due, order = {}, {}, [0.0] * n, []
    for k in range(n):
        if not missing[k]:
            ready.setdefault(ops[k]["e"], []).append(k)
    while len(order) < n:
        offers = []
        for e, calls in ready.items():
            if not calls:
                continue
            now = max(free.get(e, 0.0), min(due[k] for k in calls))
            fits = [k for k in calls if due[k] <= now and not any(
                now < due[q] < now + ops[k]["busy"] - WAKE / 8 and chain[q] > chain[k] + due[q] - now for q in calls)]
            k = max(fits or calls, key=lambda q: (chain[q] - (0 if fits else due[q]), -q))
            offers.append((max(now, due[k]), k))
        start, k = min(offers)
        o = ops[k]
        ready[o["e"]].remove(k)
        order.append(k)
        free[o["e"]] = start + o["busy"]
        for u in users[k]:
            due[u] = max(due[u], start + o["busy"] + (o["late"] + WAKE if k in ops[u]["d"] else 0))
            missing[u] -= 1
            if not missing[u]:
                ready.setdefault(ops[u]["e"], []).append(u)
    return order


def emit(ops, g, T):
    hazards(ops)
    order = issue_order(ops)
    queue = {"v": g.vector, "s": g.scalar, "t": g.tensor, "g": g, "y": g.sync}
    place = {k: n for n, k in enumerate(order)}
    groups, total, waited = {}, {}, {}
    for k, o in enumerate(ops):
        if o["sem"]:
            groups.setdefault(o["sem"], []).append(k)
            total[o["sem"]] = total.get(o["sem"], 0) + o["inc"]
    known = {e: {} for e in queue}
    for k in order:
        o = ops[k]
        o["waits"], o["knew"] = [], {}
        if o["fn"] is None:
            continue
        kn = known[o["e"]]
        for q in sorted(o["d"], key=lambda a: -place[a]):
            p = ops[q]
            key, pos = (p["sem"], len(ops)) if p["sem"] else (p["e"], place[q])
            if kn.get(key, -1) >= pos:
                continue
            o["waits"].append(q)
            p["sig"] = True
            kn[key] = pos
            for z in groups[p["sem"]] if p["sem"] else [q]:
                for a, b in ops[z].get("knew", {}).items():
                    kn[a] = max(kn.get(a, -1), b)
        o["knew"] = dict(kn)
    for k in order:
        o = ops[k]
        if not o["sem"] and o.get("sig"):
            name = "e" + o["e"]
            total[name] = total.get(name, 0) + 1
            o["val"] = total[name]
    for k in order:
        o = ops[k]
        if o["fn"] is None:
            continue
        for q in o["waits"]:
            p = ops[q]
            name, val = (p["sem"], total[p["sem"]]) if p["sem"] else ("e" + p["e"], p["val"])
            queue[o["e"]].wait_ge(T.sem[name], val)
            waited[name] = max(waited.get(name, 0), val)
        ins = o["fn"]()
        if o["sem"] and not o["sem"].startswith("out"):
            ins.then_inc(T.sem[o["sem"]], 16)
        elif o.get("sig") and not o["sem"]:
            ins.then_inc(T.sem["e" + o["e"]], 1)
    for name, val in total.items():
        if waited.get(name, 0) < val:
            g.wait_ge(T.sem[name], val)


def rank_program(g, core, T, topo):
    rank = T.rank_of(core)
    if rank is None:
        return
    n_ranks = len(T.cores)
    turn = L * rank
    back = (24 - turn // 16) % 24
    ops = []
    V, S = g.vector, g.scalar

    def op(eng, fn, r=(), w=(), x=(), n=64, sem=None, inc=16, late=0):
        ops.append({"e": eng, "fn": fn, "r": list(r), "w": list(w), "x": list(x), "sem": sem, "inc": inc,
                    "busy": CYCLE * max(n, 64), "late": late})

    def ts(out, in0, s1, s2, o0, o1, r, w, x=(), n=64):
        if o1 is None:
            op("v", lambda: V.tensor_scalar(out, in0, s1, None, o0), r, w, x, n)
        else:
            op("v", lambda: V.tensor_scalar(out, in0, s1, s2, o0, o1), r, w, x, n)

    def tt(out, a, b, o, r, w, x=(), n=64):
        op("v", lambda: V.tensor_tensor(out, a, b, o), r, w, x, n)

    def cp(out, a, r, w, x=(), n=64):
        op("v", lambda: V.tensor_copy(out, a), r, w, x, n)

    def ms(ap, c, w, n=64):
        op("v", lambda: V.memset(ap, c), (), w, (), n)

    def scan(out, d0, d1, init, o0, o1, r, w, x=(), n=64):
        op("v", lambda: V.tensor_tensor_scan(out, d0, d1, init, o0, o1), r, w, x, n)

    def tr(out, a, r, w, n=64):
        op("v", lambda: V.transpose(out, a), r, w, (), n)

    def quant(q, s, a, r, w, n=128):
        op("v", lambda: V.quantize_mx(q, s, a), r, w, (), n + 16)

    def act(out, a, f, r, w, x=(), n=64, **kw):
        op("s", lambda: S.activation(out, a, f, **kw), r, w, x, n)

    def mm(bank, n, lq, ls, rq, rs_, r, start=True, stop=True):
        op("t", lambda: g.tensor.matmul_mx(T.ps[:, 512 * bank:512 * bank + n], lq, ls, rq, rs_, start, stop), r, (), ["b%d" % bank],
           (n + 16) * 5 // 4)

    def iota(out, pat, base, ch, w, small=True):
        n = 160 + 2 * pat[0][1] * (pat[1][1] if len(pat) > 1 else 1) * (pat[2][1] if len(pat) > 2 else 1)
        if small:
            op("g", lambda: g.iota(out, pat, base, ch, allow_small_or_imprecise_dtypes=True), (), w, (), n)
        else:
            op("g", lambda: g.iota(out, pat, base, ch), (), w, (), n)

    def dma(eng, out, a, r, w, sem, late=COPY):
        q = {"y": g.sync, "s": g.scalar}[eng]
        op(eng, lambda: q.dma_start(out, a), r, w, sem=sem, late=late)

    def gathered(n):
        return 70 + n * 3 // 2

    def offs(a, k):
        return T.off[:, a:a + k]

    def bank(b, n, a=0):
        return T.ps[:, 512 * b + a:512 * b + n]

    def piece(buf, c, w=128):
        return buf[:, w * c:w * c + w]

    def col(buf, k):
        return buf[:, k:k + 1]

    def pc(k):
        return col(T.pf, k)

    def runs(first, n):
        first %= C
        cut = min(n, C - first)
        return [(0, first, cut)] + ([(cut, 0, n - cut)] if cut < n else [])

    dma("s", T.uin[:], T.u[:], (), ["uin"], "lu")
    for n, (first, k) in enumerate(((0, 256), (256, 128))):
        for a, j, m in runs(turn + first, k):
            dma("y", T.xin[:, 4 * (first + a):4 * (first + a + m)], T.x[:, 4 * j:4 * (j + m)], (), ["xin%d" % n], "lx%d" % n, COPY + 600 * (n + 1))
    dma("y", T.wq[:].bitcast(dt.uint8), T.wc[:], ["xin1"], ["w"], "lw")
    dma("y", T.wsc[:], T.ws[:], ["xin1"], ["w"], "lw")
    dma("y", T.vin[:], T.v[:], ["xin1"], ["vin"], "lv")

    P_I, P_G, P_I8, P_A, P_F, P_E = range(1, 7)
    every = [(k, c) for k in range(7) for c in range(3)]
    iota(T.pi[:, 0:1], [[0, 1]], 0, 1, ["p"], False)
    iota(T.it[:, 0:8], [[0, 2], [32, 4]], 0, 0, ["it0"], False)
    iota(T.q128[:], [[1, 128]], 0, 0, ["q128"])
    iota(T.htab[:], [[0, 8], [-1, 8]], 136, 0, ["htab"])
    iota(T.htab[:, 0:64:8], [[0, 8]], 128, 0, ["htab"])
    iota(T.stp[:, 7:21 * SW:SW], [[0, 21]], 0, 0, ["stp_a"])
    for e in (72, 73):
        iota(T.stp[:, e:21 * SW:SW], [[0, 21]], 1, 0, ["stp_%d" % e])
    for h in range(8):
        rest = 16 - LOW + (8 - h if h else 0) - (7 if h else 8) / 32
        iota(T.sk[:, 18 * h + 17:3 * KW:KW], [[128, 3]], -int(PART * rest), 1, ["skj%d" % h])
    iota(T.it[:, 8:56], [[0, 2], [1, 24]], 0, 0, ["it7"], False)
    iota(T.it[:, 104:106], [[4, 2]], 0, 0, ["it6"], False)
    for q in range(2):
        iota(T.it[:, 56 + 24 * q:80 + 24 * q], [[4, 3], [12, 4], [2, 2]], 0, 0, ["it4%d" % q], False)
    iota(T.g512[:], [[1, 8], [0, 64]], 0, 0, ["g512"])
    iota(T.keep[:], [[0, KW]], 1, 0, ["keep"])
    iota(T.keep[:, 0:KW:9], [[0, 16]], 0, 0, ["keep"])
    iota(T.keep[:, 17:KW:18], [[0, 8]], PART, 0, ["keep"])
    iota(T.yy[:, 48:64], [[0, 16]], 0, 0, ["ypad"])
    iota(T.sk[:, 8:3 * KW:18], [[0, 24]], 0, 0, ["skz"])
    iota(T.hs[:, 21 * SW:24 * SW], [[0, 3 * SW]], 0, 0, ["hs_last"])
    iota(T.en[:], [[0, 516]], 0, 0, ["en"])
    for k, t in enumerate(TILES):
        lo = 16 * (min(m for m in t if m != "E") + 1)
        iota(T.ct[:, 4 * (TB[k] + lo):4 * (TB[k] + TN[k])], [[0, 4 * (TN[k] - lo)]], 0, 0, ["ct%d_%d" % (k, s) for s in range(4)])

    ms(T.ep[:], 0.0, ["ep"], 258)
    ms(T.low[:], -HIGH, ["low"])
    ms(T.wh[:, 0:64], 1.0, ["wh"])
    ms(T.wh[:, 0:64:8], -7 - 1 / 32, ["wh"])
    ms(T.wh[:, 64:65], -LOW, ["wh64"])
    ms(T.wh[:, 65:66], 128 + LOW, ["wh65"])
    ms(T.lik[:, 0:C:2], HIGH, ["pads"], 192)
    for k in range(CAPS):
        ms(T.cap[:, C * k:C * k + C:2], FREE, ["cap%d_%d%s" % (k, c, a) for c in range(3) for a in ("", "p")], 96)
    for k, sh, mask in ((P_I, 0, 15), (P_G, 4, 7), (P_I8, 3, 1), (P_A, 1, 3), (P_F, 0, 1), (P_E, 4, 1)):
        ts(col(T.pi, k), T.pi[:, 0:1], sh, mask, ALU.logical_shift_right, ALU.bitwise_and, ["p"], ["pi%d" % k])
    cp(T.pf[:, 0:7], T.pi[:, 0:7], ["p"] + ["pi%d" % k for k in range(1, 7)], ["pf"])
    ts(pc(8), pc(P_I8), 8.0, pc(P_I), ALU.mult, ALU.add, ["pf"], ["pf8"])
    ts(pc(10), pc(P_I), 8.0, pc(P_G), ALU.mult, ALU.add, ["pf"], ["pf10"])
    ts(offs(O_U, 8), T.it[:, 0:8], pc(8), None, ALU.add, None, ["pf8", "it0"], ["o_u"])
    quant(T.uq[:], T.us[:], T.uin[:], ["uin"], ["uq"])
    op("v", lambda: V.tensor_copy(T.upq[:].bitcast(dt.uint32), T.uq[:].bitcast(dt.uint32).indirect(offs(O_U, 8))), ["uq", "o_u"], ["upq"], (), gathered(128))
    op("s", lambda: S.activation(T.ups[:], T.us[:].indirect(offs(O_U, 8)), ACT.Copy), ["uq", "o_u"], ["ups"], (), gathered(128))
    for e, q, s, at, name in ((T.ep, T.epq, T.eps, 10, "ep"), (T.en, T.enq, T.ens, 0, "en")):
        ts(e[:, 3:515:4], T.q128[:], pc(at), None, ALU.is_equal, None, ["pf", "pf10", "q128", name], [name])
        for b in range(4):
            quant(piece(q, b), piece(s, b), e[:, 3 - b:515 - b], [name], ["%sq%d" % (name, b)])
    quant(T.vq[:], T.vs[:], T.vin[:], ["vin"], ["vq"])
    act(pc(17), pc(P_I), ACT.Identity, ["pf"], ["pf17"], bias=1.0)
    act(pc(14), pc(P_G), ACT.Identity, ["pf"], ["pf14"], scale=16.0, bias=15.0)
    act(pc(11), pc(P_A), ACT.Identity, ["pf"], ["pf11"], scale=3.0, bias=pc(P_I8))
    act(pc(12), pc(11), ACT.Identity, ["pf", "pf11"], ["pf12"], scale=2.0, bias=pc(P_E))
    ts(pc(15), pc(P_I), 15.0, LIFT, ALU.not_equal, ALU.mult, ["pf"], ["pf15"])
    ts(pc(18), pc(15), 1.0, None, ALU.max, None, ["pf15"], ["pf18"])
    ts(pc(16), pc(P_I), 15.0, 1.0 / LIFT, ALU.is_equal, ALU.max, ["pf"], ["pf16"])
    ts(pc(13), pc(P_F), pc(P_E), None, ALU.is_equal, None, ["pf"], ["pf13"])
    act(pc(19), pc(18), ACT.Copy, ["pf18"], ["pf19"], scale=-1.0)
    for n, m in enumerate(ON_SCALAR):
        act(pc(20 + n), pc(18), ACT.Copy, ["pf18"], ["pf%d" % (20 + n)], scale=16.0 * m)
    ts(T.h16[:, 0:16], T.q128[:, 0:16], pc(P_I), None, ALU.not_equal, None, ["pf", "q128"], ["h16a"])
    ts(T.h16[:, 16:32], T.q128[:, 0:16], pc(17), LIFT, ALU.is_equal, ALU.mult, ["pf17", "q128"], ["h16b"])
    tt(T.h16[:, 32:48], T.h16[:, 0:16], T.h16[:, 16:32], ALU.max, ["h16a", "h16b"], ["h16c"])
    ts(offs(O_I, 24), T.it[:, 8:32], 0.0, pc(P_I), ALU.mult, ALU.add, ["it7", "pf"], ["o_i"])
    for q in range(4):
        act(piece(T.horn, q, L), T.h16[:, 32:48].indirect(offs(O_I, 6)), ACT.Copy, ["h16c", "o_i"], ["horn%d" % q], n=gathered(L))
    horn = ["horn%d" % q for q in range(4)]
    ts(T.t128[:, 0:128], T.q128[:], pc(0), None, ALU.is_gt, None, ["pf", "q128"], ["t128a"])
    ts(T.t128[:, 128:256], T.q128[:], pc(14), None, ALU.is_le, None, ["pf14", "q128"], ["t128b"])
    for q in range(2):
        ts(piece(T.wall, q, 256), piece(T.g512, q, 256), pc(P_G), None, ALU.is_equal, None, ["pf", "g512"], ["wall%d" % q], n=128)
    quant(T.waq[:, 0:128], T.was[:, 0:128], T.wall[:], ["wall0", "wall1"], ["waq0"])
    for q in range(2):
        tt(T.wall[:, 256 * q + 3:256 * q + 256:4], piece(T.t128, q, 64), piece(T.t128, 2 + q, 64), ALU.mult, ["t128a", "t128b"], ["wall%d" % q], n=128)
    quant(T.waq[:, 128:256], T.was[:, 128:256], T.wall[:], ["wall0", "wall1"], ["waq1"])
    ts(T.tq1[:, 0:2], T.it[:, 104:106], pc(12), None, ALU.add, None, ["pf12", "it6"], ["tq1a"])
    ts(T.tq1[:, 2:4], T.tq1[:, 0:2], 64.0, pc(13), ALU.subtract, ALU.mult, ["tq1a", "pf13"], ["tq1b"])
    tt(T.tq1[:, 4:6], T.tq1[:, 0:2], T.tq1[:, 2:4], ALU.add, ["tq1a", "tq1b"], ["tq1c"])
    ts(offs(O_OWN, 2), T.tq1[:, 4:6], 64.0, None, ALU.add, None, ["tq1c"], ["o_own"])
    cp(offs(O_XS, 24), T.it[:, 56 + back:80 + back], ["it40", "it41"], ["o_xs"])
    ts(offs(O_XV, 24), T.it[:, 56 + back:80 + back], 1.0, None, ALU.add, None, ["it40", "it41"], ["o_xv"])
    cp(offs(O_OX, 24), T.it[:, 8 + back:32 + back], ["it7"], ["o_ox"])

    def quant_piece(t, c, tile, r):
        tq, tsc, name = piece(T["tq_%d" % t], c), piece(T["ts_%d" % t], c), "t%d_%d" % (t, c)
        quant(tq, tsc, piece(tile, c, 512), r, [name])
        if t < R:
            mm(2 * c, 128, tq, tsc, T.upq[:], T.ups[:], [name, "upq", "ups"])

    def match(c):
        def likings(k):
            n = 0 if k == 0 else 1 + k % 2
            return piece(T.lik, 3 * n + c), T.lik[:, C * n + 128 * c + 1:C * n + 128 * c + 128:2], "lik%d_%d" % (n, c)

        def record(k, top, count, r):
            a, one = KW * c + k, piece(T.one, 3 * k + c, 8)
            act(T.sk[:, a + 9:KW * c + KW:18], one, ACT.Relu, r + ["one%d_%d" % (k, c)], ["sk1_%d_%d" % (k, c)], scale=16.0, bias=count)
            if top is not None:
                act(T.sk[:, a:KW * c + KW:18], one, ACT.Copy, r + ["one%d_%d" % (k, c)], ["sk0_%d_%d" % (k, c)], scale=top)

        for k in range(7):
            n, tag = 3 * k + c, "%d_%d" % (k, c)
            run, top, s, cap = piece(T.run, n, 64), col(T.run, 64 * n + 63), SW * n, C * (k % CAPS) + 128 * c
            caps = "cap%d_%d" % (k % CAPS, c)
            whole, entries, lik = likings(k)
            if k:
                scan(run, T.low[:], entries, -HIGH, ALU.max, ALU.max, ["low", lik], ["run" + tag])
            else:
                scan(run, T.low[:], bank(2 * c, 64), -HIGH, ALU.max, ALU.max, ["low"], ["run" + tag], ["b%d" % (2 * c)])
                act(entries, bank(2 * c, 64), ACT.Copy, ["pads"], [lik], ["b%d" % (2 * c)])
            ts(T.stp[:, s + 8:s + 72], run, top, None, ALU.is_ge, None, ["run" + tag], ["stp" + tag])
            tt(piece(T.ohg, n, 8), T.stp[:, s + 15:s + 72:8], T.stp[:, s + 7:s + 64:8], ALU.subtract, ["stp" + tag, "stp_a"], ["ohg" + tag])
            act(T.cap[:, cap:cap + 128:16], piece(T.ohg, n, 8), ACT.Identity, ["ohg" + tag], [caps + "p"], scale=-(RISE + SINK), bias=RISE)
            scan(T.hs[:, s:s + 66], T.wh[:], T.stp[:, s + 8:s + 74], 0.0, ALU.add, ALU.mult,
                 ["stp" + tag, "stp_72", "stp_73", "wh", "wh64", "wh65"], ["hs" + tag])
            ts(T.cap[:, cap + 1:cap + 128:2], T.htab[:], col(T.hs, s + 65), -DROP, ALU.is_equal, ALU.mult, ["hs" + tag, "htab"], [caps])
            act(piece(T.one, n, 8), T.cap[:, cap + 1:cap + 16:2], ACT.Copy, [caps], ["one" + tag], scale=-1.0 / DROP)
            record(k, top, col(T.hs, s + 64), ["run" + tag, "hs" + tag])
            scan(likings(k + 1)[0], T.cap[:, cap:cap + 128], whole, 0.0, ALU.add, ALU.min, [caps, caps + "p", lik], [likings(k + 1)[2]], n=128)
        counts, top = ["hs%d_%d" % (k, c) for k in range(7)] + ["hs_last"], col(T.run, 64 * (21 + c) + 63)
        for w, total in enumerate((28 - 29 / 32 - 8 * LOW, 8 * 128 + 28)):
            act(piece(T.junk, 2 * c + w, 8), T.hs[:, SW * c + 64 + w:24 * SW:3 * SW], ACT.Identity, counts, ["v7_%d_%d" % (w, c)],
                scale=-1.0, bias=total / 8, accum_out=col(T.v7, 2 * c + w))
        ts(piece(T.one, 21 + c, 8), T.htab[:, 0:8], col(T.v7, 2 * c + 1), None, ALU.is_equal, None, ["v7_1_%d" % c, "htab"], ["one7_%d" % c])
        record(7, None, col(T.v7, 2 * c), ["v7_0_%d" % c])
        op("v", lambda: V.tensor_reduce(top, likings(7)[1], AxisListType.X, ALU.max), [likings(7)[2]], ["run7_%d" % c])
        ts(T.sk[:, KW * c + 7:KW * c + KW:18], piece(T.one, 21 + c, 8), top, None, ALU.mult, None, ["one7_%d" % c, "run7_%d" % c], ["sk0_7_%d" % c])
        scan(T.sks[:, c, :], T.keep[:], piece(T.sk, c, KW), 0.0, ALU.mult, ALU.add,
             ["keep", "skz"] + ["skj%d" % h for h in range(8)] + ["sk%d_%d_%d" % (w, k, c) for w in range(2) for k in range(8)], ["sks%d" % c], n=KW)

    def one_round(t):
        tq, tsc, tn = T["tq_%d" % t], T["ts_%d" % t], ["t%d_%d" % (t, c) for c in range(3)]
        for c in range(3):
            match(c)
        for b in range(4):
            mm(2 * b + 1, C, piece(T.epq, b), piece(T.eps, b), tq[:], tsc[:], tn + ["epq%d" % b])
            for c in range(3):
                act(piece(T.dp, 3 * b + c), bank(2 * b + 1, 128 * c + 128, 128 * c), ACT.Copy, (), ["dp%d_%d" % (b, c)], ["b%d" % (2 * b + 1)], n=128)
        for h in range(8):
            dma("y", T.win[16 * h:16 * h + 16, :], T.dp[:], ["dp%d_%d" % (b, c) for b in range(4) for c in range(3)], ["win"], "rep%d" % t, FILL)

        yy = ["ypad"]
        for n in range(16):
            b, a = divmod(n, 4)
            src, dst = T.sks[32 * a:32 * a + 32, :, 36 * b + 8:36 * b + 36:9], T.yy[32 * b:32 * b + 32, 12 * a:12 * a + 12]
            yy.append("yy%d_%d" % (a, b))
            if n >= MOVES_ON_SCALAR:
                cp(dst, src, ["sks0", "sks1", "sks2"], [yy[-1]])
            else:
                act(dst, src, ACT.Copy, ["sks0", "sks1", "sks2"], [yy[-1]])
        tr(T.zz[:, 0:32], T.yy[:, 0:64:2], yy, ["zz0"])
        tr(T.zz[:, 32:64], T.yy[:, 0:64:2], yy, ["zz1"])
        tr(T.yy[:, 64:96], T.zz[:, 16:48], ["zz0", "zz1"], ["ysw"])
        cp(T.own[:], T.yy[:].indirect(offs(O_OWN, 2)), yy + ["ysw", "o_own"], ["own"], n=gathered(32))
        for c in range(3):
            if c in ROW_ON_VECTOR:
                cp(piece(T.xe, c), T.yy[:, 0:64].indirect(offs(O_XS + 8 * c, 8)), yy + ["o_xs"], ["xe%d" % c], n=gathered(128))
            else:
                act(piece(T.xe, c), T.yy[:, 0:64].indirect(offs(O_XS + 8 * c, 8)), ACT.Copy, yy + ["o_xs"], ["xe%d" % c], n=gathered(128))
            tr(piece(T.srow, c), piece(T.xe, c), ["xe%d" % c], ["srow%d" % c], 128)
        act(T.xv[:], T.yy[:, 0:64].indirect(offs(O_XV, 24)), ACT.Copy, yy + ["o_xv"], ["xv"], n=gathered(C))
        vrow = ["vrow%d" % n for n in range(4)]
        for n in range(4):
            tr(piece(T.vrow, n, L), piece(T.xv, n, L), ["xv"], [vrow[n]], L)

        def own(m):
            return col(T.own, (m + back) % 24)

        def slot(k, s, a, b):
            return T.ct[:, 4 * (TB[k] + a) + s:4 * (TB[k] + b):4]

        for k, tile in enumerate(TILES):
            parts = ["ct%d_%d" % (k, s) for s in range(4)]
            for s, m in enumerate(tile):
                if m == "E":
                    tt(slot(k, s, 0, C), T.own[:].indirect(offs(O_OX, 24)), T.srow[:], ALU.is_equal, ["own", "srow0", "srow1", "srow2", "o_ox"], [parts[s]],
                       n=gathered(C))
                    continue
                n, srow = 16 * m, ["own"] + ["srow%d" % c for c in range(m // 8 + 1)]
                if m in ON_SCALAR:
                    e = ON_SCALAR.index(m)
                    sg = C * e
                    act(T.sg[:, sg:sg + n + 16], T.srow[:, 0:n + 16], ACT.Sign, srow, ["sg%d" % e], n=n + 16, bias=own(m), scale=-1.0)
                    act(slot(k, s, 0, n), T.sg[:, sg:sg + n], ACT.Relu, ["sg%d" % e], [parts[s], "won%d" % e], n=n + 24, accum_out=col(T.rs2, e))
                    act(slot(k, s, n, n + 16), T.sg[:, sg + n:sg + n + 16], ACT.Relu, ["sg%d" % e], ["cd%d" % m])
                    act(col(T.rs, m), col(T.rs2, e), ACT.Identity, ["won%d" % e, "pf19", "pf%d" % (20 + e)], ["rs%d" % m], scale=pc(19), bias=pc(20 + e))
                    parts.append("cd%d" % m)
                else:
                    ts(slot(k, s, 0, n + 16), T.srow[:, 0:n + 16], own(m), None, ALU.is_lt, None, srow, [parts[s]], n=n + 16)
                    act(T.sj[:, 8 * m * (m - 1):8 * m * (m + 1)], slot(k, s, 0, n), ACT.Identity, [parts[s], "pf18", "pf19"], ["rs%d" % m],
                        n=n + 24, scale=pc(19), bias=pc(18), accum_out=col(T.rs, m))
            w, cq, cs = 128 if "E" in tile else 0, T.cq[:, TB[k]:TB[k] + TN[k]], T.cs[:, TB[k]:TB[k] + TN[k]]
            quant(cq, cs, T.ct[:, 4 * TB[k]:4 * (TB[k] + TN[k])], parts, ["cq%d" % k], TN[k])
            mm(6, TN[k], T.waq[:, w:w + 128], T.was[:, w:w + 128], cq, cs, ["cq%d" % k, "waq%d" % (w // 128)], k == 0, k == len(TILES) - 1)
        for m in range(ROWS):
            a, n = 32 * ROWS * m, 16 * ROWS
            if m:
                ts(T.rows[:, a:a + 16 * m], T.srow[:, 0:16 * m], own(m), None, ALU.is_ge, None, ["own", "srow0"], ["ge%d" % m])
            ts(T.rows[:, a + 16 * m:a + n], T.srow[:, 16 * m:n], own(m), None, ALU.is_gt, None, ["own", "srow0"], ["gt%d" % m], n=n - 16 * m)
            act(T.rows[:, a + n:a + 2 * n], T.rows[:, a:a + n], ACT.Copy, ["ge%d" % m, "gt%d" % m, "pf18"], ["rs%d" % m], n=n + 24,
                scale=pc(18), accum_out=col(T.rs, m))
        scan(T.m1[:], T.horn[:], bank(6, C), 0.0, ALU.mult, ALU.add, horn, ["m1"], ["b6"], n=C)
        tt(T.rk[:], T.m1[:, 15:C:16], T.rs[:], ALU.add, ["m1"] + ["rs%d" % m for m in range(24)], ["rk"])
        ts(T.rku[:], T.rk[:], pc(16), None, ALU.mult, None, ["rk", "pf16"], ["rku"])
        cp(T.orow[:].indirect(T.rku[:]), T.vrow[:], ["rku"] + vrow, ["orow"], n=4 * C)
        if t == R - 1:
            o0, o1 = piece(T.ot, 0, C), piece(T.ot, 1, C)
            act(o1, T.vrow[:], ACT.Identity, vrow, ["ot1"], n=C, scale=1.0 / (4 * C), bias=MAGIC)
            act(T.olb[:, C:2 * C], o1, ACT.Identity, ["ot1"], ["ol1"], n=C, bias=-MAGIC)
            act(o0, T.orow[:], ACT.Identity, ["orow"], ["ot0"], n=C, scale=1.0 / C, bias=(turn - (C - 1) / 2) / C)
            ts(o0, o0, MAGIC, MAGIC, ALU.add, ALU.subtract, ["ot0"], ["ot0"], n=C)
            act(o0, o0, ACT.Identity, ["ot0"], ["ot0"], n=C, scale=float(-C), bias=float(turn))
            for n in range(4):
                tt(piece(T.olb, n, L), piece(T.orow, n, L), piece(T.ot, n, L), ALU.add, ["orow", "ot0"], ["ol0%d" % n], n=H)
            dma("y", T.ol[:], T.olb[0:128:16, :], ["ol0%d" % n for n in range(4)] + ["ol1"], (), "sl")

        bq, bs, mq, msc = [T["%s_%d" % (a, t)] for a in ("bq", "bs", "mq", "ms")]
        halves = ((turn + H, bq, bs, "b%d_" % t, ((2, 0), (3, L))), (turn, mq, msc, "mo%d" % t, ((1, L),)))
        for n, (first, q, s, name, moves) in enumerate(halves):
            for a, j, k in runs(first, H):
                scan(T.m2[:, H * n + a:H * n + a + k], T.horn[:, 0:k], T.orow[:, j:j + k], 0.0, ALU.mult, ALU.add, horn + ["orow"], ["m2%d_%d" % (n, a)], n=k)
            pick = T.pick[:, 12 * n:12 * n + 12]
            ts(pick, T.m2[:, H * n + 15:H * n + H:16], pc(16), None, ALU.mult, None,
               ["m2%d_%d" % (n, a) for a, j, k in runs(first, H)] + ["pf16"], ["pick%d" % n])
            for b in range(4):
                src, dst = T.win[:, C * b:32 * C].indirect(pick), T.bt[:, 4 * H * n + b:4 * H * (n + 1):4]
                if b % 2:
                    act(dst, src, ACT.Copy, ["win", "pick%d" % n], ["bt%d_%d" % (n, b)], n=gathered(H))
                else:
                    cp(dst, src, ["win", "pick%d" % n], ["bt%d_%d" % (n, b)], n=gathered(H))
            quant(q[:, 0:H], s[:, 0:H], T.bt[:, 4 * H * n:4 * H * (n + 1)], ["bt%d_%d" % (n, b) for b in range(4)], [name], H)
            for src, dst in ((q, mq), (s, msc)):
                trs, sent = [], 0
                for i, (ahead, j) in enumerate(moves):
                    peer = T.cores[(rank + ahead) % n_ranks]
                    rid, pid = topo.addr(peer)[:2]
                    eng = topo.engines(core, peer)
                    share = len(eng) // len(moves)
                    a, b = src[:, j:j + L], dst[:, L * (n_ranks + 1 - ahead):L * (n_ranks + 2 - ahead)]
                    if dst is mq:
                        a, b = a.bitcast(dt.uint8), b.bitcast(dt.uint8)
                    sent += share
                    trs.append(RemoteDMATransfer(dst_ids=[DstId(rid=rid, pnc=pid)], remote_sem=T.sem["arr%d_%d" % (n, t)], src=a, dst=b,
                                                 dma_engine_mask=sum(1 << e for e in eng[share * i:share * (i + 1)])))
                call = "call%d_%d_%d" % (n, t, dst is mq)
                op("g", lambda trs=trs: g.remote_dma_fused(trs, local_sem=T.sem["out%d" % t]), [name], [call], ["calls"], CALL / CYCLE, "out%d" % t, sent)
                op("far", None, [call], ["ma%d_%d" % (n, t)], (), 64, "arr%d_%d" % (n, t), sent, TRAVEL)

        xs = {}

        def new_state(first, n, keep, to, banks, name):
            for (w, b), k in zip(PRODUCTS, banks):
                lq, ls, r = (T.wq, T.wsc, "w") if w else (T.enq, T.ens, "enq%d" % b)
                z, zn = C * b + to, "z%d_%d" % (b, to)
                mm(k, n, piece(lq, b), piece(ls, b), mq[:, first:first + n], msc[:, first:first + n], name + [r])
                if w:
                    act(T.z[:, z:z + keep], bank(k, keep), ACT.Relu, (), [zn], ["b%d" % k], n=keep, scale=0.03125)
                    continue
                for a, j, m in runs(to + (turn if t == R - 1 else 0), keep):
                    xs.setdefault(to, []).append("xs%d_%d" % (b, j))
                    tt(T.xs[:, 4 * j + b:4 * (j + m):4], bank(k, a + m, a), T.z[:, z + a:z + a + m], ALU.add, [zn], [xs[to][-1]], ["b%d" % k], n=m)

        mid = 256
        late = {(j + e) // 128 for a, j, k in runs(mid + (turn if t == R - 1 else 0), C - mid) for e in (0, k - 1)}
        new_state(0, 128, L, 0, EARLY_BANKS, ["mo%d" % t])
        new_state(H, mid - L, mid - L, L, EARLY_BANKS, ["ma0_%d" % t])
        for c in range(3):
            if c not in late:
                quant_piece(t + 1, c, T.xs, xs[0] + xs[L])
        new_state(L + mid, C - mid, C - mid, mid, LAST_BANKS, ["ma0_%d" % t, "ma1_%d" % t])
        for c in sorted(late):
            quant_piece(t + 1, c, T.xs, xs[0] + xs[L] + xs[mid])

    for c in range(3):
        quant_piece(0, c, T.xin, ["xin%d" % (c // 2)])
    for t in range(R):
        one_round(t)

    tq, tsc, tn = T["tq_%d" % R], T["ts_%d" % R], ["t%d_%d" % (R, c) for c in range(3)]
    for c in range(3):
        mm(2 * c, 128, T.vq[:], T.vs[:], piece(tq, c), piece(tsc, c), [tn[c], "vq"])
        if c % 2:
            act(piece(T.yo, c), bank(2 * c, 128), ACT.Copy, (), ["yo%d" % c], ["b%d" % (2 * c)], n=128)
        else:
            cp(piece(T.yo, c), bank(2 * c, 128), (), ["yo%d" % c], ["b%d" % (2 * c)], n=128)
    dma("y", T.oc[:], tq[:].bitcast(dt.uint8), tn, (), "so")
    dma("s", T.y[:], T.yo[:], ["yo0", "yo1", "yo2"], (), "sy")
    for k in range(4):
        dma("y" if k < 3 else "s", T.osc[4 * k:4 * k + 4, :], tsc[32 * k:32 * k + 4, :], tn, (), "so")
    emit(ops, g, T)
